import numpy as np, ml_dtypes
CORES = [242,247,114,119]
N = 4
BF = ml_dtypes.bfloat16
def gentries(a):
    return np.ascontiguousarray(a.reshape(8, 16, -1).transpose(0, 2, 1)).reshape(8, -1)
def gtable(e):
    e = np.asarray(e); return np.ascontiguousarray(e.reshape(8, -1, 16).transpose(0, 2, 1)).reshape(128, -1).astype(np.int32)
W, P, S, V, Q, F = 3072, 192, 16, 6, 16, 2048
def parts(rng):
    return (rng.integers(0, 256, (N, 8, 16, W)), rng.integers(0, W, (N, 8, P, S)), rng.integers(0, W, (N, 8, P, S)), rng.integers(0, S + 1, (N, 8, P)),
            rng.integers(0, S + 1, (N, 8, P)), rng.integers(600, 1201, (N, 8, P)), rng.integers(0, 16, (N, 8, 16)))
def first(h, m):
    return np.where(m > 0, h[..., 0], (37 * np.arange(P)) & (F - 1))
def pack(x, h, t, m, n, th, w):
    return {"x0": np.ascontiguousarray(x.reshape(N, 128, W)).astype(np.float32).astype(BF), "hands": np.stack([gtable(a.reshape(8, -1)) for a in h]), "trains": np.stack([gtable(a.reshape(8, -1)) for a in t]),
            "mh": m.astype(np.int32), "nt": n.astype(np.int32), "th": th.astype(np.int32), "wt": np.ascontiguousarray(w.reshape(N, 128, 1)).astype(np.int32)}
def setup_inputs(rng):
    return pack(*parts(rng))
def setup_inputs_spread(rng):
    x, h, t, m, n, th, w = parts(rng)
    x = np.minimum((np.exp2(8 * rng.random((N, 8, 1, W))) * rng.random((N, 8, 16, W))).astype(np.int64), 255)
    h = np.minimum((W * rng.random(h.shape) ** 3).astype(np.int64), W - 1); t = W - 1 - np.minimum((W * rng.random(t.shape) ** 2).astype(np.int64), W - 1)
    m = np.minimum(((S + 1) * rng.random(m.shape) ** 2).astype(np.int64), S); n = S - np.minimum(((S + 1) * rng.random(n.shape) ** 2).astype(np.int64), S)
    th = np.minimum(np.exp2(12 * rng.random(th.shape)).astype(np.int64) - 1, 4080)
    return pack(x, h, t, m, n, th, w)
def setup_inputs_ends(rng):
    x, h, t, m, n, th, w = parts(rng); e = W - 1; q = N - 1
    x = 255 * rng.integers(0, 2, (N, 8, 16, W)); x = np.where(rng.random((N, 8, 1, W)) < 0.25, x[:, :, :1, :], x)
    for g, b in enumerate((0, 1, 2, 1, 0, 2, 1, 0)):
        if b < 2: x[:, g, :, 0] = 255 * b
    x[:, :, :, e] = 255 - x[:, :, :, 0]
    h = np.where(rng.random(h.shape) < 0.8, e * rng.integers(0, 2, h.shape), h); t = np.where(rng.random(t.shape) < 0.8, e * rng.integers(0, 2, t.shape), t)
    m = np.where(rng.random(m.shape) < 0.85, S * rng.integers(0, 2, m.shape), m); n = np.where(rng.random(n.shape) < 0.85, S * rng.integers(0, 2, n.shape), n)
    th = np.where(rng.random(th.shape) < 0.8, 4080 * rng.integers(0, 2, th.shape), np.maximum(255 * rng.integers(0, 17, th.shape) - rng.integers(0, 2, th.shape), 0))
    w = 15 * rng.integers(0, 2, w.shape); w[:, 0] = 15; w[:, 7] = 15; w[:, 3] = 0
    a = rng.integers(0, 2, (8, P - 8))
    h[q, :, 8:, 0] = e * a; t[q, :, 8:, 0] = e * a; t[q, :, 8:, 1:] = (e * (1 - a))[:, :, None]
    m[q, :, 8:] = S; n[q, :, 8:] = S; th[q, :, 8:] = 0
    th[q, :, 2] = 4080; n[q, :, 2] = S; m[q, :, 3] = 0; n[q, :, 3] = 0
    h[q, 7, P - 1, 0] = e; n[q, 7, P - 1] = 0
    h[q, 7, 1, 0] = e; t[q, 7, 1] = 0; m[q, 7, 1] = S; n[q, 7, 1] = S; th[q, 7, 1] = 0
    return pack(x, h, t, m, n, th, w)
def setup_inputs_corners(rng):
    x, h, t, m, n, th, w = parts(rng)
    kd = rng.integers(0, 10, (N, 8, P)); kd[:, :, :10] = np.arange(10); kd[:, :, P - 10:] = np.arange(10)
    kd[0] = rng.choice(np.array([1, 4, 6]), (8, P)); kd[1] = rng.choice(np.array([0, 2, 3]), (8, P))
    kd[0, 2, 5] = 5; kd[0, 7, P - 1] = 0
    m = np.array([0, 0, S, S, 1, 1, S, 2, S - 1, 3])[kd]; n = np.array([0, S, 0, S, S, S - 1, S, S, S, 1])[kd]
    c = np.where(m > 0, h[..., 0], (37 * np.arange(P)) & (F - 1))
    t = (c[..., None] + rng.integers(1, W, t.shape)) % W; s = np.arange(S); k = kd[..., None]
    own = (((k == 1) | (k == 4) | (k == 5) | (k == 6)) & (s == 0)) | ((k == 7) & (s == S - 1)) | ((k == 8) & ((s == 3) | (s == 5))) | (k == 9)
    t = np.where(own, c[..., None], t)
    th = np.where((kd == 0) | (kd == 2), rng.choice(np.array([0, 1, 4079, 4080]), th.shape), 0)
    w[:, 1] = 0; w[:, 3] = 15; w[:, 5] = 0; w[:, 5, 15] = 1; w[:, 6] = 0; w[:, 6, 0] = 15
    return pack(x, h, t, m, n, th, w)
def setup_inputs_ties(rng):
    x, h, t, m, n, th, w = parts(rng)
    x = 4 * rng.integers(0, 64, (N, 8, 1, W)) + np.zeros((1, 1, 16, 1), np.int64)
    x[:, ::2] = x[:, ::2] + rng.integers(0, 2, (N, 4, 16, W)) * (rng.random((N, 4, 1, W)) < 0.25)
    th = np.maximum(64 * rng.integers(0, 12, th.shape) + rng.integers(-1, 2, th.shape), 0)
    t[:, 1::2] = np.where(rng.random((N, 4, P, S)) < 0.15, h[:, 1::2, :, :1], t[:, 1::2])
    t[:, 2] = rng.choice(np.array([0, 1, W - 2, W - 1]), (N, P, S)); h[:, 4] = rng.choice(np.array([0, 7, W - 1]), (N, P, S)); t[:, 6] = t[:, 6, :, :1]
    a = np.maximum(n[1], 1).reshape(-1); a[rng.permutation(8 * P)[:256]] = 0; n[1] = a.reshape(8, P)
    t[1] = np.where(np.arange(S) == n[1][..., None] - 1, first(h[1], m[1])[..., None], t[1])
    return pack(x, h, t, m, n, th, w)
def setup_inputs_counts(rng):
    x, h, t, m, n, th, w = parts(rng); b = N - 1; D = min(N - 3, V - 2, 3); p = b - D; s = np.arange(S)
    x[:2, 7] = np.where(np.arange(W) % 2 == 0, rng.integers(250, 256, (2, 16, W)), rng.integers(0, 10, (2, 16, W))); w[0, 7] = 15
    m[0, 1] = 0; n[0] = S
    m[1, 2] = 0; n[1] = np.maximum(n[1], 1); n[1, 2] = 0; n[1, 3, rng.permutation(P)[:99]] = 0
    c = first(h, m)
    t[:2] = (c[:2, ..., None] + 1 + 2 * rng.integers(0, W // 2, (2, 8, P, S))) % W
    t[0, ..., 0] = c[0]
    t[1, :7] = np.where(s == n[1, :7, :, None] - 1, c[1, :7, :, None], t[1, :7])
    XT = np.take_along_axis(x[:2], t[:2].reshape(2, 8, 1, P * S), 3).reshape(2, 8, 16, P, S); XC = np.take_along_axis(x[:2], c[:2, :, None, :], 3)
    d = np.add.reduce(np.abs(XT - XC[..., None]), axis=2)
    th[0] = np.maximum(np.min(d[0, ..., 1:], axis=-1) - 1, 0)
    th[1, 7] = np.take_along_axis(d[1, 7], n[1, 7][:, None] - 1, 1)[:, 0]
    th[p:] = 0; n[p:] = np.maximum(n[p:], 1); n[p] = S - D
    t[p:] = 8 * rng.integers(0, W // 8, (N - p, 8, P, S)); t[p, ..., 1:] = (t[p, ..., :1] + 8 * rng.integers(1, W // 8, (8, P, S - 1))) % W
    t[p:, :, P - 2:] = t[p:, :, P - 2:] + 4
    for u in range(D):
        h[p + u] = 8 * rng.integers(0, W // 8, (8, P, S)) + 1 + u; m[p + u] = rng.integers(D, S + 1, (8, P))
    h[b] = 8 * rng.integers(0, W // 8, (8, P, S)) + 7; h[b, ..., D] = np.roll(t[p, ..., 0], D, axis=0)
    m[b] = rng.integers(D + 1, S + 1, (8, P)); m[b, :, P - 2:] = 0
    return pack(x, h, t, m, n, th, w)
def check_inputs(d):
    bad = []
    for k, lo, hi in (("x0", 0, 255), ("hands", 0, W - 1), ("trains", 0, W - 1), ("mh", 0, S), ("nt", 0, S), ("th", 0, 4080), ("wt", 0, 15)):
        v = np.asarray(d[k]).astype(np.float64)
        if not (np.min(v) >= lo and np.max(v) <= hi): bad.append("range of " + k)
        elif np.any(v != np.rint(v)): bad.append("whole numbers of " + k)
    return bad
def reference(x0, hands, trains, mh, nt, th, wt):
    X = x0.astype(np.float32).astype(np.int32).reshape(N, 8, 16, W); s = np.arange(S); i = np.arange(P)
    H = np.stack([gentries(a) for a in hands]).astype(np.int64).reshape(N, 8, P, S); T = np.stack([gentries(a) for a in trains]).astype(np.int64).reshape(N, 8, P, S)
    m = mh.astype(np.int64); n = nt.astype(np.int64); lim = th.astype(np.int64); wv = wt.astype(np.int64).reshape(N, 8, 16, 1)
    H = np.where(s < m[..., None], H, 0); T = np.where(s < n[..., None], T, 0)
    A = np.zeros(N, np.int64); zero = np.zeros((N, 8, P, 1), np.int64)
    for t in range(V):
        if t > 0:
            j = 1 + t // N - (t - 1) // N
            T = np.roll(T, (1, j), axis=(0, 1)); n = np.roll(n, (1, j), axis=(0, 1))
        A3 = A[:, None, None]
        c = np.where(m > 0, H[..., 0], (37 * i + 613 * t + A3) & (F - 1))
        H = np.concatenate([H[..., 1:], zero], axis=-1); m = np.maximum(m - 1, 0)
        XT = np.take_along_axis(X, T.reshape(N, 8, 1, P * S), 3).reshape(N, 8, 16, P, S); XC = np.take_along_axis(X, c[:, :, None, :], 3)
        dist = np.add.reduce(np.abs(XT - XC[..., None]), axis=2)
        ok = (dist <= (lim + (A3 & 255))[..., None]) & (s < n[..., None])
        k = np.max(np.where(ok, s, -1), axis=-1); hit = k >= 0; got = np.where(hit, n - k, 0)
        XS = np.take_along_axis(XT, np.maximum(k, 0)[:, :, None, :, None], 4)[..., 0]
        y = np.where(hit[:, :, None, :], (XC + XS) >> 1, np.where((n == 0)[:, :, None, :], XC, np.abs(XC - XS)))
        z = np.add.reduce(wv * y, axis=2) & (Q - 1)
        np.put_along_axis(X, (Q * i + z)[:, :, None, :], y, 3)
        h1 = hit[..., None]; m1 = m[..., None]; c1 = c[..., None]; n1 = n[..., None]
        back = np.take_along_axis(T, np.clip(m1 + n1 - s, 0, S - 1), 3)
        H = np.where(h1 & (s == m1), c1, np.where(h1 & (s > m1) & (s <= m1 + got[..., None]), back, H))
        m = np.where(hit, np.minimum(m + 1 + got, S), m)
        grown = np.where(n1 == S, np.concatenate([T[..., 1:], zero], axis=-1), T)
        grown = np.where(s == np.minimum(n1, S - 1), c1, grown)
        T = np.where(h1, np.where(s < k[..., None], T, 0), grown); n = np.where(hit, k, np.minimum(n + 1, S))
        A = np.sum(got, axis=(1, 2))
    return {"yx": X.reshape(N, 128, W).astype(np.float32).astype(BF), "yh": np.stack([gtable(a.reshape(8, -1)) for a in H]).astype(np.float32), "yt": np.stack([gtable(a.reshape(8, -1)) for a in T]).astype(np.float32),
            "ym": m.astype(np.float32), "yn": n.astype(np.float32)}

@@ -1,0 +1,585 @@
+from concourse.mybir import AluOpType, AxisListType, ActivationFunctionType
+
+OP = AluOpType
+AF = ActivationFunctionType
+V = 6
+NP = 192
+CW = 3088
+EMPTY = 1536.0
+PARTS = ("MX", "cols", "b", "RW", "RA", "WIN", "WINA", "MB")
+CA = 8 * 16 * (191 * 192 // 2)
+RND = 8388608.0
+
+SCRATCH = {
+    "X": ("sbuf", [128, CW], "bfloat16"),
+    "XT": ("sbuf", [128, 3072], "bfloat16"),
+    "MX": ("sbuf", [128, 3072], "bfloat16"),
+    "IOT": ("sbuf", [128, 3072], "float32"),
+    "WIN": ("sbuf", [128, 4096], "float32"),
+    "WINA": ("sbuf", [128, 1024], "float32"),
+    "RW": ("sbuf", [128, 16 * 128], "float16"), "RA": ("sbuf", [128, 4 * 128], "float16"), "Tg": ("sbuf", [128, NP], "float16"),
+    "qm": ("sbuf", [128, 12], "uint16"),
+    "nmi": ("sbuf", [8, 576], "int32"), "nmf": ("sbuf", [8, 576], "float32"), "R8": ("sbuf", [8, 128], "float32"),
+    "tri": ("sbuf", [128, NP], "int32"), "hai": ("sbuf", [128, NP], "int32"), "wti": ("sbuf", [128, 1], "int32"),
+    "smB": ("sbuf", [128, 272], "bfloat16"), "smC": ("sbuf", [128, 256], "bfloat16"), "smA": ("sbuf", [128, 256], "bfloat16"),
+    "cwi": ("sbuf", [128, 16], "int32"), "cwj": ("sbuf", [128, 16], "int32"), "cw": ("sbuf", [128, 16], "float32"),
+    "SC": ("sbuf", [128, 16], "float32"), "E0": ("sbuf", [128, 16], "float32"), "PC": ("sbuf", [128, 16], "float32"),
+    "WB": ("sbuf", [128, 16], "float32"), "cols": ("sbuf", [128, 16], "float32"),
+    "iq": ("sbuf", [128, 12], "float32"), "bi": ("sbuf", [128, 12], "float32"), "b16i": ("sbuf", [128, 12], "int32"),
+    "b16h": ("sbuf", [128, 12], "float16"), "b37": ("sbuf", [128, 12 * V], "float32"),
+    "onesf": ("sbuf", [128, 128], "float32"), "ones": ("sbuf", [128, NP], "bfloat16"), "oneh": ("sbuf", [128, NP], "float16"),
+    "Ib": ("sbuf", [128, 128], "bfloat16"), "NB": ("sbuf", [128, 128], "bfloat16"),
+    "W2": ("sbuf", [128, 144], "bfloat16"), "WN": ("sbuf", [128, 144], "bfloat16"), "Ww": ("sbuf", [128, 144], "bfloat16"),
+    "Wk": ("sbuf", [128, 144], "float16"), "W0": ("sbuf", [128, 144], "float16"), "W256": ("sbuf", [128, 144], "float16"),
+    "Ih": ("sbuf", [128, 256], "float16"), "SI": ("sbuf", [128, 256], "float16"), "E15": ("sbuf", [128, 256], "float16"),
+    "IN": ("sbuf", [128, 256], "float16"), "TUr": ("sbuf", [128, 256], "float16"), "BA": ("sbuf", [128, 128], "float16"),
+    "BH": ("sbuf", [128, 256], "float16"), "TUi": ("sbuf", [128, 128], "float16"), "TU8": ("sbuf", [128, 128], "float16"),
+    "I8": ("sbuf", [128, 128], "float16"), "I8n": ("sbuf", [128, 128], "float16"), "MB": ("sbuf", [128, 8 * 128], "float16"),
+    "M8": ("sbuf", [128, 8], "float16"), "UR": ("sbuf", [128, 128], "float16"),
+    "thr": ("sbuf", [128, NP], "float32"), "lim": ("sbuf", [128, NP], "float32"),
+    "Th": ("sbuf", [128, NP], "float16"), "IH": ("sbuf", [128, 3 * NP], "float16"), "Hs": ("sbuf", [128, NP], "float16"),
+    "Hp": ("sbuf", [128, NP], "float16"), "ff": ("sbuf", [128, NP], "float16"), "oh": ("sbuf", [128, NP], "float16"),
+    "fT": ("sbuf", [128, NP], "float16"), "ohc": ("sbuf", [128, NP], "float16"), "crep0": ("sbuf", [128, NP], "float32"),
+    "crep1": ("sbuf", [128, NP], "float32"),
+    "Trot": ("sbuf", [128, NP], "float32"), "xc": ("sbuf", [128, NP], "bfloat16"), "na": ("sbuf", [128, NP], "bfloat16"),
+    "ok": ("sbuf", [128, NP], "float16"), "K1": ("sbuf", [128, NP], "float16"), "fst": ("sbuf", [128, NP], "float16"),
+    "Tc": ("sbuf", [128, NP], "float16"), "ac": ("sbuf", [128, NP], "float32"), "vv": ("sbuf", [128, NP], "float32"),
+    "uu": ("sbuf", [128, NP], "float32"), "au": ("sbuf", [128, NP], "float32"), "y": ("sbuf", [128, NP], "bfloat16"),
+    "Tcap": ("sbuf", [128, NP], "float16"), "hoc": ("sbuf", [128, NP], "float16"),
+    "Rv": ("sbuf", [128, NP], "float32"), "R2": ("sbuf", [128, NP], "float32"),
+    "cf": ("sbuf", [128, 12], "float32"), "cl": ("sbuf", [128, 12], "uint16"), "kl": ("sbuf", [128, 12], "uint16"),
+    "zl": ("sbuf", [128, 12], "uint16"), "ql": ("sbuf", [128, 12], "uint16"),
+    "zi": ("sbuf", [128, 12], "int32"), "zj": ("sbuf", [128, 12], "int32"), "zk": ("sbuf", [128, 12], "int32"),
+    "x1": ("sbuf", [128, 12], "float32"), "nd": ("sbuf", [128, 12], "float32"),
+    "sm": ("sbuf", [128, 12 * 10], "float32"), "smi": ("sbuf", [128, 12 * 5], "int32"),
+    "aa": ("sbuf", [128, 4], "float32"), "ai": ("sbuf", [128, 2], "int32"),
+    "oyh": ("sbuf", [128, NP], "float32"), "oyt": ("sbuf", [128, NP], "float32"), "oya": ("sbuf", [128, NP], "float32"),
+    "oyb": ("sbuf", [128, NP], "float32"), "omn": ("sbuf", [8, 2 * NP], "float32"),
+}
+for _i in range(8):
+    SCRATCH["bk%d" % _i] = ("psum", [128, 512], "float32")
+for _i in range(V):
+    SCRATCH["TT%d" % _i] = ("sbuf", [128, NP], "uint16")
+for _i in range(V - 1):
+    SCRATCH["TO%d" % _i] = ("sbuf", [128, NP], "uint16")
+
+DMAS = ["dx", "dt", "dh", "dn", "dm", "dth", "dw", "ox", "oh", "ot", "om", "on"]
+SEMAPHORES = ["qV", "qA", "qP", "qG", "snd"] + ["arr%d" % i for i in range(1, V)] + ["d_" + n for n in DMAS]
+
+
+def send_engines(topo, src, dst):
+    return topo.engines(src, dst)[:8]
+
+
+def rank_program(g, core, T, topo):
+    rank = T.rank_of(core)
+    if rank is None:
+        return
+    ops = []
+    writer, readers, bank = {}, {}, {}
+
+    def op(q, f, r=(), w=(), dma=None):
+        k = len(ops)
+        deps = set()
+        for n in r:
+            if n[:2] == "bk":
+                continue
+            if n in writer:
+                deps.add(writer[n])
+            readers.setdefault(n, []).append(k)
+        for n in w:
+            if n[:2] == "bk":
+                continue
+            if n in writer and (ops[writer[n]]["q"] != q or ops[writer[n]]["dma"] or n.rstrip("0123456789_") not in PARTS):
+                deps.add(writer[n])
+            for i in readers.get(n, []):
+                if i != k:
+                    deps.add(i)
+            writer[n] = k
+            readers[n] = []
+        for n in list(r) + list(w):
+            if n[:2] == "bk":
+                a = bank.setdefault(n, {})
+                for q2 in a:
+                    if q2 != q:
+                        deps.add(a[q2])
+                a[q] = k
+        ops.append({"q": q, "f": f, "deps": deps, "dma": dma})
+        return k
+
+    def ts(out, in0, s1, o1, s2, o2, r, w):
+        if o2 is None:
+            op("V", lambda: g.vector.tensor_scalar(out, in0, s1, None, o1), r, w)
+        else:
+            op("V", lambda: g.vector.tensor_scalar(out, in0, s1, s2, o1, o2), r, w)
+
+    def tt(out, a, b, o, r, w):
+        op("V", lambda: g.vector.tensor_tensor(out, a, b, o), r, w)
+
+    def cp(out, a, r, w):
+        op("V", lambda: g.vector.tensor_copy(out, a), r, w)
+
+    def act(out, a, fn, r, w, bias=0.0, scale=1.0):
+        op("A", lambda: g.scalar.activation(out, a, fn, bias=bias, scale=scale), r, w)
+
+    def mm(out, l, rr, st, sp, r, w):
+        op("P", lambda: g.tensor.matmul(out, l, rr, st, sp), r, w)
+
+    def dma(q, name, out, in_, r, w):
+        e = {"S": g.sync, "A": g.scalar}[q]
+        op(q, lambda: e.dma_start(out, in_), r, w, dma="d_" + name)
+
+    def ms(ap, c, w):
+        op("V", lambda: g.vector.memset(ap, c), [], [w])
+
+    def MB(j):
+        return T.MB[:, 128 * j:128 * j + 128]
+
+    def S(j):
+        return T.sm[:, 12 * j:12 * j + 12]
+
+    def diag(o, mat, src, so, n, r, wb, first=True):
+        for j in range(16):
+            mm(o, T[mat][:, 16 - j:144 - j], T[src][:, so + j:so + NP * n:16], first and j == 0, j == 15, r + [mat], [wb])
+
+    B = [T["bk%d" % i] for i in range(8)]
+    SP = T.SC[:, 15:16]
+
+    dma("S", "dm", T.nmi[:, NP:2 * NP], T.mh[:, :], [], ["nmi_m"])
+    dma("A", "dh", T.hai[:, :], T.hands[:, :], [], ["hai"])
+    dma("S", "dn", T.nmi[:, 0:NP], T.nt[:, :], [], ["nmi_n"])
+    dma("A", "dx", T.X[:, 0:3072], T.x0[:, :], [], ["X"])
+    dma("S", "dt", T.tri[:, :], T.trains[:, :], [], ["tri"])
+    dma("S", "dth", T.nmi[:, 2 * NP:3 * NP], T.th[:, :], [], ["nmi_t"])
+    dma("S", "dw", T.wti[:, :], T.wt[:, :], [], ["wti"])
+
+    blk = [[0, 2], [-16, 8], [0, 16]]
+    blk2 = [[0, 2], [16, 8], [0, 16]]
+    op("G", lambda: g.iota(T.cwi[:, :], [[1, 16]], 128, -1), [], ["cwi"])
+    op("G", lambda: g.iota(T.smA[:, :], [[0, 16], [1, 16]], 0, 0, allow_small_or_imprecise_dtypes=True), [], ["smA"])
+    ms(T.R8[:, :], 1.0, "R8")
+    ms(T.smB[:, 0:16], -99.0, "smBp")
+    ms(T.X[:, 3072:CW], 0.0, "Xp")
+    ms(T.onesf[:, :], 1.0, "onesf")
+    ms(T.ones[:, :], 1.0, "ones")
+    for b in (6, 7):
+        ms(B[b][:, 192:256], 0.0, "bk%d" % b)
+
+    def blocks(nm, fill, o):
+        op("G", lambda: g.affine_select(T[nm][:, o:o + 256], T.smA[:, :], blk, OP.is_ge, fill, 0, 1), ["smA"], [nm])
+        op("G", lambda: g.affine_select(T[nm][:, o:o + 256], T[nm][:, o:o + 256], blk2, OP.is_ge, fill, 15, -1), [nm], [nm])
+
+    blocks("smB", -99.0, 16)
+    op("G", lambda: g.affine_select(T.R8[:, :], T.R8[:, :], [[1, 128]], OP.is_ge, 0.0, 0, -16), ["R8"], ["R8"])
+    op("G", lambda: g.affine_select(T.R8[:, :], T.R8[:, :], [[-1, 128]], OP.is_ge, 0.0, 15, 16), ["R8"], ["R8"])
+    op("G", lambda: g.iota(T.iq[:, :], [[16, 12]], 0, 0, allow_small_or_imprecise_dtypes=True), [], ["iq"])
+    blocks("smC", 99.0, 0)
+    op("G", lambda: g.iota(T.IOT[:, :], [[1, 3072]], -1536, 0, allow_small_or_imprecise_dtypes=True), [], ["IOT"])
+
+    smb = T.smB[:, 16:144]
+    smb2 = T.smB[:, 16:272]
+    smp = T.smB[:, 0:144]
+    ts(T.cwj[:, :], T.cwi[:, :], 15, OP.bitwise_and, None, None, ["cwi"], ["cwj"])
+    cp(T.cw[:, :], T.cwj[:, :], ["cwj"], ["cw"])
+    ts(T.SC[:, :], T.cw[:, :], -1.0, OP.mult, 15.0, OP.add, ["cw"], ["SC"])
+    ts(T.E0[:, :], T.cw[:, :], 0.0, OP.is_equal, None, None, ["cw"], ["E0"])
+    ts(T.cols[:, 0:1], SP, 1.0, OP.is_ge, None, None, ["SC"], ["cols"])
+    ts(T.cols[:, 1:2], SP, -1.0, OP.add, None, None, ["SC"], ["cols"])
+    ts(T.cols[:, 2:3], SP, -1.0, OP.mult, 16.0, OP.add, ["SC"], ["cols"])
+    row0 = (1536.0, -4096.0, 512.0, -1025.0 / 2048, 1.0, 2048.0, 6144.0, -512.0)
+    for j, v in enumerate(row0):
+        ts(T.cols[:, 3 + j:4 + j], T.E0[:, 0:1], v, OP.mult, None, None, ["E0"], ["cols"])
+    ts(T.PC[:, :], T.E0[:, :], 5632.0, OP.mult, -4096.0, OP.add, ["E0"], ["PC"])
+    ts(T.WB[:, :], T.SC[:, :], -4096.0, OP.mult, 4096.0 * 16.5, OP.add, ["SC"], ["WB"])
+    ts(T.W0[:, :], smp, 0.0, OP.is_equal, T.E0[:, 0:1], OP.mult, ["smB", "smBp", "E0"], ["W0"])
+
+    ts(T.Ib[:, :], smb, SP, OP.is_equal, None, None, ["smB", "SC"], ["Ib"])
+    ts(T.NB[:, :], smb, 0.0, OP.is_ge, -1.0, OP.mult, ["smB"], ["NB"])
+    ts(T.W2[:, :], smp, 0.0, OP.is_equal, 2.0, OP.mult, ["smB", "smBp"], ["W2"])
+    ts(T.WN[:, :], smp, 0.0, OP.is_equal, -1.0, OP.mult, ["smB", "smBp"], ["WN"])
+    ts(T.BA[:, :], smb, 0.0, OP.is_ge, None, None, ["smB"], ["BA"])
+    ts(T.I8[:, :], smb, SP, OP.is_equal, 8192.0, OP.mult, ["smB", "SC"], ["I8"])
+    ts(T.Ih[:, :], smb2, SP, OP.is_equal, None, None, ["smB", "SC"], ["Ih"])
+
+    def spread(j, nm, b):
+        cp(T.nmf[:, NP * j:NP * j + NP], T.nmi[:, NP * j:NP * j + NP], [nm], [nm + "f"])
+        mm(B[b][:, 0:NP], T.R8[:, :], T.nmf[:, NP * j:NP * j + NP], True, True, ["R8", nm + "f"], ["bk%d" % b])
+
+    spread(1, "nmi_m", 4)
+    ts(T.bi[:, :], T.iq[:, :], SP, OP.add, None, None, ["iq", "SC"], ["bi"])
+    ts(T.b37[:, 0:12], T.bi[:, :], 37.0, OP.mult, None, None, ["bi"], ["b37"])
+    ts(T.oyt[:, :], B[4][:, 0:NP], SP, OP.is_le, 3072.0, OP.mult, ["bk4", "SC"], ["tb"])
+    tt(T.oyb[:, :], T.oyt[:, :], T.hai[:, :], OP.max, ["tb", "hai"], ["h0f"])
+    ts(T.Hs[:, :], T.oyb[:, :], -1536.0, OP.add, None, None, ["h0f"], ["Hs"])
+    diag(B[2][:, 408:420], "W0", "Hs", 0, 1, ["Hs"], "bk2")
+    spread(0, "nmi_n", 5)
+    ts(T.oyh[:, :], B[5][:, 0:NP], SP, OP.is_le, 3072.0, OP.mult, ["bk5", "SC"], ["ta"])
+    tt(T.oya[:, :], T.oyh[:, :], T.tri[:, :], OP.max, ["ta", "tri"], ["t0f"])
+    cp(T.TT0[:, :], T.oya[:, :], ["t0f"], ["TT0"])
+
+    def empties(scale):
+        pd = B[2][:, 408:420]
+        ts(S(1), pd, EMPTY * scale, OP.is_lt, 4096.0, OP.mult, ["bk2"], ["s1"])
+        ts(S(0), pd, 1.0 / scale, OP.mult, 1536.0, OP.add, ["bk2"], ["s0"])
+
+    empties(1.0)
+    cp(T.smi[:, 0:12], T.b37[:, 0:12], ["b37"], ["fi"])
+    ts(T.smi[:, 12:24], T.smi[:, 0:12], 2047, OP.bitwise_and, None, None, ["fi"], ["fj"])
+    tt(S(4), S(1), T.smi[:, 12:24], OP.max, ["fj", "s1"], ["s4"])
+    tt(T.cf[:, :], S(0), S(4), OP.min, ["s0", "s4"], ["cf"])
+    cp(T.cl[:, :], T.cf[:, :], ["cf"], ["cl"])
+
+    def matrices():
+        ts(T.SI[:, :], smb2, T.cols[:, 1:2], OP.is_equal, None, None, ["smB", "cols"], ["SI"])
+        ts(T.E15[:, :], smb2, 15.0, OP.is_equal, T.cols[:, 3:4], OP.mult, ["smB", "cols"], ["E15"])
+        tt(T.SI[:, :], T.SI[:, :], T.Ih[:, :], OP.subtract, ["SI", "Ih"], ["SI"])
+        ts(T.IN[:, :], smb2, SP, OP.is_equal, -1536.0, OP.mult, ["smB", "SC"], ["IN"])
+        ts(T.TUr[:, :], T.smC[:, :], SP, OP.is_lt, -4096.0, OP.mult, ["smC", "SC"], ["TUr"])
+        ts(T.TUi[:, :], T.smC[:, 0:128], SP, OP.is_le, None, None, ["smC", "SC"], ["TUi"])
+        ts(T.TU8[:, :], T.smC[:, 0:128], SP, OP.is_lt, 4096.0, OP.mult, ["smC", "SC"], ["TU8"])
+        ts(T.BH[:, :], smb2, 0.0, OP.is_ge, 8192.0, OP.mult, ["smB"], ["BH"])
+        for j in range(len(row0)):
+            ts(MB(j), smb, 0.0, OP.is_ge, T.cols[:, 3 + j:4 + j], OP.mult, ["smB", "cols"], ["MB"])
+        for t in range(1, V):
+            ts(T.b37[:, 12 * t:12 * t + 12], T.bi[:, :], 37.0, OP.mult, float(613 * t + CA), OP.add, ["bi"], ["b37"])
+        ts(T.b16h[:, :], T.bi[:, :], 16.0, OP.mult, None, None, ["bi"], ["b16h"])
+        ts(T.Wk[:, :], smp, 0.0, OP.is_equal, T.cols[:, 0:1], OP.mult, ["smB", "smBp", "cols"], ["Wk"])
+        ts(T.W256[:, :], smp, 0.0, OP.is_equal, 256.0, OP.mult, ["smB", "smBp"], ["W256"])
+        cp(T.oneh[:, :], T.ones[:, :], ["ones"], ["oneh"])
+
+    def matrices2():
+        cp(T.cols[:, 12:13], T.wti[:, :], ["wti"], ["wtf"])
+        ts(T.b16i[:, :], T.bi[:, :], 16.0, OP.mult, None, None, ["bi"], ["b16i"])
+        ts(T.I8n[:, :], smb, SP, OP.is_equal, -4096.0, OP.mult, ["smB", "SC"], ["I8n"])
+        ts(T.Ww[:, :], smp, 0.0, OP.is_equal, T.cols[:, 12:13], OP.mult, ["smB", "smBp", "wtf"], ["Ww"])
+
+        for w in range(4):
+            ts(T.RA[:, 128 * w:128 * w + 128], smb, T.SC[:, 15 - w:16 - w], OP.is_equal, None, None, ["smB", "SC"], ["RA"])
+
+    def matrices3():
+        for w in range(16):
+            ts(T.RW[:, 128 * w:128 * w + 128], smb, T.cw[:, w:w + 1], OP.is_equal, None, None, ["smB", "cw"], ["RW"])
+        ts(T.M8[:, :], T.smB[:, 16:144:16], 0.0, OP.is_ge, None, None, ["smB"], ["M8"])
+        ts(T.UR[:, :], smb, T.SC[:, V - 1:V], OP.is_equal, None, None, ["smB", "SC"], ["UR"])
+
+
+    def turn1():
+        for c in range(2):
+            for h in range(2):
+                w = 2 * c + h
+                mm(B[6 + c][:, 256 * h:256 * h + NP], T.RA[:, 128 * w:128 * w + 128], T.Tcap[:, :], True, True, ["RA", "Tcap"], ["bk%d" % (6 + c)])
+            act(T.WINA[:, 512 * c:512 * c + 448], B[6 + c][:, 0:448], AF.Copy, ["bk%d" % (6 + c)], ["WINA"])
+
+    def turn2(t):
+        cp(T.Tg[:, :], T.WINA[:, :].indirect(T.ql[:, :]), ["WINA", "ql"], ["Tg"])
+        for c in range(2):
+            for h in range(2):
+                w = (t + 1 - 4 * (2 * c + h)) % 16
+                mm(B[6 + c][:, 256 * h:256 * h + NP], T.RW[:, 128 * w:128 * w + 128], T.Tg[:, :], True, True, ["RW", "Tg"], ["bk%d" % (6 + c)])
+
+    def turned():
+        for c in range(2):
+            for h in range(2):
+                o = 1024 * (2 * c + h)
+                act(T.WIN[:, o:o + NP], B[6 + c][:, 256 * h:256 * h + NP], AF.Copy, ["bk%d" % (6 + c)], ["WIN"])
+        act(T.Rv[:, :], T.WIN[:, :].indirect(T.qm[:, :]), AF.Copy, ["WIN", "qm"], ["Rv"])
+
+    def lists():
+        tt(T.x1[:, :], B[2][:, 384:396], T.bi[:, :], OP.add, ["bk2", "bi"], ["x1"])
+        tt(T.smi[:, 24:36], B[2][:, 396:408], T.x1[:, :], OP.add, ["bk2", "x1"], ["x2"])
+        ts(T.smi[:, 36:48], T.smi[:, 24:36], 1023, OP.bitwise_and, None, None, ["x2"], ["x3"])
+        ts(T.smi[:, 48:60], T.smi[:, 24:36], 3072 + 255, OP.bitwise_and, None, None, ["x2"], ["x4"])
+        cp(T.ql[:, :], T.smi[:, 36:48], ["x3"], ["ql"])
+        cp(T.qm[:, :], T.smi[:, 48:60], ["x4"], ["qm"])
+
+    def card_c(t):
+        ts(T.hoc[:, :], B[2][:, NP:2 * NP], T.SC[:, t:t + 1], OP.add, 16.0, OP.is_equal, ["bk2", "SC"], ["hoc"])
+        mm(B[3][:, NP:2 * NP], T.I8n[:, :], T.hoc[:, :], False, True, ["I8n", "hoc"], ["bk3"])
+
+    def card_c2(t):
+        tt(B[5][:, NP:2 * NP], B[3][:, NP:2 * NP], T["crep%d" % (t % 2)][:, :], OP.max, ["bk3", "crep%d" % (t % 2)], ["bk5", "C1"])
+
+    def hand_end():
+        tt(T.R2[:, :], B[5][:, 0:NP], T.Rv[:, :], OP.max, ["Rv", "bk5", "wall"], ["R2"])
+        tt(T.Hs[:, :], B[5][:, NP:2 * NP], T.R2[:, :], OP.min, ["R2", "bk5", "R3p"], ["Hs"])
+
+    def hand_begin(t):
+        ts(T.Hp[:, :], T.Hs[:, :], T.PC[:, t:t + 1], OP.max, None, None, ["Hs", "PC"], ["Hp"])
+        ts(T.IH[:, NP:2 * NP], T.Hp[:, :], EMPTY, OP.is_ge, None, None, ["Hp"], ["hinv"])
+        if t < V - 1:
+            ts(T.IH[:, 2 * NP:3 * NP], T.Hp[:, :], T.E0[:, t + 1:t + 2], OP.mult, None, None, ["Hp", "E0"], ["hfr"])
+
+    cp(T.xc[:, :], T.X[:, :].indirect(T.cl[:, :]), ["X", "Xp", "cl"], ["xc"])
+    for t in range(V):
+        last = t == V - 1
+        tn = "TT%d" % t
+        tab = T[tn]
+        jj = 0 if last else (2 if t == 3 else 1)
+        ro = 128 - 16 * jj
+
+        def rot(nm):
+            return T[nm][:, ro:ro + 128] if jj else T[nm][:, 0:128]
+
+        def chunk(c):
+            for s in range(4):
+                o = 256 * (c % 2)
+                tt(T.MX[:, 1024 * c + s:1024 * c + 1024:4], B[1][:, o:o + 256], T.XT[:, 1024 * c + s:1024 * c + 1024:4], OP.max,
+                   ["bk1", "XT%d" % c], ["MX%d_%d" % (c, s)])
+
+        def fours(c, n):
+            for s in range(4):
+                mm(B[1][:, s:256 * n:4], T.Ib[:, :], T.xc[:, 64 * c:64 * c + 64 * n], True, True, ["Ib", "xc"], ["bk1"])
+
+        def sumx(c):
+            for s in range(16):
+                mm(B[0][:, 64 * c:64 * c + 64], T.WN[:, 16 - s:144 - s], T.XT[:, 1024 * c + s:1024 * c + 1024:16], False, False, ["WN", "XT%d" % c], ["bk0"])
+
+        def summ(c):
+            for k in range(16):
+                s = k // 4 + 4 * (k % 4)
+                mm(B[0][:, 64 * c:64 * c + 64], T.W2[:, 16 - s:144 - s], T.MX[:, 1024 * c + s:1024 * c + 1024:16], False, c == 2 and k == 15,
+                   ["W2", "MX%d_%d" % (c, s % 4)], ["bk0"])
+
+        if t > 0:
+            op("R", None, [], [tn], dma="arr%d" % t)
+        cp(T.xc[:, :], T.X[:, :].indirect(T.cl[:, :]), ["X", "Xp", "cl"], ["xc"])
+        def gather(c):
+            act(T.XT[:, 1024 * c:1024 * c + 1024], T.X[:, :].indirect(tab[:, 64 * c:64 * c + 64]), AF.Copy, ["X", "Xp", tn], ["XT%d" % c])
+
+        crn = "crep%d" % (t % 2)
+        fours(0, 2)
+        mm(B[0][:, 0:NP], T.NB[:, :], T.xc[:, :], True, False, ["NB", "xc"], ["bk0"])
+        if t > 0:
+            lists()
+            ts(T.ai[:, 0:1], B[4][:, 0:1], float(CA), OP.add, None, None, ["bk4"], ["ai0"])
+            ts(T.ai[:, 1:2], T.ai[:, 0:1], 255, OP.bitwise_and, None, None, ["ai0"], ["ai1"])
+            cp(T.aa[:, 1:2], T.ai[:, 1:2], ["ai1"], ["a256"])
+            card_c(t - 1)
+        ts(T.Th[:, :], tab[:, :], -1536.0, OP.add, None, None, [tn], ["Th"])
+        ts(T.IH[:, 0:NP], tab[:, :], 3072.0, OP.is_ge, None, None, [tn], ["inv"])
+        ts(T.na[:, :], T.xc[:, :], -1.0, OP.mult, None, None, ["xc"], ["na"])
+        gather(0)
+        mm(B[2][:, 0:NP], T.BA[:, :], T.IH[:, 0:NP], True, True, ["BA", "inv"], ["bk2"])
+        mm(B[4][:, 0:NP], rot("Ih"), T.Th[:, :], True, True, ["Ih", "Th"], ["bk4"])
+        mm(B[0][:, 0:NP], T.I8[:, :], T.IH[:, 0:NP], False, False, ["I8", "inv"], ["bk0"])
+        sumx(0)
+        chunk(0)
+        summ(0)
+        if t == 0:
+            spread(2, "nmi_t", 6)
+            matrices()
+            matrices2()
+        gather(1)
+        act(T.Trot[:, :], B[4][:, 0:NP], AF.Copy, ["bk4"], ["Trot"])
+        act(T[crn][:, :], T.IOT[:, :].indirect(T.cl[:, :]), AF.Copy, ["IOT", "cl"], [crn])
+        gather(2)
+        if t == 0:
+            act(T.thr[:, :], B[6][:, 0:NP], AF.Copy, ["bk6"], ["thr"])
+            act(T.lim[:, :], T.thr[:, :], AF.Copy, ["thr"], ["lim"])
+        else:
+            act(T.lim[:, :], T.thr[:, :], AF.Identity, ["thr", "a256"], ["lim"], bias=T.aa[:, 1:2])
+        if t > 0:
+            card_c2(t - 1)
+            tt(B[5][:, NP:2 * NP], B[5][:, NP:2 * NP], T.Hp[:, :], OP.min, ["C1", "bk5", "Hp"], ["bk5", "R3p"])
+        mm(B[7][:, 0:NP], T.Ih[:, 0:128], T.Th[:, :], True, True, ["Ih", "Th"], ["bk7"])
+        sumx(1)
+        ts(T.ff[:, :], B[2][:, 0:NP], 0.0, OP.is_equal, None, None, ["bk2"], ["ff"])
+        ts(T.oh[:, :], B[2][:, 0:NP], 1.0, OP.max, T.cols[:, 2:3], OP.is_equal, ["bk2", "cols"], ["oh"])
+        tt(T.fT[:, :], B[7][:, 0:NP], T.ff[:, :], OP.mult, ["ff", "bk7"], ["fT"])
+        pt = B[3][:, 0:NP]
+        mm(pt, rot("Ih"), T.Th[:, :], True, False, ["Ih", "Th"], ["bk3"])
+        mm(pt, rot("E15"), T.ff[:, :], False, False, ["E15", "ff"], ["bk3"])
+        mm(pt, rot("IN"), T.oh[:, :], False, False, ["IN", "oh"], ["bk3"])
+        mm(pt, rot("SI"), T.fT[:, :], False, False, ["SI", "fT"], ["bk3"])
+        mm(B[2][:, 0:NP], MB(0), T.oneh[:, :], True, False, ["MB", "oneh"], ["bk2"])
+        pac = B[4][:, NP:2 * NP]
+        mm(pac, T.Ib[:, :], T.xc[:, :], True, False, ["Ib", "xc"], ["bk4"])
+        mm(pac, MB(7), T.oneh[:, :], False, False, ["MB", "oneh"], ["bk4"])
+        if t > 0:
+            turn2(t - 1)
+        chunk(1)
+        summ(1)
+        fours(2, 1)
+        if t > 0:
+            turned()
+        tt(T.ohc[:, :], T.oh[:, :], T[crn][:, :], OP.mult, ["oh", crn], ["ohc"])
+        sumx(2)
+        mm(pt, rot("Ih"), T.ohc[:, :], False, False, ["Ih", "ohc"], ["bk3"])
+        chunk(2)
+        summ(2)
+
+        tt(T.ok[:, :], B[0][:, 0:NP], T.lim[:, :], OP.is_le, ["bk0", "lim"], ["ok"])
+        mm(B[1][:, 0:NP], T.TUi[:, :], T.ok[:, :], True, True, ["TUi", "ok"], ["bk1"])
+        mm(B[2][:, 0:NP], rot("TUr"), T.ok[:, :], False, True, ["TUr", "ok"], ["bk2"])
+        mm(pt, rot("BH"), T.ok[:, :], False, True, ["BH", "ok"], ["bk3"])
+        mm(B[0][:, 256:268], T.Ih[:, 0:128], T.b16h[:, :], True, False, ["Ih", "b16h"], ["bk0"])
+        ts(T.K1[:, :], B[1][:, 0:NP], 0.5, OP.is_ge, None, None, ["bk1"], ["K1"])
+        mm(pac, MB(2), T.K1[:, :], False, True, ["MB", "K1"], ["bk4"])
+        diag(B[0][:, 256:268], "Wk", "K1", 0, 1, ["K1"], "bk0", first=False)
+        tt(T.fst[:, :], B[2][:, 0:NP], T.Trot[:, :], OP.max, ["bk2", "Trot"], ["fst"])
+        tt(T.Tc[:, :], B[3][:, 0:NP], T.fst[:, :], OP.min, ["bk3", "fst"], ["Tc"])
+        if not last:
+            to = T["TO%d" % t]
+            nxt = T.cores[(rank + 1) % len(T.cores)]
+            ts(to[:, :], T.Tc[:, :], 1536.0, OP.add, None, None, ["Tc"], ["TO%d" % t])
+            rid, pid = topo.addr(nxt, core)
+            mask = 0
+            for e in send_engines(topo, core, nxt):
+                mask |= 1 << e
+            op("G", lambda to=to, t=t, rid=rid, pid=pid, mask=mask: g.remote_dma(T["TT%d" % (t + 1)][:, :], to[:, :], T.sem["arr%d" % (t + 1)], T.sem.snd, pid, rid, mask),
+               ["TO%d" % t], [], dma="snd")
+        mm(B[1][:, NP:2 * NP], MB(4), T.oneh[:, :], True, False, ["MB", "oneh"], ["bk1"])
+        mm(B[1][:, NP:2 * NP], MB(3), T.K1[:, :], False, True, ["MB", "K1"], ["bk1"])
+        mm(B[3][:, 0:NP], MB(5), T.oneh[:, :], True, False, ["MB", "oneh"], ["bk3"])
+        mm(B[3][:, 0:NP], T.TU8[:, :], T.ok[:, :], False, False, ["TU8", "ok"], ["bk3"])
+        mm(B[3][:, 0:NP], MB(1), T.K1[:, :], False, True, ["MB", "K1"], ["bk3"])
+        tt(T.ac[:, :], B[4][:, NP:2 * NP], T.na[:, :], OP.max, ["bk4", "na"], ["ac"])
+        if t > 0:
+            hand_end()
+        cp(T.kl[:, :], B[0][:, 256:268], ["bk0"], ["kl"])
+        tt(T.vv[:, :], T.XT[:, :].indirect(T.kl[:, :]), T.ac[:, :], OP.add, ["XT0", "XT1", "XT2", "kl", "ac"], ["vv"])
+        tt(T.uu[:, :], B[1][:, NP:2 * NP], T.vv[:, :], OP.mult, ["bk1", "vv"], ["uu"])
+        act(T.au[:, :], T.uu[:, :], AF.Abs, ["uu"], ["au"])
+        tt(T.Tcap[:, :], B[3][:, 0:NP], T.Th[:, :], OP.max, ["bk3", "Th"], ["Tcap"])
+        if not last:
+            diag(B[0][:, 192:204], "W0", "K1", 0, 1, ["K1"], "bk0")
+        turn1()
+        ts(T.y[:, :], T.au[:, :], RND, OP.add, -RND, OP.add, ["au"], ["y"])
+        diag(B[1][:, 0:12], "Ww", "y", 0, 1, ["y"], "bk1")
+        hand_begin(t)
+        mm(B[2][:, NP:2 * NP], T.BA[:, :], T.IH[:, NP:2 * NP], True, True, ["BA", "hinv"], ["bk2"])
+        diag(B[2][:, 384:408 if last else 420], "W256", "IH", 0, 2 if last else 3, ["inv", "hinv", "hfr"], "bk2")
+        if not last:
+            tt(S(5), B[0][:, 192:204], T.cf[:, :], OP.mult, ["bk0", "cf"], ["s5"])
+            ts(S(9), B[0][:, 192:204], -4096.0, OP.mult, 4096.0, OP.add, ["bk0"], ["s9"])
+        cp(T.zi[:, :], B[1][:, 0:12], ["bk1"], ["zi"])
+        ts(T.zj[:, :], T.zi[:, :], 15, OP.bitwise_and, None, None, ["zi"], ["zj"])
+        tt(T.zk[:, :], T.zj[:, :], T.b16i[:, :], OP.add, ["zj", "b16i"], ["zk"])
+        cp(T.zl[:, :], T.zk[:, :], ["zk"], ["zl"])
+        cp(T.X[:, :].indirect(T.zl[:, :]), T.y[:, :], ["y", "zl", "Xp"], ["X"])
+        if not last:
+            ts(T.nd[:, :], B[2][:, 384:396], -1.0 / 256, OP.mult, 16.0, OP.add, ["bk2"], ["nd"])
+            empties(256.0)
+            tt(S(7), B[0][:, 192:204], T.nd[:, :], OP.mult, ["bk0", "nd"], ["s7"])
+            tt(S(6), S(1), S(5), OP.max, ["s1", "s5"], ["s6"])
+            tt(S(8), S(7), B[0][:, 256:268], OP.subtract, ["s7", "bk0"], ["s8"])
+            op("V", lambda: g.vector.tensor_reduce(T.aa[:, 0:1], S(8), AxisListType.X, OP.add), ["s8"], ["ar"])
+            mm(B[4][:, 0:1], T.onesf[:, :], T.aa[:, 0:1], True, True, ["onesf", "ar"], ["bk4"])
+            ts(T.smi[:, 0:12], T.b37[:, 12 * t + 12:12 * t + 24], B[4][:, 0:1], OP.add, None, None, ["b37", "bk4"], ["fi"])
+            ts(T.smi[:, 12:24], T.smi[:, 0:12], 2047, OP.bitwise_and, None, None, ["fi"], ["fj"])
+            tt(S(4), S(9), T.smi[:, 12:24], OP.min, ["s9", "fj"], ["s4"])
+            tt(S(3), S(6), S(4), OP.max, ["s6", "s4"], ["s3"])
+            tt(T.cf[:, :], S(0), S(3), OP.min, ["s0", "s3"], ["cf"])
+            cp(T.cl[:, :], T.cf[:, :], ["cf"], ["cl"])
+            cp(T.xc[:, :], T.X[:, :].indirect(T.cl[:, :]), ["X", "Xp", "cl"], ["xc"])
+        if t == 0:
+            matrices3()
+        act(B[5][:, 0:NP], B[2][:, NP:2 * NP], AF.Identity, ["bk2", "WB"], ["bk5", "wall"], bias=T.WB[:, t:t + 1], scale=-4096.0)
+        mm(B[3][:, NP:2 * NP], MB(6), T.oneh[:, :], True, False, ["MB", "oneh"], ["bk3"])
+        mm(B[3][:, NP:2 * NP], MB(1), T.K1[:, :], False, False, ["MB", "K1"], ["bk3"])
+
+    dma("S", "ox", T.yx[:, :], T.X[:, 0:3072], ["X"], [])
+    lists()
+    turn2(V - 1)
+    card_c(V - 1)
+    turned()
+    ts(T.oya[:, :], T.Tc[:, :], 1536.0, OP.add, None, None, ["Tc"], ["oya"])
+    ts(T.IH[:, 0:NP], T.Tc[:, :], EMPTY, OP.is_lt, None, None, ["Tc"], ["inv"])
+    tt(T.oyt[:, :], T.oya[:, :], T.IH[:, 0:NP], OP.mult, ["oya", "inv"], ["oyt"])
+    dma("S", "ot", T.yt[:, :], T.oyt[:, :], ["oyt"], [])
+    card_c2(V - 1)
+    tt(B[5][:, NP:2 * NP], B[5][:, NP:2 * NP], T.Hp[:, :], OP.min, ["C1", "bk5", "Hp"], ["bk5", "R3p"])
+    hand_end()
+    ts(T.IH[:, NP:2 * NP], T.Hs[:, :], EMPTY, OP.is_lt, None, None, ["Hs"], ["hinv"])
+    mm(B[1][:, 0:NP], T.UR[:, :], T.Hs[:, :], True, True, ["UR", "Hs"], ["bk1"])
+    mm(B[0][0:8, 0:2 * NP], T.M8[:, :], T.IH[:, 0:2 * NP], True, True, ["M8", "inv", "hinv"], ["bk0"])
+    ts(T.oyb[:, :], B[1][:, 0:NP], 1536.0, OP.add, None, None, ["bk1"], ["oyb"])
+    ts(T.oya[:, :], B[1][:, 0:NP], EMPTY, OP.is_lt, None, None, ["bk1"], ["oya"])
+    tt(T.oyh[:, :], T.oya[:, :], T.oyb[:, :], OP.mult, ["oya", "oyb"], ["oyh"])
+    dma("S", "oh", T.yh[:, :], T.oyh[:, :], ["oyh"], [])
+    cp(T.omn[:, :], B[0][0:8, 0:2 * NP], ["bk0"], ["omn"])
+    dma("A", "on", T.yn[:, :], T.omn[:, 0:NP], ["omn"], [])
+    dma("A", "om", T.ym[:, :], T.omn[:, NP:2 * NP], ["omn"], [])
+
+    emit(g, core, T, topo, ops, rank)
+
+
+def emit(g, core, T, topo, ops, rank):
+    Q = {"V": g.vector, "A": g.scalar, "P": g.tensor, "G": g, "S": g.sync}
+    sems = {"V": "qV", "A": "qA", "P": "qP", "G": "qG"}
+    seq, pos = {}, {}
+    for k, o in enumerate(ops):
+        pos[k] = len(seq.setdefault(o["q"], []))
+        seq[o["q"]].append(k)
+    know = {q: ({}, set()) for q in "VAPGS"}
+    after, needed, waits = {}, set(), {}
+    for k, o in enumerate(ops):
+        q = o["q"]
+        if q == "R":
+            after[k] = ({}, set())
+            continue
+        kn, kd = know[q]
+        wl = []
+
+        def learn(d):
+            wl.append(d)
+            kn2, kd2 = after[d]
+            for a in kn2:
+                kn[a] = max(kn.get(a, -1), kn2[a])
+            kd.update(kd2)
+
+        need = {}
+        for d in sorted(o["deps"], reverse=True):
+            od = ops[d]
+            if not od["dma"]:
+                need[od["q"]] = max(need.get(od["q"], -1), pos[d])
+            elif d not in kd:
+                kd.add(d)
+                learn(d)
+        for q2 in sorted(need, key=lambda a: -seq[a][need[a]]):
+            p = need[q2]
+            if kn.get(q2, -1) < p:
+                kn[q2] = p
+                needed.add(seq[q2][p])
+                learn(seq[q2][p])
+        waits[k] = wl
+        after[k] = (dict(kn), set(kd))
+    for q in "VAPG":
+        comp = [k for k in seq.get(q, []) if not ops[k]["dma"]]
+        if comp:
+            needed.add(comp[-1])
+    count = {}
+    cnt = {q: 0 for q in "VAPG"}
+    for k, o in enumerate(ops):
+        if k in needed:
+            cnt[o["q"]] += 1
+            count[k] = cnt[o["q"]]
+    n = len(T.cores)
+    ein = len(send_engines(topo, T.cores[(rank - 1) % n], core))
+    eout = len(send_engines(topo, core, T.cores[(rank + 1) % n]))
+    nsend = 0
+    for k, o in enumerate(ops):
+        q = o["q"]
+        if q == "R":
+            continue
+        e = Q[q]
+        for d in waits[k]:
+            od = ops[d]
+            if od["dma"]:
+                e.wait_ge(T.sem[od["dma"]], ein if od["dma"][:3] == "arr" else 16)
+            else:
+                e.wait_ge(T.sem[sems[od["q"]]], count[d])
+        ins = o["f"]()
+        if o["dma"] == "snd":
+            nsend += 1
+        elif o["dma"]:
+            ins.then_inc(T.sem[o["dma"]], 16)
+        elif k in needed:
+            ins.then_inc(T.sem[sems[q]], 1)
+    for k, o in enumerate(ops):
+        if o["dma"] and o["dma"] != "snd":
+            g.wait_ge(T.sem[o["dma"]], ein if o["dma"][:3] == "arr" else 16)
+    g.wait_ge(T.sem.snd, eout * nsend)
+    for q in "VAPG":
+        if cnt[q]:
+            g.wait_ge(T.sem[sems[q]], cnt[q])

@@ -1,61 +1,38 @@
-from concourse.mybir import AluOpType, AxisListType, ActivationFunctionType
+from concourse.mybir import AluOpType, ActivationFunctionType
 
 OP = AluOpType
 AF = ActivationFunctionType
 V = 6
 NP = 192
 CW = 3088
-EMPTY = 1536.0
-PARTS = ("MX", "cols", "b", "RW", "RA", "WIN", "WINA", "MB")
-CA = 8 * 16 * (191 * 192 // 2)
-RND = 8388608.0
+E = 1536.0
+NH = 8192
+OFF = 3072.5
+R2 = 1.5 * 2 ** 24
+R2K = 1.5 * 2 ** 34
+BIG = 30000.0
+PIECES = ((0, 64, "A"), (64, 64, "A"), (128, 16, "V"), (144, 32, "A"), (176, 16, "A"))
 
+F16 = ("Ih:256 W1:144 Ipen Sh SI Moh M15 MH ShN CI PI PK B16 HQ RA:384 RW:512 IL I3 tA tB M8:8 R8 R8n "
+       "Th:192 fT:192 Tapp:192 Hs:192 Hp:192 Tg:192 u:192 DG:768 KB:48 ZB:12 AB:78 nmh:576 Tc:192 VL:384")
+B16 = ("raw:272 smB:272 smC:256 tm:272 Ib NIb BAb NB W1b:144 W2:144 WN:144 Ww:144 TUi TUr:256 BH:256 "
+       "C15 CE15 CE CP CPL CR ones:192 half:192 onesq xc:192 ok:192 y2:192 cap:192 kap:14 rA:14")
+F32 = ("crep:192 ohc:192 Trot:192 fst:192 ac:192 Rv:192 RR:192 t0:192 oyt:192 oyh:192 cw:16 cols:24 "
+       "iq:12 bi:12 D0:36 D1:40 cf:36 rr:14 zt:12 x1:12 acc:2 r8")
 SCRATCH = {
-    "X": ("sbuf", [128, CW], "bfloat16"),
-    "XT": ("sbuf", [128, 3072], "bfloat16"),
-    "MX": ("sbuf", [128, 3072], "bfloat16"),
-    "IOT": ("sbuf", [128, 3072], "float32"),
-    "WIN": ("sbuf", [128, 4096], "float32"),
-    "WINA": ("sbuf", [128, 1024], "float32"),
-    "RW": ("sbuf", [128, 16 * 128], "float16"), "RA": ("sbuf", [128, 4 * 128], "float16"), "Tg": ("sbuf", [128, NP], "float16"),
-    "qm": ("sbuf", [128, 12], "uint16"),
-    "nmi": ("sbuf", [8, 576], "int32"), "nmf": ("sbuf", [8, 576], "float32"), "R8": ("sbuf", [8, 128], "float32"),
+    "X": ("sbuf", [128, CW], "bfloat16"), "XT": ("sbuf", [128, NH + 3072], "bfloat16"), "MX": ("sbuf", [128, 3072], "bfloat16"),
+    "IOT": ("sbuf", [128, 3072], "float32"), "WIN": ("sbuf", [128, 4096], "float32"), "WINA": ("sbuf", [128, 1024], "float32"),
+    "nmi": ("sbuf", [8, 576], "int32"), "omn": ("sbuf", [8, 2 * NP], "float32"),
     "tri": ("sbuf", [128, NP], "int32"), "hai": ("sbuf", [128, NP], "int32"), "wti": ("sbuf", [128, 1], "int32"),
-    "smB": ("sbuf", [128, 272], "bfloat16"), "smC": ("sbuf", [128, 256], "bfloat16"), "smA": ("sbuf", [128, 256], "bfloat16"),
-    "cwi": ("sbuf", [128, 16], "int32"), "cwj": ("sbuf", [128, 16], "int32"), "cw": ("sbuf", [128, 16], "float32"),
-    "SC": ("sbuf", [128, 16], "float32"), "E0": ("sbuf", [128, 16], "float32"), "PC": ("sbuf", [128, 16], "float32"),
-    "WB": ("sbuf", [128, 16], "float32"), "cols": ("sbuf", [128, 16], "float32"),
-    "iq": ("sbuf", [128, 12], "float32"), "bi": ("sbuf", [128, 12], "float32"), "b16i": ("sbuf", [128, 12], "int32"),
-    "b16h": ("sbuf", [128, 12], "float16"), "b37": ("sbuf", [128, 12 * V], "float32"),
-    "onesf": ("sbuf", [128, 128], "float32"), "ones": ("sbuf", [128, NP], "bfloat16"), "oneh": ("sbuf", [128, NP], "float16"),
-    "Ib": ("sbuf", [128, 128], "bfloat16"), "NB": ("sbuf", [128, 128], "bfloat16"),
-    "W2": ("sbuf", [128, 144], "bfloat16"), "WN": ("sbuf", [128, 144], "bfloat16"), "Ww": ("sbuf", [128, 144], "bfloat16"),
-    "Wk": ("sbuf", [128, 144], "float16"), "W0": ("sbuf", [128, 144], "float16"), "W256": ("sbuf", [128, 144], "float16"),
-    "Ih": ("sbuf", [128, 256], "float16"), "SI": ("sbuf", [128, 256], "float16"), "E15": ("sbuf", [128, 256], "float16"),
-    "IN": ("sbuf", [128, 256], "float16"), "TUr": ("sbuf", [128, 256], "float16"), "BA": ("sbuf", [128, 128], "float16"),
-    "BH": ("sbuf", [128, 256], "float16"), "TUi": ("sbuf", [128, 128], "float16"), "TU8": ("sbuf", [128, 128], "float16"),
-    "I8": ("sbuf", [128, 128], "float16"), "I8n": ("sbuf", [128, 128], "float16"), "MB": ("sbuf", [128, 8 * 128], "float16"),
-    "M8": ("sbuf", [128, 8], "float16"), "UR": ("sbuf", [128, 128], "float16"),
-    "thr": ("sbuf", [128, NP], "float32"), "lim": ("sbuf", [128, NP], "float32"),
-    "Th": ("sbuf", [128, NP], "float16"), "IH": ("sbuf", [128, 3 * NP], "float16"), "Hs": ("sbuf", [128, NP], "float16"),
-    "Hp": ("sbuf", [128, NP], "float16"), "ff": ("sbuf", [128, NP], "float16"), "oh": ("sbuf", [128, NP], "float16"),
-    "fT": ("sbuf", [128, NP], "float16"), "ohc": ("sbuf", [128, NP], "float16"), "crep0": ("sbuf", [128, NP], "float32"),
-    "crep1": ("sbuf", [128, NP], "float32"),
-    "Trot": ("sbuf", [128, NP], "float32"), "xc": ("sbuf", [128, NP], "bfloat16"), "na": ("sbuf", [128, NP], "bfloat16"),
-    "ok": ("sbuf", [128, NP], "float16"), "K1": ("sbuf", [128, NP], "float16"), "fst": ("sbuf", [128, NP], "float16"),
-    "Tc": ("sbuf", [128, NP], "float16"), "ac": ("sbuf", [128, NP], "float32"), "vv": ("sbuf", [128, NP], "float32"),
-    "uu": ("sbuf", [128, NP], "float32"), "au": ("sbuf", [128, NP], "float32"), "y": ("sbuf", [128, NP], "bfloat16"),
-    "Tcap": ("sbuf", [128, NP], "float16"), "hoc": ("sbuf", [128, NP], "float16"),
-    "Rv": ("sbuf", [128, NP], "float32"), "R2": ("sbuf", [128, NP], "float32"),
-    "cf": ("sbuf", [128, 12], "float32"), "cl": ("sbuf", [128, 12], "uint16"), "kl": ("sbuf", [128, 12], "uint16"),
-    "zl": ("sbuf", [128, 12], "uint16"), "ql": ("sbuf", [128, 12], "uint16"),
-    "zi": ("sbuf", [128, 12], "int32"), "zj": ("sbuf", [128, 12], "int32"), "zk": ("sbuf", [128, 12], "int32"),
-    "x1": ("sbuf", [128, 12], "float32"), "nd": ("sbuf", [128, 12], "float32"),
-    "sm": ("sbuf", [128, 12 * 10], "float32"), "smi": ("sbuf", [128, 12 * 5], "int32"),
-    "aa": ("sbuf", [128, 4], "float32"), "ai": ("sbuf", [128, 2], "int32"),
-    "oyh": ("sbuf", [128, NP], "float32"), "oyt": ("sbuf", [128, NP], "float32"), "oya": ("sbuf", [128, NP], "float32"),
-    "oyb": ("sbuf", [128, NP], "float32"), "omn": ("sbuf", [8, 2 * NP], "float32"),
+    "cwi": ("sbuf", [128, 32], "int32"), "abi": ("sbuf", [128, 144], "int32"), "zf": ("sbuf", [128, 12], "int32"),
+    "xi": ("sbuf", [128, 36], "int32"),
+    "cl": ("sbuf", [128, 12], "uint16"), "kl": ("sbuf", [128, 12], "uint16"), "zl": ("sbuf", [128, 12], "uint16"),
+    "ql": ("sbuf", [128, 24], "uint16"),
 }
+for _names, _dt in ((F16, "float16"), (B16, "bfloat16"), (F32, "float32")):
+    for _n in _names.split():
+        _n, _w = (_n.split(":") + ["128"])[:2]
+        SCRATCH[_n] = ("sbuf", [128, int(_w)], _dt)
 for _i in range(8):
     SCRATCH["bk%d" % _i] = ("psum", [128, 512], "float32")
 for _i in range(V):
@@ -78,36 +55,30 @@ def rank_program(g, core, T, topo):
     ops = []
     writer, readers, bank = {}, {}, {}
 
-    def op(q, f, r=(), w=(), dma=None):
+    def op(q, f, r="", w="", dma=None):
         k = len(ops)
+        r, w = r.split(), w.split()
         deps = set()
         for n in r:
-            if n[:2] == "bk":
-                continue
-            if n in writer:
-                deps.add(writer[n])
-            readers.setdefault(n, []).append(k)
+            if n[:2] != "bk":
+                if n in writer:
+                    deps.add(writer[n])
+                readers.setdefault(n, []).append(k)
         for n in w:
-            if n[:2] == "bk":
-                continue
-            if n in writer and (ops[writer[n]]["q"] != q or ops[writer[n]]["dma"] or n.rstrip("0123456789_") not in PARTS):
-                deps.add(writer[n])
-            for i in readers.get(n, []):
-                if i != k:
-                    deps.add(i)
-            writer[n] = k
-            readers[n] = []
-        for n in list(r) + list(w):
+            if n[:2] != "bk":
+                if n in writer:
+                    deps.add(writer[n])
+                deps.update(i for i in readers.get(n, []) if i != k)
+                writer[n] = k
+                readers[n] = []
+        for n in r + w:
             if n[:2] == "bk":
                 a = bank.setdefault(n, {})
-                for q2 in a:
-                    if q2 != q:
-                        deps.add(a[q2])
+                deps.update(a[q2] for q2 in a if q2 != q)
                 a[q] = k
         ops.append({"q": q, "f": f, "deps": deps, "dma": dma})
-        return k
 
-    def ts(out, in0, s1, o1, s2, o2, r, w):
+    def ts(out, in0, s1, o1, r, w, s2=None, o2=None):
         if o2 is None:
             op("V", lambda: g.vector.tensor_scalar(out, in0, s1, None, o1), r, w)
         else:
@@ -119,8 +90,8 @@ def rank_program(g, core, T, topo):
     def cp(out, a, r, w):
         op("V", lambda: g.vector.tensor_copy(out, a), r, w)
 
-    def act(out, a, fn, r, w, bias=0.0, scale=1.0):
-        op("A", lambda: g.scalar.activation(out, a, fn, bias=bias, scale=scale), r, w)
+    def act(out, a, fn, r, w, bias=0.0, scale=1.0, acc=None):
+        op("A", lambda: g.scalar.activation(out, a, fn, bias=bias, scale=scale, accum_out=acc), r, w)
 
     def mm(out, l, rr, st, sp, r, w):
         op("P", lambda: g.tensor.matmul(out, l, rr, st, sp), r, w)
@@ -130,186 +101,212 @@ def rank_program(g, core, T, topo):
         op(q, lambda: e.dma_start(out, in_), r, w, dma="d_" + name)
 
     def ms(ap, c, w):
-        op("V", lambda: g.vector.memset(ap, c), [], [w])
+        op("V", lambda: g.vector.memset(ap, c), "", w)
 
-    def MB(j):
-        return T.MB[:, 128 * j:128 * j + 128]
+    def iota(out, pat, base, cm, w):
+        op("G", lambda: g.iota(out, pat, base, cm, allow_small_or_imprecise_dtypes=True), "", w)
 
-    def S(j):
-        return T.sm[:, 12 * j:12 * j + 12]
-
-    def diag(o, mat, src, so, n, r, wb, first=True):
+    def diag(o, mat, src, lo, hi, r, wb, first=False):
         for j in range(16):
-            mm(o, T[mat][:, 16 - j:144 - j], T[src][:, so + j:so + NP * n:16], first and j == 0, j == 15, r + [mat], [wb])
+            mm(o, T[mat][:, 16 - j:144 - j], T[src][:, lo + j:hi:16], first and j == 0, j == 15, r + " " + mat, wb)
 
     B = [T["bk%d" % i] for i in range(8)]
-    SP = T.SC[:, 15:16]
 
-    dma("S", "dm", T.nmi[:, NP:2 * NP], T.mh[:, :], [], ["nmi_m"])
-    dma("A", "dh", T.hai[:, :], T.hands[:, :], [], ["hai"])
-    dma("S", "dn", T.nmi[:, 0:NP], T.nt[:, :], [], ["nmi_n"])
-    dma("A", "dx", T.X[:, 0:3072], T.x0[:, :], [], ["X"])
-    dma("S", "dt", T.tri[:, :], T.trains[:, :], [], ["tri"])
-    dma("S", "dth", T.nmi[:, 2 * NP:3 * NP], T.th[:, :], [], ["nmi_t"])
-    dma("S", "dw", T.wti[:, :], T.wt[:, :], [], ["wti"])
+    def L(b):
+        return B[b][:, 0:NP]
 
-    blk = [[0, 2], [-16, 8], [0, 16]]
-    blk2 = [[0, 2], [16, 8], [0, 16]]
-    op("G", lambda: g.iota(T.cwi[:, :], [[1, 16]], 128, -1), [], ["cwi"])
-    op("G", lambda: g.iota(T.smA[:, :], [[0, 16], [1, 16]], 0, 0, allow_small_or_imprecise_dtypes=True), [], ["smA"])
-    ms(T.R8[:, :], 1.0, "R8")
-    ms(T.smB[:, 0:16], -99.0, "smBp")
+    def H(b):
+        return B[b][:, NP:2 * NP]
+
+    def A(nm):
+        return T[nm][:, :]
+
+    K1, INV, HINV, HFR = (T.DG[:, NP * j:NP * j + NP] for j in range(4))
+
+    dma("S", "dn", T.nmi[:, 0:NP], T.nt[:, :], "", "nmi0")
+    dma("A", "dm", T.nmi[:, NP:2 * NP], T.mh[:, :], "", "nmi1")
+    dma("S", "dt", A("tri"), T.trains[:, :], "", "tri")
+    dma("A", "dh", A("hai"), T.hands[:, :], "", "hai")
+    dma("S", "dx", T.X[:, 0:3072], T.x0[:, :], "", "X")
+    dma("A", "dth", T.nmi[:, 2 * NP:3 * NP], T.th[:, :], "", "nmi2")
+    dma("A", "dw", A("wti"), T.wt[:, :], "", "wti")
+
+    op("G", lambda: g.iota(T.cwi[:, 0:16], [[1, 16]], 128, -1), "", "cwi")
+    iota(T.tm[:, 0:144], [[1, 144]], -16, -1, "tm")
+    iota(T.r8[0:8, :], [[1, 8], [0, 16]], 0, -1, "r8")
+    iota(A("iq"), [[16, 12]], 0, 0, "iq")
+    iota(A("IOT"), [[1, 3072]], -3072, 0, "IOT")
+    ms(A("ones"), 1.0, "ones")
     ms(T.X[:, 3072:CW], 0.0, "Xp")
-    ms(T.onesf[:, :], 1.0, "onesf")
-    ms(T.ones[:, :], 1.0, "ones")
-    for b in (6, 7):
-        ms(B[b][:, 192:256], 0.0, "bk%d" % b)
+    ts(T.cwi[:, 16:32], T.cwi[:, 0:16], 15, OP.bitwise_and, "cwi", "cwj")
+    cp(A("cw"), T.cwi[:, 16:32], "cwj", "cw")
+    cols = {}
 
-    def blocks(nm, fill, o):
-        op("G", lambda: g.affine_select(T[nm][:, o:o + 256], T.smA[:, :], blk, OP.is_ge, fill, 0, 1), ["smA"], [nm])
-        op("G", lambda: g.affine_select(T[nm][:, o:o + 256], T[nm][:, o:o + 256], blk2, OP.is_ge, fill, 15, -1), [nm], [nm])
+    def col(nm, src, a, o1, b=None, o2=None):
+        cols[nm] = T.cols[:, len(cols):len(cols) + 1]
+        if src in cols:
+            ts(cols[nm], cols[src], a, o1, "c_" + src, "c_" + nm, b, o2)
+        else:
+            ts(cols[nm], T.cw[:, src:src + 1], a, o1, "cw", "c_" + nm, b, o2)
 
-    blocks("smB", -99.0, 16)
-    op("G", lambda: g.affine_select(T.R8[:, :], T.R8[:, :], [[1, 128]], OP.is_ge, 0.0, 0, -16), ["R8"], ["R8"])
-    op("G", lambda: g.affine_select(T.R8[:, :], T.R8[:, :], [[-1, 128]], OP.is_ge, 0.0, 15, 16), ["R8"], ["R8"])
-    op("G", lambda: g.iota(T.iq[:, :], [[16, 12]], 0, 0, allow_small_or_imprecise_dtypes=True), [], ["iq"])
-    blocks("smC", 99.0, 0)
-    op("G", lambda: g.iota(T.IOT[:, :], [[1, 3072]], -1536, 0, allow_small_or_imprecise_dtypes=True), [], ["IOT"])
+    col("s", 15, -1.0, OP.mult, 15.0, OP.add)
+    ts(T.raw[:, 0:144], T.tm[:, 0:144], cols["s"], OP.add, "tm c_s", "raw")
+    ts(T.raw[:, 144:272], T.tm[:, 16:144], cols["s"], OP.add, "tm c_s", "raw2")
+    rw, rw2, rp = T.raw[:, 16:144], T.raw[:, 16:272], T.raw[:, 0:144]
+    sb, sb2 = T.smB[:, 16:144], T.smB[:, 16:272]
 
-    smb = T.smB[:, 16:144]
-    smb2 = T.smB[:, 16:272]
-    smp = T.smB[:, 0:144]
-    ts(T.cwj[:, :], T.cwi[:, :], 15, OP.bitwise_and, None, None, ["cwi"], ["cwj"])
-    cp(T.cw[:, :], T.cwj[:, :], ["cwj"], ["cw"])
-    ts(T.SC[:, :], T.cw[:, :], -1.0, OP.mult, 15.0, OP.add, ["cw"], ["SC"])
-    ts(T.E0[:, :], T.cw[:, :], 0.0, OP.is_equal, None, None, ["cw"], ["E0"])
-    ts(T.cols[:, 0:1], SP, 1.0, OP.is_ge, None, None, ["SC"], ["cols"])
-    ts(T.cols[:, 1:2], SP, -1.0, OP.add, None, None, ["SC"], ["cols"])
-    ts(T.cols[:, 2:3], SP, -1.0, OP.mult, 16.0, OP.add, ["SC"], ["cols"])
-    row0 = (1536.0, -4096.0, 512.0, -1025.0 / 2048, 1.0, 2048.0, 6144.0, -512.0)
-    for j, v in enumerate(row0):
-        ts(T.cols[:, 3 + j:4 + j], T.E0[:, 0:1], v, OP.mult, None, None, ["E0"], ["cols"])
-    ts(T.PC[:, :], T.E0[:, :], 5632.0, OP.mult, -4096.0, OP.add, ["E0"], ["PC"])
-    ts(T.WB[:, :], T.SC[:, :], -4096.0, OP.mult, 4096.0 * 16.5, OP.add, ["SC"], ["WB"])
-    ts(T.W0[:, :], smp, 0.0, OP.is_equal, T.E0[:, 0:1], OP.mult, ["smB", "smBp", "E0"], ["W0"])
+    def eye(nm, at, by=None, src=None, out=None):
+        rd = ("smB" if src is sb else "raw raw2") + " c_" + at + (" c_" + by if by in cols else "")
+        ts(A(nm) if out is None else out, rw if src is None else src, cols[at], OP.is_equal, rd, nm,
+           cols.get(by, by), None if by is None else OP.mult)
 
-    ts(T.Ib[:, :], smb, SP, OP.is_equal, None, None, ["smB", "SC"], ["Ib"])
-    ts(T.NB[:, :], smb, 0.0, OP.is_ge, -1.0, OP.mult, ["smB"], ["NB"])
-    ts(T.W2[:, :], smp, 0.0, OP.is_equal, 2.0, OP.mult, ["smB", "smBp"], ["W2"])
-    ts(T.WN[:, :], smp, 0.0, OP.is_equal, -1.0, OP.mult, ["smB", "smBp"], ["WN"])
-    ts(T.BA[:, :], smb, 0.0, OP.is_ge, None, None, ["smB"], ["BA"])
-    ts(T.I8[:, :], smb, SP, OP.is_equal, 8192.0, OP.mult, ["smB", "SC"], ["I8"])
-    ts(T.Ih[:, :], smb2, SP, OP.is_equal, None, None, ["smB", "SC"], ["Ih"])
+    def blk(nm, by, src=None):
+        ts(A(nm), sb if src is None else src, 0.0, OP.is_ge, "smB" + (" c_" + by if by in cols else ""), nm, cols.get(by, by), OP.mult)
 
-    def spread(j, nm, b):
-        cp(T.nmf[:, NP * j:NP * j + NP], T.nmi[:, NP * j:NP * j + NP], [nm], [nm + "f"])
-        mm(B[b][:, 0:NP], T.R8[:, :], T.nmf[:, NP * j:NP * j + NP], True, True, ["R8", nm + "f"], ["bk%d" % b])
+    def scaled(nm, src, by):
+        act(A(nm), A(src), AF.Identity, src + (" c_" + by if by in cols else ""), nm, scale=cols.get(by, by))
 
-    spread(1, "nmi_m", 4)
-    ts(T.bi[:, :], T.iq[:, :], SP, OP.add, None, None, ["iq", "SC"], ["bi"])
-    ts(T.b37[:, 0:12], T.bi[:, :], 37.0, OP.mult, None, None, ["bi"], ["b37"])
-    ts(T.oyt[:, :], B[4][:, 0:NP], SP, OP.is_le, 3072.0, OP.mult, ["bk4", "SC"], ["tb"])
-    tt(T.oyb[:, :], T.oyt[:, :], T.hai[:, :], OP.max, ["tb", "hai"], ["h0f"])
-    ts(T.Hs[:, :], T.oyb[:, :], -1536.0, OP.add, None, None, ["h0f"], ["Hs"])
-    diag(B[2][:, 408:420], "W0", "Hs", 0, 1, ["Hs"], "bk2")
-    spread(0, "nmi_n", 5)
-    ts(T.oyh[:, :], B[5][:, 0:NP], SP, OP.is_le, 3072.0, OP.mult, ["bk5", "SC"], ["ta"])
-    tt(T.oya[:, :], T.oyh[:, :], T.tri[:, :], OP.max, ["ta", "tri"], ["t0f"])
-    cp(T.TT0[:, :], T.oya[:, :], ["t0f"], ["TT0"])
+    eye("Ib", "s")
+    col("cr", "s", 8192.0, OP.mult, 4096.0, OP.add)
+    scaled("CR", "Ib", "cr")
+    ts(T.R8n[0:8, :], T.r8[0:8, :], 0.0, OP.is_equal, "r8", "R8n", -8.0, OP.mult)
 
-    def empties(scale):
-        pd = B[2][:, 408:420]
-        ts(S(1), pd, EMPTY * scale, OP.is_lt, 4096.0, OP.mult, ["bk2"], ["s1"])
-        ts(S(0), pd, 1.0 / scale, OP.mult, 1536.0, OP.add, ["bk2"], ["s0"])
+    def masked(j, src, b):
+        ts(T.nmh[0:8, NP * j:NP * j + NP], T.nmi[:, NP * j:NP * j + NP], 1024.0, OP.mult, "nmi%d" % j, "nmh%d" % j)
+        mm(L(b), T.R8n[0:8, :], T.nmh[0:8, NP * j:NP * j + NP], True, False, "R8n nmh%d" % j, "bk%d" % b)
+        mm(L(b), A("CR"), A("ones"), False, True, "CR ones", "bk%d" % b)
+        tt(A("t0"), L(b), A(src), OP.max, "bk%d %s" % (b, src), "t0")
 
-    empties(1.0)
-    cp(T.smi[:, 0:12], T.b37[:, 0:12], ["b37"], ["fi"])
-    ts(T.smi[:, 12:24], T.smi[:, 0:12], 2047, OP.bitwise_and, None, None, ["fi"], ["fj"])
-    tt(S(4), S(1), T.smi[:, 12:24], OP.max, ["fj", "s1"], ["s4"])
-    tt(T.cf[:, :], S(0), S(4), OP.min, ["s0", "s4"], ["cf"])
-    cp(T.cl[:, :], T.cf[:, :], ["cf"], ["cl"])
+    col("e0", 0, 0.0, OP.is_equal)
+    col("e15", 15, 0.0, OP.is_equal)
+    ts(A("W1"), rp, 0.0, OP.is_equal, "raw", "W1")
+    ts(T.tm[:, 0:272], T.raw[:, 0:272], 16.0, OP.is_ge, "raw raw2", "tm", -200.0, OP.mult)
+    masked(1, "hai", 4)
+    ts(A("Hs"), A("t0"), 3072.0, OP.min, "t0", "Hs", -E, OP.add)
+    ts(HFR, A("Hs"), cols["e0"], OP.mult, "Hs c_e0", "hfr")
+    masked(0, "tri", 5)
+    ts(A("TT0"), A("t0"), 3072.0, OP.min, "t0", "TT0")
+    diag(B[2][:, 292:304], "W1", "DG", 3 * NP, 4 * NP, "hfr", "bk2", first=True)
+    ts(A("bi"), A("iq"), cols["s"], OP.add, "iq c_s", "bi")
+    ms(A("D0"), BIG, "D0a D0b D0c")
+    ms(T.D0[:, 1:36:3], -BIG, "D0b")
+    ms(A("D1"), BIG, "D1a D1b D1c")
+    ms(T.D1[:, 36:37], OFF, "D1a")
+    ts(T.abi[:, 0:12], A("bi"), 37.0, OP.mult, "bi", "abi")
+    ts(T.abi[:, 72:84], T.abi[:, 0:12], 2047, OP.bitwise_and, "abi", "abj")
+    ts(T.D1[:, 0:36:3], T.abi[:, 72:84], OFF, OP.add, "abj", "D1a")
 
-    def matrices():
-        ts(T.SI[:, :], smb2, T.cols[:, 1:2], OP.is_equal, None, None, ["smB", "cols"], ["SI"])
-        ts(T.E15[:, :], smb2, 15.0, OP.is_equal, T.cols[:, 3:4], OP.mult, ["smB", "cols"], ["E15"])
-        tt(T.SI[:, :], T.SI[:, :], T.Ih[:, :], OP.subtract, ["SI", "Ih"], ["SI"])
-        ts(T.IN[:, :], smb2, SP, OP.is_equal, -1536.0, OP.mult, ["smB", "SC"], ["IN"])
-        ts(T.TUr[:, :], T.smC[:, :], SP, OP.is_lt, -4096.0, OP.mult, ["smC", "SC"], ["TUr"])
-        ts(T.TUi[:, :], T.smC[:, 0:128], SP, OP.is_le, None, None, ["smC", "SC"], ["TUi"])
-        ts(T.TU8[:, :], T.smC[:, 0:128], SP, OP.is_lt, 4096.0, OP.mult, ["smC", "SC"], ["TU8"])
-        ts(T.BH[:, :], smb2, 0.0, OP.is_ge, 8192.0, OP.mult, ["smB"], ["BH"])
-        for j in range(len(row0)):
-            ts(MB(j), smb, 0.0, OP.is_ge, T.cols[:, 3 + j:4 + j], OP.mult, ["smB", "cols"], ["MB"])
+    def front():
+        act(T.D1[:, 2:36:3], B[2][:, 292:304], AF.Identity, "bk2", "D1c", bias=E + OFF)
+        act(T.D0[:, 2:36:3], B[2][:, 292:304], AF.Identity, "bk2", "D0c", bias=16384.0 * (E - 0.5), scale=-16384.0)
+
+    def choose():
+        op("V", lambda: g.vector.tensor_tensor_scan(A("cf"), A("D0"), T.D1[:, 0:36], 0.0, OP.max, OP.min),
+           "D0a D0b D0c D1a D1b D1c", "cf")
+
+    def clist():
+        ts(A("cl"), T.cf[:, 2:36:3], -OFF, OP.add, "cf", "cl")
+
+    def crep():
+        act(A("crep"), A("IOT").indirect(A("cl")), AF.Copy, "IOT cl", "crep")
+
+    front()
+    tt(A("smB"), A("raw"), A("tm"), OP.add, "raw raw2 tm", "smB")
+    choose()
+    clist()
+    ts(A("W1b"), rp, 0.0, OP.is_equal, "raw", "W1b")
+    blk("BAb", 1.0)
+    scaled("NB", "BAb", -8.0)
+    scaled("WN", "W1b", -8.0)
+    scaled("W2", "W1b", 16.0)
+    col("ic", "e15", 3840.0, OP.mult, 256.0, OP.add)
+    col("ip", "e15", -240.0, OP.mult, 256.0, OP.add)
+    eye("Ipen", "s", "ip")
+    ts(T.nmh[0:8, 2 * NP:3 * NP], T.nmi[:, 2 * NP:3 * NP], -2040.0, OP.add, "nmi2", "nmh2")
+    col("s0", "e0", -200.0, OP.mult, -1.0, OP.add)
+    cols["sm"] = T.cols[:, len(cols):len(cols) + 1]
+    tt(cols["sm"], cols["s0"], cols["s"], OP.add, "c_s0 c_s", "c_sm")
+    eye("Sh", "sm")
+
+    def more_constants():
+        col("m15", "e15", -1.0 / 4096, OP.mult)
+        blk("M15", "m15")
+        col("n15", "e15", -1.0, OP.add)
+        eye("tA", "s", "n15")
+        tt(A("SI"), A("Sh"), A("tA"), OP.add, "Sh tA", "SI")
+        col("sp", "s", 1.0, OP.add)
+        eye("tB", "sp", None, src=sb)
+        tt(A("tA"), A("tA"), A("tB"), OP.add, "tA tB", "tA")
+        ts(A("Moh"), A("tA"), -1.0 / 256, OP.mult, "tA", "Moh")
+        eye("Ih", "s", src=rw2)
+        scaled("C15", "Ib", "e15")
+        scaled("CE15", "C15", E)
+        scaled("CE", "Ib", E)
+        scaled("NIb", "Ib", -1.0)
+
+    def late_constants():
+        ts(T.tm[:, 0:256], rw2, 0.0, OP.is_lt, "raw raw2", "tm", 300.0, OP.mult)
+        tt(A("smC"), rw2, T.tm[:, 0:256], OP.add, "raw raw2 tm", "smC")
+        ts(A("TUi"), T.smC[:, 0:128], cols["s"], OP.is_le, "smC c_s", "TUi")
+        ts(A("TUr"), A("smC"), cols["s"], OP.is_lt, "smC c_s", "TUr", -4096.0, OP.mult)
+        blk("BH", 4096.0, src=sb2)
+        col("kc", "e0", -float(NH) - 1, OP.mult, 1.0, OP.add)
+        col("mh", "e0", -512.0 / NH, OP.mult)
+        blk("MH", "mh")
+        for w in range(1, 4):
+            col("a%d" % w, 15 - w, -1.0, OP.mult, 15.0, OP.add)
+            eye("RA%d" % w, "a%d" % w, out=T.RA[:, 128 * w - 128:128 * w])
+        ms(A("KB"), 0.0, "KB")
+        ts(T.KB[:, 0:12], A("bi"), 16.0, OP.mult, "bi KB", "KB0", float(NH), OP.add)
+        cp(T.KB[:, 12:24], A("bi"), "bi KB", "KB1")
+        ms(A("ZB"), -7.5 / 16, "ZB")
+        ms(A("half"), 0.5, "half")
+        cols["w"] = T.cols[:, len(cols):len(cols) + 1]
+        ts(cols["w"], A("wti"), 1.0 / 32, OP.mult, "wti", "c_w")
+        scaled("Ww", "W1b", "w")
+        ts(A("ShN"), A("Sh"), -512.0, OP.mult, "Sh", "ShN")
+        col("ci", "e15", 1.875, OP.mult, -2.0, OP.add)
+        eye("CI", "s", "ci")
+        ms(A("onesq"), 1.0, "onesq")
+        ms(T.kap[:, 0:12], 1.0, "kap0")
+        ms(T.kap[:, 12:14], 8.0, "kap1")
         for t in range(1, V):
-            ts(T.b37[:, 12 * t:12 * t + 12], T.bi[:, :], 37.0, OP.mult, float(613 * t + CA), OP.add, ["bi"], ["b37"])
-        ts(T.b16h[:, :], T.bi[:, :], 16.0, OP.mult, None, None, ["bi"], ["b16h"])
-        ts(T.Wk[:, :], smp, 0.0, OP.is_equal, T.cols[:, 0:1], OP.mult, ["smB", "smBp", "cols"], ["Wk"])
-        ts(T.W256[:, :], smp, 0.0, OP.is_equal, 256.0, OP.mult, ["smB", "smBp"], ["W256"])
-        cp(T.oneh[:, :], T.ones[:, :], ["ones"], ["oneh"])
+            ts(T.abi[:, 12 * t:12 * t + 12], A("bi"), 37.0, OP.mult, "bi", "abi%d" % t, float(613 * t), OP.add)
+        ts(T.abi[:, 84:144], T.abi[:, 12:72], 2047, OP.bitwise_and, "abi1 abi2 abi3 abi4 abi5", "abk")
+        ms(A("AB"), -1023.5, "AB")
+        for t in range(1, V):
+            ts(T.AB[:, 13 * t:13 * t + 12], T.abi[:, 72 + 12 * t:84 + 12 * t], -1023.5, OP.add, "abk AB", "AB%d" % t)
 
-    def matrices2():
-        cp(T.cols[:, 12:13], T.wti[:, :], ["wti"], ["wtf"])
-        ts(T.b16i[:, :], T.bi[:, :], 16.0, OP.mult, None, None, ["bi"], ["b16i"])
-        ts(T.I8n[:, :], smb, SP, OP.is_equal, -4096.0, OP.mult, ["smB", "SC"], ["I8n"])
-        ts(T.Ww[:, :], smp, 0.0, OP.is_equal, T.cols[:, 12:13], OP.mult, ["smB", "smBp", "wtf"], ["Ww"])
+    def hand_constants():
+        for h in range(4):
+            ts(T.RW[:, 128 * h:128 * h + 128], rw, T.cw[:, 14 - 4 * h:15 - 4 * h], OP.is_equal, "raw cw", "RW%d" % h)
+        blk("B16", 16.0)
+        col("pi", "e15", -15.0, OP.mult, 16.0, OP.add)
+        blk("PI", "pi")
+        col("pk", "e0", -4080.0, OP.mult, 4096.0, OP.add)
+        blk("PK", "pk")
+        col("cp", "s", 4096.0, OP.mult, 2048.0 * 65, OP.add)
+        scaled("CP", "Ib", "cp")
+        col("hc", "e15", -85.0, OP.mult, 99.0, OP.add)
+        ts(A("HQ"), sb, cols["hc"], OP.min, "smB c_hc c_sm", "HQ", cols["sm"], OP.is_equal)
 
-        for w in range(4):
-            ts(T.RA[:, 128 * w:128 * w + 128], smb, T.SC[:, 15 - w:16 - w], OP.is_equal, None, None, ["smB", "SC"], ["RA"])
+    def last_constants():
+        col("cq", "cp", -4096.0, OP.add)
+        scaled("CPL", "Ib", "cq")
+        eye("IL", "s", -512.0)
+        eye("I3", "s", 3072.0)
+        ts(A("M8"), T.raw[:, 16:144:16], 0.0, OP.is_equal, "raw", "M8")
 
-    def matrices3():
-        for w in range(16):
-            ts(T.RW[:, 128 * w:128 * w + 128], smb, T.cw[:, w:w + 1], OP.is_equal, None, None, ["smB", "cw"], ["RW"])
-        ts(T.M8[:, :], T.smB[:, 16:144:16], 0.0, OP.is_ge, None, None, ["smB"], ["M8"])
-        ts(T.UR[:, :], smb, T.SC[:, V - 1:V], OP.is_equal, None, None, ["smB", "SC"], ["UR"])
+    def hand_flags():
+        ts(HINV, A("Hp"), E, OP.is_ge, "Hp", "hinv", 256.0, OP.mult)
+        ts(HFR, A("Hp"), cols["e0"], OP.mult, "Hp c_e0", "hfr")
 
+    def hand_merge(nm):
+        tt(A("RR"), L(3), A("Rv"), OP.max, "bk3 Rv", "RR")
+        tt(A(nm), H(5), A("RR"), OP.min, "bk5 RR", nm)
 
-    def turn1():
-        for c in range(2):
-            for h in range(2):
-                w = 2 * c + h
-                mm(B[6 + c][:, 256 * h:256 * h + NP], T.RA[:, 128 * w:128 * w + 128], T.Tcap[:, :], True, True, ["RA", "Tcap"], ["bk%d" % (6 + c)])
-            act(T.WINA[:, 512 * c:512 * c + 448], B[6 + c][:, 0:448], AF.Copy, ["bk%d" % (6 + c)], ["WINA"])
+    xt_all = " ".join("XT%d" % j for j in range(len(PIECES)))
 
-    def turn2(t):
-        cp(T.Tg[:, :], T.WINA[:, :].indirect(T.ql[:, :]), ["WINA", "ql"], ["Tg"])
-        for c in range(2):
-            for h in range(2):
-                w = (t + 1 - 4 * (2 * c + h)) % 16
-                mm(B[6 + c][:, 256 * h:256 * h + NP], T.RW[:, 128 * w:128 * w + 128], T.Tg[:, :], True, True, ["RW", "Tg"], ["bk%d" % (6 + c)])
-
-    def turned():
-        for c in range(2):
-            for h in range(2):
-                o = 1024 * (2 * c + h)
-                act(T.WIN[:, o:o + NP], B[6 + c][:, 256 * h:256 * h + NP], AF.Copy, ["bk%d" % (6 + c)], ["WIN"])
-        act(T.Rv[:, :], T.WIN[:, :].indirect(T.qm[:, :]), AF.Copy, ["WIN", "qm"], ["Rv"])
-
-    def lists():
-        tt(T.x1[:, :], B[2][:, 384:396], T.bi[:, :], OP.add, ["bk2", "bi"], ["x1"])
-        tt(T.smi[:, 24:36], B[2][:, 396:408], T.x1[:, :], OP.add, ["bk2", "x1"], ["x2"])
-        ts(T.smi[:, 36:48], T.smi[:, 24:36], 1023, OP.bitwise_and, None, None, ["x2"], ["x3"])
-        ts(T.smi[:, 48:60], T.smi[:, 24:36], 3072 + 255, OP.bitwise_and, None, None, ["x2"], ["x4"])
-        cp(T.ql[:, :], T.smi[:, 36:48], ["x3"], ["ql"])
-        cp(T.qm[:, :], T.smi[:, 48:60], ["x4"], ["qm"])
-
-    def card_c(t):
-        ts(T.hoc[:, :], B[2][:, NP:2 * NP], T.SC[:, t:t + 1], OP.add, 16.0, OP.is_equal, ["bk2", "SC"], ["hoc"])
-        mm(B[3][:, NP:2 * NP], T.I8n[:, :], T.hoc[:, :], False, True, ["I8n", "hoc"], ["bk3"])
-
-    def card_c2(t):
-        tt(B[5][:, NP:2 * NP], B[3][:, NP:2 * NP], T["crep%d" % (t % 2)][:, :], OP.max, ["bk3", "crep%d" % (t % 2)], ["bk5", "C1"])
-
-    def hand_end():
-        tt(T.R2[:, :], B[5][:, 0:NP], T.Rv[:, :], OP.max, ["Rv", "bk5", "wall"], ["R2"])
-        tt(T.Hs[:, :], B[5][:, NP:2 * NP], T.R2[:, :], OP.min, ["R2", "bk5", "R3p"], ["Hs"])
-
-    def hand_begin(t):
-        ts(T.Hp[:, :], T.Hs[:, :], T.PC[:, t:t + 1], OP.max, None, None, ["Hs", "PC"], ["Hp"])
-        ts(T.IH[:, NP:2 * NP], T.Hp[:, :], EMPTY, OP.is_ge, None, None, ["Hp"], ["hinv"])
-        if t < V - 1:
-            ts(T.IH[:, 2 * NP:3 * NP], T.Hp[:, :], T.E0[:, t + 1:t + 2], OP.mult, None, None, ["Hp", "E0"], ["hfr"])
-
-    cp(T.xc[:, :], T.X[:, :].indirect(T.cl[:, :]), ["X", "Xp", "cl"], ["xc"])
     for t in range(V):
         last = t == V - 1
         tn = "TT%d" % t
@@ -320,186 +317,195 @@ def rank_program(g, core, T, topo):
         def rot(nm):
             return T[nm][:, ro:ro + 128] if jj else T[nm][:, 0:128]
 
-        def chunk(c):
-            for s in range(4):
-                o = 256 * (c % 2)
-                tt(T.MX[:, 1024 * c + s:1024 * c + 1024:4], B[1][:, o:o + 256], T.XT[:, 1024 * c + s:1024 * c + 1024:4], OP.max,
-                   ["bk1", "XT%d" % c], ["MX%d_%d" % (c, s)])
+        def gather(j):
+            p, n, q = PIECES[j]
+            out, src = T.XT[:, 16 * p:16 * (p + n)], A("X").indirect(tab[:, p:p + n])
+            if q == "A":
+                act(out, src, AF.Identity, "X Xp " + tn, "XT%d" % j, bias=-2.0)
+            else:
+                ts(out, src, -2.0, OP.add, "X Xp " + tn, "XT%d" % j)
 
-        def fours(c, n):
+        def maxes(j):
+            p, n, q = PIECES[j]
+            b, o = (1, 4 * p) if p < 128 else (2, 4 * (p - 128))
             for s in range(4):
-                mm(B[1][:, s:256 * n:4], T.Ib[:, :], T.xc[:, 64 * c:64 * c + 64 * n], True, True, ["Ib", "xc"], ["bk1"])
+                tt(T.MX[:, 16 * p + s:16 * (p + n):4], B[b][:, o:o + 4 * n], T.XT[:, 16 * p + s:16 * (p + n):4], OP.max,
+                   "bk%d XT%d" % (b, j), "MX%d_%d" % (j, s))
+
+        def fours(b, p, n):
+            for s in range(4):
+                mm(B[b][:, s:4 * n:4], A("Ib"), T.xc[:, p:p + n], True, True, "Ib xc", "bk%d" % b)
+
+        def inside(c):
+            return [j for j in range(len(PIECES)) if PIECES[j][0] // 64 == c]
 
         def sumx(c):
             for s in range(16):
-                mm(B[0][:, 64 * c:64 * c + 64], T.WN[:, 16 - s:144 - s], T.XT[:, 1024 * c + s:1024 * c + 1024:16], False, False, ["WN", "XT%d" % c], ["bk0"])
+                mm(B[0][:, 64 * c:64 * c + 64], T.WN[:, 16 - s:144 - s], T.XT[:, 1024 * c + s:1024 * c + 1024:16], False, False,
+                   "WN " + " ".join("XT%d" % j for j in inside(c)), "bk0")
 
         def summ(c):
             for k in range(16):
                 s = k // 4 + 4 * (k % 4)
                 mm(B[0][:, 64 * c:64 * c + 64], T.W2[:, 16 - s:144 - s], T.MX[:, 1024 * c + s:1024 * c + 1024:16], False, c == 2 and k == 15,
-                   ["W2", "MX%d_%d" % (c, s % 4)], ["bk0"])
+                   "W2 " + " ".join("MX%d_%d" % (j, s % 4) for j in inside(c)), "bk0")
 
         if t > 0:
-            op("R", None, [], [tn], dma="arr%d" % t)
-        cp(T.xc[:, :], T.X[:, :].indirect(T.cl[:, :]), ["X", "Xp", "cl"], ["xc"])
-        def gather(c):
-            act(T.XT[:, 1024 * c:1024 * c + 1024], T.X[:, :].indirect(tab[:, 64 * c:64 * c + 64]), AF.Copy, ["X", "Xp", tn], ["XT%d" % c])
-
-        crn = "crep%d" % (t % 2)
-        fours(0, 2)
-        mm(B[0][:, 0:NP], T.NB[:, :], T.xc[:, :], True, False, ["NB", "xc"], ["bk0"])
-        if t > 0:
-            lists()
-            ts(T.ai[:, 0:1], B[4][:, 0:1], float(CA), OP.add, None, None, ["bk4"], ["ai0"])
-            ts(T.ai[:, 1:2], T.ai[:, 0:1], 255, OP.bitwise_and, None, None, ["ai0"], ["ai1"])
-            cp(T.aa[:, 1:2], T.ai[:, 1:2], ["ai1"], ["a256"])
-            card_c(t - 1)
-        ts(T.Th[:, :], tab[:, :], -1536.0, OP.add, None, None, [tn], ["Th"])
-        ts(T.IH[:, 0:NP], tab[:, :], 3072.0, OP.is_ge, None, None, [tn], ["inv"])
-        ts(T.na[:, :], T.xc[:, :], -1.0, OP.mult, None, None, ["xc"], ["na"])
+            op("R", None, "", tn, dma="arr%d" % t)
+        ts(A("xc"), A("X").indirect(A("cl")), -2.0, OP.add, "X Xp cl", "xc")
         gather(0)
-        mm(B[2][:, 0:NP], T.BA[:, :], T.IH[:, 0:NP], True, True, ["BA", "inv"], ["bk2"])
-        mm(B[4][:, 0:NP], rot("Ih"), T.Th[:, :], True, True, ["Ih", "Th"], ["bk4"])
-        mm(B[0][:, 0:NP], T.I8[:, :], T.IH[:, 0:NP], False, False, ["I8", "inv"], ["bk0"])
-        sumx(0)
-        chunk(0)
-        summ(0)
-        if t == 0:
-            spread(2, "nmi_t", 6)
-            matrices()
-            matrices2()
-        gather(1)
-        act(T.Trot[:, :], B[4][:, 0:NP], AF.Copy, ["bk4"], ["Trot"])
-        act(T[crn][:, :], T.IOT[:, :].indirect(T.cl[:, :]), AF.Copy, ["IOT", "cl"], [crn])
-        gather(2)
-        if t == 0:
-            act(T.thr[:, :], B[6][:, 0:NP], AF.Copy, ["bk6"], ["thr"])
-            act(T.lim[:, :], T.thr[:, :], AF.Copy, ["thr"], ["lim"])
+        fours(1, 0, 128)
+        mm(L(0), A("NB"), A("xc"), True, False, "NB xc", "bk0")
+        mm(L(0), T.R8n[0:8, :], T.nmh[0:8, 2 * NP:3 * NP], False, False, "R8n nmh2", "bk0")
+        fours(2, 128, 64)
+        ts(A("Th"), A(tn), -E, OP.add, tn, "Th")
+        ts(INV, A(tn), 3072.0, OP.is_ge, tn + " c_ic", "inv", cols["ic"], OP.mult)
+        if t > 0:
+            hand_merge("Hp")
+            hand_flags()
         else:
-            act(T.lim[:, :], T.thr[:, :], AF.Identity, ["thr", "a256"], ["lim"], bias=T.aa[:, 1:2])
-        if t > 0:
-            card_c2(t - 1)
-            tt(B[5][:, NP:2 * NP], B[5][:, NP:2 * NP], T.Hp[:, :], OP.min, ["C1", "bk5", "Hp"], ["bk5", "R3p"])
-        mm(B[7][:, 0:NP], T.Ih[:, 0:128], T.Th[:, :], True, True, ["Ih", "Th"], ["bk7"])
+            more_constants()
+            mm(L(6), A("Sh"), A("Hs"), True, False, "Sh Hs", "bk6")
+            mm(L(6), A("CE15"), A("ones"), False, True, "CE15 ones", "bk6")
+            cp(A("Hp"), L(6), "bk6", "Hp")
+            hand_flags()
+        mm(L(0), A("Ipen"), INV, False, False, "Ipen inv", "bk0")
+        mm(L(3), A("M15"), INV, True, True, "M15 inv", "bk3")
+        mm(H(3), A("Moh"), INV, True, False, "Moh inv", "bk3")
+        mm(H(3), A("C15"), A("ones"), False, True, "C15 ones", "bk3")
+        mm(L(4), A("Sh"), A("Th"), True, False, "Sh Th", "bk4")
+        mm(L(4), A("CE15"), A("ones"), False, False, "CE15 ones", "bk4")
+        gather(1)
+        if t == 0:
+            crep()
+        gather(2)
+        tt(A("fT"), L(3), A("Th"), OP.mult, "bk3 Th", "fT")
+        sumx(0)
+        maxes(0)
+        mm(L(4), A("SI"), A("fT"), False, True, "SI fT", "bk4")
+        summ(0)
+        tt(A("ohc"), H(3), A("crep"), OP.mult, "bk3 crep", "ohc")
+        tt(A("Tapp"), L(4), A("ohc"), OP.add, "bk4 ohc", "Tapp")
+        if t == 0:
+            late_constants()
+        maxes(2)
+        gather(3)
+        gather(4)
+        mm(L(5), rot("Ih"), A("Tapp"), True, False, "Ih Tapp", "bk5")
+        mm(L(4), rot("Ih"), A("Th"), True, True, "Ih Th", "bk4")
+        mm(L(3), A("Ib"), A("xc"), True, False, "Ib xc", "bk3")
+        for w in range(4):
+            m = T.RA[:, 128 * w - 128:128 * w] if w else T.Ih[:, 0:128]
+            mm(B[6 + w // 2][:, 256 * (w % 2):256 * (w % 2) + NP], m, A("Tapp"), True, True, "Ih RA1 RA2 RA3 Tapp", "bk%d" % (6 + w // 2))
         sumx(1)
-        ts(T.ff[:, :], B[2][:, 0:NP], 0.0, OP.is_equal, None, None, ["bk2"], ["ff"])
-        ts(T.oh[:, :], B[2][:, 0:NP], 1.0, OP.max, T.cols[:, 2:3], OP.is_equal, ["bk2", "cols"], ["oh"])
-        tt(T.fT[:, :], B[7][:, 0:NP], T.ff[:, :], OP.mult, ["ff", "bk7"], ["fT"])
-        pt = B[3][:, 0:NP]
-        mm(pt, rot("Ih"), T.Th[:, :], True, False, ["Ih", "Th"], ["bk3"])
-        mm(pt, rot("E15"), T.ff[:, :], False, False, ["E15", "ff"], ["bk3"])
-        mm(pt, rot("IN"), T.oh[:, :], False, False, ["IN", "oh"], ["bk3"])
-        mm(pt, rot("SI"), T.fT[:, :], False, False, ["SI", "fT"], ["bk3"])
-        mm(B[2][:, 0:NP], MB(0), T.oneh[:, :], True, False, ["MB", "oneh"], ["bk2"])
-        pac = B[4][:, NP:2 * NP]
-        mm(pac, T.Ib[:, :], T.xc[:, :], True, False, ["Ib", "xc"], ["bk4"])
-        mm(pac, MB(7), T.oneh[:, :], False, False, ["MB", "oneh"], ["bk4"])
-        if t > 0:
-            turn2(t - 1)
-        chunk(1)
+        maxes(1)
         summ(1)
-        fours(2, 1)
-        if t > 0:
-            turned()
-        tt(T.ohc[:, :], T.oh[:, :], T[crn][:, :], OP.mult, ["oh", crn], ["ohc"])
+        maxes(3)
         sumx(2)
-        mm(pt, rot("Ih"), T.ohc[:, :], False, False, ["Ih", "ohc"], ["bk3"])
-        chunk(2)
+        maxes(4)
         summ(2)
+        act(A("Trot"), L(4), AF.Copy, "bk4", "Trot")
+        mm(H(4), A("Ib"), T.XT[:, 0:3072:16], True, False, "Ib " + xt_all, "bk4")
+        mm(H(4), A("NIb"), A("xc"), False, True, "NIb xc", "bk4")
+        for w in range(4):
+            act(T.WINA[:, 256 * w:256 * w + NP], B[6 + w // 2][:, 256 * (w % 2):256 * (w % 2) + NP], AF.Copy, "bk%d" % (6 + w // 2), "WINA%d" % w)
+        act(T.XT[:, NH:NH + 3072:16], H(4), AF.Abs, "bk4", "N0", scale=2.0)
 
-        tt(T.ok[:, :], B[0][:, 0:NP], T.lim[:, :], OP.is_le, ["bk0", "lim"], ["ok"])
-        mm(B[1][:, 0:NP], T.TUi[:, :], T.ok[:, :], True, True, ["TUi", "ok"], ["bk1"])
-        mm(B[2][:, 0:NP], rot("TUr"), T.ok[:, :], False, True, ["TUr", "ok"], ["bk2"])
-        mm(pt, rot("BH"), T.ok[:, :], False, True, ["BH", "ok"], ["bk3"])
-        mm(B[0][:, 256:268], T.Ih[:, 0:128], T.b16h[:, :], True, False, ["Ih", "b16h"], ["bk0"])
-        ts(T.K1[:, :], B[1][:, 0:NP], 0.5, OP.is_ge, None, None, ["bk1"], ["K1"])
-        mm(pac, MB(2), T.K1[:, :], False, True, ["MB", "K1"], ["bk4"])
-        diag(B[0][:, 256:268], "Wk", "K1", 0, 1, ["K1"], "bk0", first=False)
-        tt(T.fst[:, :], B[2][:, 0:NP], T.Trot[:, :], OP.max, ["bk2", "Trot"], ["fst"])
-        tt(T.Tc[:, :], B[3][:, 0:NP], T.fst[:, :], OP.min, ["bk3", "fst"], ["Tc"])
+        ts(A("ok"), L(0), OFF - 8 * 2040.0, OP.add, "bk0 D1a", "ok", T.D1[:, 36:37], OP.is_le)
+        mm(L(2), A("CE"), A("ones"), True, False, "CE ones", "bk2")
+        mm(L(1), A("TUi"), A("ok"), True, True, "TUi ok", "bk1")
+        mm(L(2), rot("TUr"), A("ok"), False, True, "TUr ok", "bk2")
+        mm(L(5), rot("BH"), A("ok"), False, True, "BH ok", "bk5")
+        ts(K1, L(1), 0.5, OP.is_ge, "bk1 c_kc", "K1", cols["kc"], OP.mult)
+        kp = B[0][:, 256:304]
+        mm(kp, T.Ih[:, 0:128], A("KB"), True, False, "Ih KB0 KB1", "bk0")
+        mm(L(3), A("MH"), K1, False, True, "MH K1", "bk3")
+        diag(kp, "W1", "DG", 0, 4 * NP, "K1 inv hinv hfr", "bk0")
+        act(A("ac"), L(3), AF.Relu, "bk3", "ac", bias=3.5 - 512)
+        tt(A("fst"), L(2), A("Trot"), OP.max, "bk2 Trot", "fst")
+        tt(A("Tc"), L(5), A("fst"), OP.min, "bk5 fst", "Tc")
         if not last:
             to = T["TO%d" % t]
             nxt = T.cores[(rank + 1) % len(T.cores)]
-            ts(to[:, :], T.Tc[:, :], 1536.0, OP.add, None, None, ["Tc"], ["TO%d" % t])
+            ts(to[:, :], A("Tc"), E, OP.add, "Tc", "TO%d" % t)
             rid, pid = topo.addr(nxt, core)
             mask = 0
             for e in send_engines(topo, core, nxt):
                 mask |= 1 << e
-            op("G", lambda to=to, t=t, rid=rid, pid=pid, mask=mask: g.remote_dma(T["TT%d" % (t + 1)][:, :], to[:, :], T.sem["arr%d" % (t + 1)], T.sem.snd, pid, rid, mask),
-               ["TO%d" % t], [], dma="snd")
-        mm(B[1][:, NP:2 * NP], MB(4), T.oneh[:, :], True, False, ["MB", "oneh"], ["bk1"])
-        mm(B[1][:, NP:2 * NP], MB(3), T.K1[:, :], False, True, ["MB", "K1"], ["bk1"])
-        mm(B[3][:, 0:NP], MB(5), T.oneh[:, :], True, False, ["MB", "oneh"], ["bk3"])
-        mm(B[3][:, 0:NP], T.TU8[:, :], T.ok[:, :], False, False, ["TU8", "ok"], ["bk3"])
-        mm(B[3][:, 0:NP], MB(1), T.K1[:, :], False, True, ["MB", "K1"], ["bk3"])
-        tt(T.ac[:, :], B[4][:, NP:2 * NP], T.na[:, :], OP.max, ["bk4", "na"], ["ac"])
-        if t > 0:
-            hand_end()
-        cp(T.kl[:, :], B[0][:, 256:268], ["bk0"], ["kl"])
-        tt(T.vv[:, :], T.XT[:, :].indirect(T.kl[:, :]), T.ac[:, :], OP.add, ["XT0", "XT1", "XT2", "kl", "ac"], ["vv"])
-        tt(T.uu[:, :], B[1][:, NP:2 * NP], T.vv[:, :], OP.mult, ["bk1", "vv"], ["uu"])
-        act(T.au[:, :], T.uu[:, :], AF.Abs, ["uu"], ["au"])
-        tt(T.Tcap[:, :], B[3][:, 0:NP], T.Th[:, :], OP.max, ["bk3", "Th"], ["Tcap"])
+            op("G", lambda to=to, t=t, rid=rid, pid=pid, mask=mask: g.remote_dma(
+                T["TT%d" % (t + 1)][:, :], to[:, :], T.sem["arr%d" % (t + 1)], T.sem.snd, pid, rid, mask), "TO%d" % t, "", dma="snd")
+            mm(H(1), A("CI"), INV, True, False, "CI inv", "bk1")
+            mm(H(1), A("MH"), K1, False, False, "MH K1", "bk1")
+            mm(H(1), A("ShN"), K1, False, True, "ShN K1", "bk1")
+        pz = B[2][:, 256:268]
+        mm(pz, T.Ih[:, 0:128], A("ZB"), True, False, "Ih ZB", "bk2")
+        cp(A("kl"), kp[:, 0:12] if False else B[0][:, 256:268], "bk0", "kl")
         if not last:
-            diag(B[0][:, 192:204], "W0", "K1", 0, 1, ["K1"], "bk0")
-        turn1()
-        ts(T.y[:, :], T.au[:, :], RND, OP.add, -RND, OP.add, ["au"], ["y"])
-        diag(B[1][:, 0:12], "Ww", "y", 0, 1, ["y"], "bk1")
-        hand_begin(t)
-        mm(B[2][:, NP:2 * NP], T.BA[:, :], T.IH[:, NP:2 * NP], True, True, ["BA", "hinv"], ["bk2"])
-        diag(B[2][:, 384:408 if last else 420], "W256", "IH", 0, 2 if last else 3, ["inv", "hinv", "hfr"], "bk2")
+            tt(T.D1[:, 1:36:3], B[0][:, 256:268], T.cf[:, 2:36:3], OP.max, "bk0 cf", "D1b")
+        ts(A("x1"), B[0][:, 280:292], 3840.0 if last else 0.0, OP.add, "bk0", "x1")
+        tt(T.xi[:, 0:12], B[0][:, 268:280], A("x1"), OP.add, "bk0 x1", "x2")
+        tt(A("u"), A("XT").indirect(A("kl")), A("ac"), OP.add, xt_all + " N0 kl ac", "u")
         if not last:
-            tt(S(5), B[0][:, 192:204], T.cf[:, :], OP.mult, ["bk0", "cf"], ["s5"])
-            ts(S(9), B[0][:, 192:204], -4096.0, OP.mult, 4096.0, OP.add, ["bk0"], ["s9"])
-        cp(T.zi[:, :], B[1][:, 0:12], ["bk1"], ["zi"])
-        ts(T.zj[:, :], T.zi[:, :], 15, OP.bitwise_and, None, None, ["zi"], ["zj"])
-        tt(T.zk[:, :], T.zj[:, :], T.b16i[:, :], OP.add, ["zj", "b16i"], ["zk"])
-        cp(T.zl[:, :], T.zk[:, :], ["zk"], ["zl"])
-        cp(T.X[:, :].indirect(T.zl[:, :]), T.y[:, :], ["y", "zl", "Xp"], ["X"])
-        if not last:
-            ts(T.nd[:, :], B[2][:, 384:396], -1.0 / 256, OP.mult, 16.0, OP.add, ["bk2"], ["nd"])
-            empties(256.0)
-            tt(S(7), B[0][:, 192:204], T.nd[:, :], OP.mult, ["bk0", "nd"], ["s7"])
-            tt(S(6), S(1), S(5), OP.max, ["s1", "s5"], ["s6"])
-            tt(S(8), S(7), B[0][:, 256:268], OP.subtract, ["s7", "bk0"], ["s8"])
-            op("V", lambda: g.vector.tensor_reduce(T.aa[:, 0:1], S(8), AxisListType.X, OP.add), ["s8"], ["ar"])
-            mm(B[4][:, 0:1], T.onesf[:, :], T.aa[:, 0:1], True, True, ["onesf", "ar"], ["bk4"])
-            ts(T.smi[:, 0:12], T.b37[:, 12 * t + 12:12 * t + 24], B[4][:, 0:1], OP.add, None, None, ["b37", "bk4"], ["fi"])
-            ts(T.smi[:, 12:24], T.smi[:, 0:12], 2047, OP.bitwise_and, None, None, ["fi"], ["fj"])
-            tt(S(4), S(9), T.smi[:, 12:24], OP.min, ["s9", "fj"], ["s4"])
-            tt(S(3), S(6), S(4), OP.max, ["s6", "s4"], ["s3"])
-            tt(T.cf[:, :], S(0), S(3), OP.min, ["s0", "s3"], ["cf"])
-            cp(T.cl[:, :], T.cf[:, :], ["cf"], ["cl"])
-            cp(T.xc[:, :], T.X[:, :].indirect(T.cl[:, :]), ["X", "Xp", "cl"], ["xc"])
+            act(T.cap[:, :], H(1), AF.Relu, "bk1", "cap acc", scale=1.0 / 512, acc=T.acc[:, 0:1])
+            act(T.rA[:, 0:13], T.kap[:, 0:13], AF.Identity, "kap0 kap1 acc", "rA", scale=T.acc[:, 0:1])
+            act(T.D0[:, 1:36:3], B[0][:, 256:268], AF.Identity, "bk0", "D0b", bias=NH + 3071.0, scale=-1.0)
+            act(T.D1[:, 2:36:3], B[0][:, 292:304], AF.Identity, "bk0", "D1c", bias=E + OFF)
+            act(T.D0[:, 2:36:3], B[0][:, 292:304], AF.Identity, "bk0", "D0c", bias=16384.0 * (E - 0.5), scale=-16384.0)
+        ts(T.xi[:, 12:24], T.xi[:, 0:12], 1023, OP.bitwise_and, "x2", "x3")
+        ts(A("y2"), A("u"), R2, OP.add, "u", "y2", -R2, OP.add)
+        diag(pz, "Ww", "y2", 0, NP, "y2", "bk2")
+        ts(T.xi[:, 24:36], T.xi[:, 0:12], 3072 + 255, OP.bitwise_and, "x2", "x4")
+        cp(A("ql"), T.xi[:, 12:36], "x3 x4", "ql")
         if t == 0:
-            matrices3()
-        act(B[5][:, 0:NP], B[2][:, NP:2 * NP], AF.Identity, ["bk2", "WB"], ["bk5", "wall"], bias=T.WB[:, t:t + 1], scale=-4096.0)
-        mm(B[3][:, NP:2 * NP], MB(6), T.oneh[:, :], True, False, ["MB", "oneh"], ["bk3"])
-        mm(B[3][:, NP:2 * NP], MB(1), T.K1[:, :], False, False, ["MB", "K1"], ["bk3"])
+            hand_constants()
+        if t == V - 2:
+            last_constants()
+        cp(A("Tg"), A("WINA").indirect(T.ql[:, 0:12]), "WINA0 WINA1 WINA2 WINA3 ql", "Tg")
+        pa = B[1][:, 400:413]
+        if not last:
+            mm(pa, T.Ih[:, 0:128], T.AB[:, 13 * t + 13:13 * t + 26], True, False, "Ih AB AB%d" % (t + 1), "bk1")
+            mm(pa, A("onesq"), T.rA[:, 0:13], False, True, "onesq rA", "bk1")
+        for h in range(4):
+            mm(B[6 + h // 2][:, 256 * (h % 2):256 * (h % 2) + NP], T.RW[:, 128 * h:128 * h + 128], A("Tg"), True, True,
+               "RW%d Tg" % h, "bk%d" % (6 + h // 2))
+        for h in range(4):
+            act(T.WIN[:, 1024 * h:1024 * h + NP], B[6 + h // 2][:, 256 * (h % 2):256 * (h % 2) + NP], AF.Copy, "bk%d" % (6 + h // 2), "WIN%d" % h)
+        tt(A("zf"), pz, A("bi"), OP.subtract, "bk2 bi", "zf")
+        if not last:
+            ts(T.rr[:, 0:13], pa, R2K, OP.add, "bk1", "rr", -R2K - 4096, OP.add)
+        tt(A("zt"), pz, A("zf"), OP.subtract, "bk2 zf", "zt")
+        if not last:
+            tt(T.D1[:, 0:39:3], pa, T.rr[:, 0:13], OP.subtract, "bk1 rr", "D1a")
+        ts(A("zl"), A("zt"), 16.0, OP.mult, "zt", "zl", 7.5, OP.add)
+        if not last:
+            choose()
+            clist()
+        tt(A("X").indirect(A("zl")), A("y2"), A("half"), OP.mult, "y2 half zl Xp", "X")
+        act(A("Rv"), A("WIN").indirect(T.ql[:, 12:24]), AF.Copy, "WIN0 WIN1 WIN2 WIN3 ql", "Rv")
+        if not last:
+            crep()
+        mm(L(3), A("B16"), HINV, True, False, "B16 hinv", "bk3")
+        mm(L(3), A("IL" if last else "ShN"), HINV, False, False, "IL ShN hinv", "bk3")
+        mm(L(3), A("CPL" if last else "CP"), A("ones"), False, False, "CP CPL ones", "bk3")
+        mm(L(3), A("PI"), INV, False, False, "PI inv", "bk3")
+        mm(L(3), A("PK"), K1, False, True, "PK K1", "bk3")
+        mm(H(5), T.Ih[:, 0:128] if last else A("HQ"), A("Hp"), True, True, "Ih HQ Hp", "bk5")
 
-    dma("S", "ox", T.yx[:, :], T.X[:, 0:3072], ["X"], [])
-    lists()
-    turn2(V - 1)
-    card_c(V - 1)
-    turned()
-    ts(T.oya[:, :], T.Tc[:, :], 1536.0, OP.add, None, None, ["Tc"], ["oya"])
-    ts(T.IH[:, 0:NP], T.Tc[:, :], EMPTY, OP.is_lt, None, None, ["Tc"], ["inv"])
-    tt(T.oyt[:, :], T.oya[:, :], T.IH[:, 0:NP], OP.mult, ["oya", "inv"], ["oyt"])
-    dma("S", "ot", T.yt[:, :], T.oyt[:, :], ["oyt"], [])
-    card_c2(V - 1)
-    tt(B[5][:, NP:2 * NP], B[5][:, NP:2 * NP], T.Hp[:, :], OP.min, ["C1", "bk5", "Hp"], ["bk5", "R3p"])
-    hand_end()
-    ts(T.IH[:, NP:2 * NP], T.Hs[:, :], EMPTY, OP.is_lt, None, None, ["Hs"], ["hinv"])
-    mm(B[1][:, 0:NP], T.UR[:, :], T.Hs[:, :], True, True, ["UR", "Hs"], ["bk1"])
-    mm(B[0][0:8, 0:2 * NP], T.M8[:, :], T.IH[:, 0:2 * NP], True, True, ["M8", "inv", "hinv"], ["bk0"])
-    ts(T.oyb[:, :], B[1][:, 0:NP], 1536.0, OP.add, None, None, ["bk1"], ["oyb"])
-    ts(T.oya[:, :], B[1][:, 0:NP], EMPTY, OP.is_lt, None, None, ["bk1"], ["oya"])
-    tt(T.oyh[:, :], T.oya[:, :], T.oyb[:, :], OP.mult, ["oya", "oyb"], ["oyh"])
-    dma("S", "oh", T.yh[:, :], T.oyh[:, :], ["oyh"], [])
-    cp(T.omn[:, :], B[0][0:8, 0:2 * NP], ["bk0"], ["omn"])
-    dma("A", "on", T.yn[:, :], T.omn[:, 0:NP], ["omn"], [])
-    dma("A", "om", T.ym[:, :], T.omn[:, NP:2 * NP], ["omn"], [])
+    def cards(nm, j, b, out, name):
+        ts(T.VL[:, NP * j:NP * j + NP], A(nm), E, OP.is_lt, nm, "VL%d" % j)
+        mm(L(b), T.Ih[:, 0:128], A(nm), True, False, "Ih " + nm, "bk%d" % b)
+        mm(L(b), A("I3"), T.VL[:, NP * j:NP * j + NP], False, True, "I3 VL%d" % j, "bk%d" % b)
+        act(A(out), L(b), AF.Identity, "bk%d" % b, out, bias=-E)
+        dma("A", name[1], T[name[0]][:, :], A(out), out, "")
+
+    dma("S", "ox", T.yx[:, :], T.X[:, 0:3072], "X", "")
+    cards("Tc", 0, 0, "oyt", ("yt", "ot"))
+    hand_merge("Hs")
+    cards("Hs", 1, 1, "oyh", ("yh", "oh"))
+    mm(B[2][0:8, 0:2 * NP], A("M8"), A("VL"), True, True, "M8 VL0 VL1", "bk2")
+    cp(A("omn"), B[2][0:8, 0:2 * NP], "bk2", "omn")
+    dma("S", "on", T.yn[:, :], T.omn[:, 0:NP], "omn", "")
+    dma("S", "om", T.ym[:, :], T.omn[:, NP:2 * NP], "omn", "")
 
     emit(g, core, T, topo, ops, rank)
 

@@ -8,23 +8,39 @@ CW = 3088
 E = 1536.0
 NH = 8192
 OFF = 3072.5
-R2 = 1.5 * 2 ** 24
 R2K = 1.5 * 2 ** 34
 BIG = 30000.0
-PIECES = ((0, 64, "A"), (64, 64, "A"), (128, 16, "V"), (144, 32, "A"), (176, 16, "A"))
+PIECES = ((0, 64, "A"), (64, 48, "A"), (112, 16, "V"), (128, 16, "V"), (144, 32, "A"), (176, 16, "A"))
+WAKE, DMA, REMOTE, GATHER, SCATTER = 100, 1000, 2000, 1.6, 4.0
 
-F16 = ("Ih:256 W1:144 Ipen Sh SI Moh M15 MH ShN CI PI PK B16 HQ RA:384 RW:512 IL I3 tA tB M8:8 R8 R8n "
-       "Th:192 fT:192 Tapp:192 Hs:192 Hp:192 Tg:192 u:192 DG:768 KB:48 ZB:12 AB:78 nmh:576 Tc:192 VL:384")
-B16 = ("raw:272 smB:272 smC:256 tm:272 Ib NIb BAb NB W1b:144 W2:144 WN:144 Ww:144 TUi TUr:256 BH:256 "
-       "C15 CE15 CE CP CPL CR ones:192 half:192 onesq xc:192 ok:192 y2:192 cap:192 kap:14 rA:14")
-F32 = ("crep:192 ohc:192 Trot:192 fst:192 ac:192 Rv:192 RR:192 t0:192 oyt:192 oyh:192 cw:16 cols:24 "
-       "iq:12 bi:12 D0:36 D1:40 cf:36 rr:14 zt:12 x1:12 acc:2 r8")
+
+def _m(*pieces):
+    return "".join("m%d_%d " % (j, s) for s in range(4) for j in pieces)
+
+
+ORDER = {
+    "V": "xc hinv- hfr- fT ohc g2 Tapp g3 m0_0 x1 m0_1 x2 m0_2 x3 x4 m0_3 ql " + _m(2) + _m(1) + _m(3) + _m(4, 5) +
+         "Tg fst Tc to yt kl D1b u y1 y RR Hp zf rr yh zt D1a zl scan cl Th+ inv+ X",
+    "A": "g0 g1 g4 g5 Trot WINA ad front ok N0 K1 WIN cap D0b Rv yt yh crep",
+    "P": "four1 NB SI four2 LB Trot CE WINA sx0 sm0 sx1 d0a sm1a sm1b sx2 d0b sm2 N0 pt tri ramp WIN kd cap pen yt zd pa yh "
+         "thr+ oh+ pt0+ Ipen+",
+}
+LATER = {(0, "ohc"): {"V": "m2_3"}, (0, "Tapp"): {"V": "m2_3"}, (0, "Trot"): {"P": "sx1", "A": "g5"}, (0, "CE"): {"P": "sx1"},
+         (0, "WINA"): {"P": "sx1", "A": "Trot"}, (1, "Th"): {"V": "xc"}, (1, "inv"): {"V": "xc"},
+         (1, "oh"): {"P": "four1"}, (1, "pt0"): {"P": "four1"}, (1, "Ipen"): {"P": "four1"}}
+
+F16 = "Th:192 fT:192 Tapp:192 Hs:192 Hp:192 Tg:192 u:192 y1:192 DG:576 KB:12 LB:36 AB:78 nmh:576 Tc:192 VL:384"
+B16 = ("raw:144 tm:144 I:256 NI BA NB W1:144 W2:144 Wk:144 WN:144 Ww:144 TUi TUr:256 BH:256 C15 CE15 CE CP CR R8n "
+       "Ipen Sh SI Moh M15 MC CI PI PK PH HQ RA:384 RW:512 I3 tA tB tC ShN B16 M8:8 "
+       "ones:192 xc:192 ok:192 K1:192 y:192 ad:192 cap:192 kap:14 rA:14")
+F32 = ("crep:192 ohc:192 Trot:192 fst:192 Rv:192 RR:192 oyt:192 oyh:192 cw:16 SC:16 E0:16 NE:16 cols:16 "
+       "iq:12 ib:78 bi:12 bz:12 D0:36 D1:40 cf:36 rr:14 zt:12 x1:12 acc:2 r8")
 SCRATCH = {
     "X": ("sbuf", [128, CW], "bfloat16"), "XT": ("sbuf", [128, NH + 3072], "bfloat16"), "MX": ("sbuf", [128, 3072], "bfloat16"),
     "IOT": ("sbuf", [128, 3072], "float32"), "WIN": ("sbuf", [128, 4096], "float32"), "WINA": ("sbuf", [128, 1024], "float32"),
     "nmi": ("sbuf", [8, 576], "int32"), "omn": ("sbuf", [8, 2 * NP], "float32"),
     "tri": ("sbuf", [128, NP], "int32"), "hai": ("sbuf", [128, NP], "int32"), "wti": ("sbuf", [128, 1], "int32"),
-    "cwi": ("sbuf", [128, 32], "int32"), "abi": ("sbuf", [128, 144], "int32"), "zf": ("sbuf", [128, 12], "int32"),
+    "cwi": ("sbuf", [128, 32], "int32"), "abi": ("sbuf", [128, 156], "int32"), "zf": ("sbuf", [128, 12], "int32"),
     "xi": ("sbuf", [128, 36], "int32"),
     "cl": ("sbuf", [128, 12], "uint16"), "kl": ("sbuf", [128, 12], "uint16"), "zl": ("sbuf", [128, 12], "uint16"),
     "ql": ("sbuf", [128, 24], "uint16"),
@@ -53,12 +69,13 @@ def rank_program(g, core, T, topo):
     if rank is None:
         return
     ops = []
-    writer, readers, bank = {}, {}, {}
+    writer, readers, bank, lastq = {}, {}, {}, {}
+    at = [None]
 
-    def op(q, f, r="", w="", dma=None):
+    def op(q, f, r, w, c, dma=None):
         k = len(ops)
         r, w = r.split(), w.split()
-        deps = set()
+        deps, order = set(), set()
         for n in r:
             if n[:2] != "bk":
                 if n in writer:
@@ -72,43 +89,51 @@ def rank_program(g, core, T, topo):
                 writer[n] = k
                 readers[n] = []
         for n in r + w:
-            if n[:2] == "bk":
+            if n[-1] == "+":
+                order.add(bank[n[:-1]]["P"][0])
+                bank[n[:-1]]["P"].append(k)
+            elif n[:2] == "bk":
                 a = bank.setdefault(n, {})
-                deps.update(a[q2] for q2 in a if q2 != q)
-                a[q] = k
-        ops.append({"q": q, "f": f, "deps": deps, "dma": dma})
+                for q2 in a:
+                    if q2 != q:
+                        deps.update(a[q2])
+                if q == "P" and q in a:
+                    order.update(a[q])
+                a[q] = a[q] + [k] if lastq.get(n) == q and q != "P" else [k]
+                lastq[n] = q
+        ops.append({"q": q, "f": f, "deps": deps, "order": order, "dma": dma, "c": c, "at": at[0]})
 
-    def ts(out, in0, s1, o1, r, w, s2=None, o2=None):
+    def ts(out, in0, s1, o1, r, w, s2=None, o2=None, c=70):
         if o2 is None:
-            op("V", lambda: g.vector.tensor_scalar(out, in0, s1, None, o1), r, w)
+            op("V", lambda: g.vector.tensor_scalar(out, in0, s1, None, o1), r, w, c)
         else:
-            op("V", lambda: g.vector.tensor_scalar(out, in0, s1, s2, o1, o2), r, w)
+            op("V", lambda: g.vector.tensor_scalar(out, in0, s1, s2, o1, o2), r, w, c)
 
-    def tt(out, a, b, o, r, w):
-        op("V", lambda: g.vector.tensor_tensor(out, a, b, o), r, w)
+    def tt(out, a, b, o, r, w, c=200):
+        op("V", lambda: g.vector.tensor_tensor(out, a, b, o), r, w, c)
 
-    def cp(out, a, r, w):
-        op("V", lambda: g.vector.tensor_copy(out, a), r, w)
+    def cp(out, a, r, w, c=70):
+        op("V", lambda: g.vector.tensor_copy(out, a), r, w, c)
 
-    def act(out, a, fn, r, w, bias=0.0, scale=1.0, acc=None):
-        op("A", lambda: g.scalar.activation(out, a, fn, bias=bias, scale=scale, accum_out=acc), r, w)
+    def act(out, a, fn, r, w, bias=0.0, scale=1.0, acc=None, c=200):
+        op("A", lambda: g.scalar.activation(out, a, fn, bias=bias, scale=scale, accum_out=acc), r, w, c)
 
-    def mm(out, l, rr, st, sp, r, w):
-        op("P", lambda: g.tensor.matmul(out, l, rr, st, sp), r, w)
+    def mm(out, l, rr, st, sp, r, w, c=100):
+        op("P", lambda: g.tensor.matmul(out, l, rr, st, sp), r, w, c)
 
-    def dma(q, name, out, in_, r, w):
+    def dma(q, name, out, in_, r, w, kb):
         e = {"S": g.sync, "A": g.scalar}[q]
-        op(q, lambda: e.dma_start(out, in_), r, w, dma="d_" + name)
+        op(q, lambda: e.dma_start(out, in_), r, w, DMA + 3 * kb, dma="d_" + name)
 
-    def ms(ap, c, w):
-        op("V", lambda: g.vector.memset(ap, c), "", w)
+    def ms(ap, v, w, c=70):
+        op("V", lambda: g.vector.memset(ap, v), "", w, c)
 
-    def iota(out, pat, base, cm, w):
-        op("G", lambda: g.iota(out, pat, base, cm, allow_small_or_imprecise_dtypes=True), "", w)
+    def iota(out, pat, base, cm, w, n):
+        op("G", lambda: g.iota(out, pat, base, cm, allow_small_or_imprecise_dtypes=True), "", w, 130 + 2 * n)
 
-    def diag(o, mat, src, lo, hi, r, wb, first=False):
+    def diag(o, mat, src, hi, r, wb, first=False):
         for j in range(16):
-            mm(o, T[mat][:, 16 - j:144 - j], T[src][:, lo + j:hi:16], first and j == 0, j == 15, r + " " + mat, wb)
+            mm(o, T[mat][:, 16 - j:144 - j], T[src][:, j:hi:16], first and j == 0, j == 15, r + " " + mat, wb, 34)
 
     B = [T["bk%d" % i] for i in range(8)]
 
@@ -121,191 +146,170 @@ def rank_program(g, core, T, topo):
     def A(nm):
         return T[nm][:, :]
 
-    K1, INV, HINV, HFR = (T.DG[:, NP * j:NP * j + NP] for j in range(4))
+    HFR, HINV, INV = (T.DG[:, NP * j:NP * j + NP] for j in range(3))
+    I = T.I[:, 0:128]
+    G192 = 60 + GATHER * NP
 
-    dma("S", "dn", T.nmi[:, 0:NP], T.nt[:, :], "", "nmi0")
-    dma("A", "dm", T.nmi[:, NP:2 * NP], T.mh[:, :], "", "nmi1")
-    dma("S", "dt", A("tri"), T.trains[:, :], "", "tri")
-    dma("A", "dh", A("hai"), T.hands[:, :], "", "hai")
-    dma("S", "dx", T.X[:, 0:3072], T.x0[:, :], "", "X")
-    dma("A", "dth", T.nmi[:, 2 * NP:3 * NP], T.th[:, :], "", "nmi2")
-    dma("A", "dw", A("wti"), T.wt[:, :], "", "wti")
+    dma("S", "dn", T.nmi[:, 0:NP], T.nt[:, :], "", "nmi0", 6)
+    dma("A", "dm", T.nmi[:, NP:2 * NP], T.mh[:, :], "", "nmi1", 6)
+    dma("S", "dt", A("tri"), T.trains[:, :], "", "tri", 96)
+    dma("A", "dh", A("hai"), T.hands[:, :], "", "hai", 96)
+    dma("S", "dx", T.X[:, 0:3072], T.x0[:, :], "", "X", 960)
+    dma("A", "dth", T.nmi[:, 2 * NP:3 * NP], T.th[:, :], "", "nmi2", 6)
+    dma("A", "dw", A("wti"), T.wt[:, :], "", "wti", 1)
 
-    op("G", lambda: g.iota(T.cwi[:, 0:16], [[1, 16]], 128, -1), "", "cwi")
-    iota(T.tm[:, 0:144], [[1, 144]], -16, -1, "tm")
-    iota(T.r8[0:8, :], [[1, 8], [0, 16]], 0, -1, "r8")
-    iota(A("iq"), [[16, 12]], 0, 0, "iq")
-    iota(A("IOT"), [[1, 3072]], -3072, 0, "IOT")
-    ms(A("ones"), 1.0, "ones")
+    op("G", lambda: g.iota(T.cwi[:, 0:16], [[1, 16]], 128, -1), "", "cwi", 160)
+    iota(A("tm"), [[1, 144]], -16, -1, "tm", 144)
+    iota(T.r8[0:8, :], [[1, 8], [0, 16]], 0, -1, "r8", 128)
+    iota(A("iq"), [[16, 12]], 0, 0, "iq", 12)
+    iota(A("ib"), [[613, V], [16 * 37, 13]], 0, 0, "ib", 78)
+    iota(A("IOT"), [[1, 3072]], -3072, 0, "IOT", 3072)
+    ms(A("ones"), 1.0, "ones", 100)
     ms(T.X[:, 3072:CW], 0.0, "Xp")
     ts(T.cwi[:, 16:32], T.cwi[:, 0:16], 15, OP.bitwise_and, "cwi", "cwj")
     cp(A("cw"), T.cwi[:, 16:32], "cwj", "cw")
-    cols = {}
+    ts(A("SC"), A("cw"), -1.0, OP.mult, "cw", "SC", 15.0, OP.add)
+    ts(A("E0"), A("cw"), 0.0, OP.is_equal, "cw", "E0")
+    ts(A("NE"), A("cw"), 0.0, OP.not_equal, "cw", "NE")
+    cols = {"s": T.SC[:, 15:16], "e0": T.E0[:, 0:1], "e15": T.E0[:, 15:16], "n0": T.NE[:, 0:1], "n15": T.NE[:, 15:16]}
+    home = {"s": "SC", "e0": "E0", "e15": "E0", "n0": "NE", "n15": "NE"}
 
-    def col(nm, src, a, o1, b=None, o2=None):
-        cols[nm] = T.cols[:, len(cols):len(cols) + 1]
-        if src in cols:
-            ts(cols[nm], cols[src], a, o1, "c_" + src, "c_" + nm, b, o2)
-        else:
-            ts(cols[nm], T.cw[:, src:src + 1], a, o1, "cw", "c_" + nm, b, o2)
+    def col(nm, src, a, b):
+        cols[nm], home[nm] = T.cols[:, len(cols) - 5:len(cols) - 4], "c_" + nm
+        act(cols[nm], cols[src], AF.Identity, home[src], home[nm], bias=b, scale=a, c=70)
 
-    col("s", 15, -1.0, OP.mult, 15.0, OP.add)
-    ts(T.raw[:, 0:144], T.tm[:, 0:144], cols["s"], OP.add, "tm c_s", "raw")
-    ts(T.raw[:, 144:272], T.tm[:, 16:144], cols["s"], OP.add, "tm c_s", "raw2")
-    rw, rw2, rp = T.raw[:, 16:144], T.raw[:, 16:272], T.raw[:, 0:144]
-    sb, sb2 = T.smB[:, 16:144], T.smB[:, 16:272]
+    ts(A("raw"), A("tm"), cols["s"], OP.add, "tm SC", "raw")
+    rw = T.raw[:, 16:144]
 
-    def eye(nm, at, by=None, src=None, out=None):
-        rd = ("smB" if src is sb else "raw raw2") + " c_" + at + (" c_" + by if by in cols else "")
-        ts(A(nm) if out is None else out, rw if src is None else src, cols[at], OP.is_equal, rd, nm,
-           cols.get(by, by), None if by is None else OP.mult)
+    def eye(out, where, nm, by=None):
+        ts(out, rw, where, OP.is_equal, "raw cw SC " + home.get(by, ""), nm, cols.get(by), OP.mult if by else None)
 
-    def blk(nm, by, src=None):
-        ts(A(nm), sb if src is None else src, 0.0, OP.is_ge, "smB" + (" c_" + by if by in cols else ""), nm, cols.get(by, by), OP.mult)
+    def scaled(nm, src, by, out=None):
+        act(A(nm) if out is None else out, I if src == "I" else A(src), AF.Identity, src + " " + home.get(by, ""), nm,
+            scale=cols.get(by, by), c=140)
 
-    def scaled(nm, src, by):
-        act(A(nm), A(src), AF.Identity, src + (" c_" + by if by in cols else ""), nm, scale=cols.get(by, by))
+    def less(nm, a, b, scale, bk):
+        mm(B[bk][:, 0:128], I, A(a), True, False, "I " + a, "bk%d" % bk, 70)
+        mm(B[bk][:, 0:128], A("NI"), A(b), False, True, "NI " + b, "bk%d" % bk, 70)
+        act(A(nm), B[bk][:, 0:128], AF.Identity, "bk%d" % bk, nm, scale=scale, c=140)
 
-    eye("Ib", "s")
-    col("cr", "s", 8192.0, OP.mult, 4096.0, OP.add)
-    scaled("CR", "Ib", "cr")
-    ts(T.R8n[0:8, :], T.r8[0:8, :], 0.0, OP.is_equal, "r8", "R8n", -8.0, OP.mult)
+    eye(I, cols["s"], "I")
+    eye(T.I[:, 128:256], cols["s"], "I2")
+    ms(T.R8n[0:32, :], -8.0, "R8n")
+    ts(T.R8n[0:8, :], T.r8[0:8, :], 0.0, OP.is_equal, "r8", "R8n", -8.0, OP.mult, c=140)
+    ts(A("W1"), A("raw"), 0.0, OP.is_equal, "raw", "W1")
+    R8 = T.R8n[0:8, :]
+    mm(B[7][:, 0:128], R8, R8, True, True, "R8n", "bk7", 70)
+    act(A("BA"), B[7][:, 0:128], AF.Identity, "bk7", "BA", scale=1.0 / 64, c=140)
+    for nm, src, a, b in (("cr", "s", 8192.0, 4096.0), ("ic", "e15", 3840.0, 256.0), ("ip", "e15", -240.0, 256.0),
+                          ("ci", "e15", 1.875, -2.0), ("pi", "e15", -15.0, 16.0), ("kc", "e0", -NH - 1.0, 1.0),
+                          ("pk", "e0", -135168.0, 4096.0), ("cp", "s", 4096.0, 2048.0 * 65), ("cq", "s", 4096.0, 2048.0 * 63),
+                          ("zc", "s", -1.0, 128.0), ("s37", "s", 37.0, 0.0)):
+        col(nm, src, a, b)
+    cols["w"], home["w"] = T.cols[:, 15:16], "c_w"
+    ts(cols["w"], A("wti"), 1.0 / 16, OP.mult, "wti", "c_w")
+    eye(A("Sh"), T.SC[:, 0:1], "Sh", "n0")
+    eye(A("tA"), cols["s"], "tA", "n15")
+    eye(A("tB"), T.SC[:, 14:15], "tB", "n15")
+    for w in range(1, 4):
+        eye(T.RA[:, 128 * w - 128:128 * w], T.SC[:, 15 - w:16 - w], "RA%d" % w)
+    for h in range(4):
+        eye(T.RW[:, 128 * h:128 * h + 128], T.cw[:, 14 - 4 * h:15 - 4 * h], "RW%d" % h)
+    ts(A("M8"), T.raw[:, 16:144:16], 0.0, OP.is_equal, "raw", "M8")
+    for nm, src, by in (("CR", "I", "cr"), ("NI", "I", -1.0), ("NB", "BA", -8.0), ("WN", "W1", -8.0), ("W2", "W1", 16.0),
+                        ("Ipen", "I", "ip"), ("C15", "I", "e15"), ("CE15", "C15", E), ("CE", "I", E), ("Ww", "W1", "w"),
+                        ("CI", "I", "ci"), ("PI", "BA", "pi"), ("PK", "BA", "pk"), ("I3", "I", 3072.0), ("Wk", "W1", "kc"),
+                        ("CP", "I", "cp")):
+        scaled(nm, src, by)
+    ts(A("M15"), A("BA"), cols["e15"], OP.mult, "BA E0", "M15", -1.0 / 4096, OP.mult)
+    ts(A("tC"), A("BA"), cols["e0"], OP.mult, "BA E0", "tC", 512.0, OP.mult)
+    ts(A("ShN"), A("Sh"), -512.0, OP.mult, "Sh", "ShN")
+    ts(A("B16"), A("BA"), 16.0, OP.mult, "BA", "B16")
+    tt(A("MC"), A("tC"), A("ShN"), OP.add, "tC ShN", "MC", 270)
+    tt(A("PH"), A("B16"), A("ShN"), OP.add, "B16 ShN", "PH", 270)
+    tt(A("HQ"), A("Sh"), A("C15"), OP.add, "Sh C15", "HQ", 270)
+    less("SI", "Sh", "tA", 1.0, 6)
+    less("Moh", "tA", "tB", 1.0 / 256, 7)
+    for h in range(2):
+        scaled("BH%d" % h, "BA", 8192.0, out=T.BH[:, 128 * h:128 * h + 128])
+    mm(B[1][:, 0:128], R8, R8, True, False, "R8n", "bk1", 70)
+    mm(B[1][:, 0:128], R8, R8, False, False, "R8n", "bk1", 70)
+    mm(B[1][:, 0:128], A("NI"), rw, False, True, "NI raw", "bk1", 70)
+    act(T.oyh[:, 0:128], B[1][:, 0:128], AF.Copy, "bk1", "oyh", c=140)
+    ts(A("TUi"), T.oyh[:, 0:128], cols["zc"], OP.is_ge, "oyh c_zc", "TUi", c=140)
+    ts(T.TUr[:, 0:128], T.oyh[:, 0:128], cols["zc"], OP.is_gt, "oyh c_zc", "TUr0", -8192.0, OP.mult, c=140)
+    cp(T.TUr[:, 128:256], T.TUr[:, 0:128], "TUr0", "TUr1")
+    ts(A("bi"), A("iq"), cols["s"], OP.add, "iq SC", "bi")
+    ts(A("bz"), A("bi"), 7.5 / 16, OP.add, "bi", "bz")
+    ts(A("KB"), A("bi"), 16.0, OP.mult, "bi", "KB", float(NH), OP.add)
+    ms(T.LB[:, 0:24], 0.0, "LB0")
+    cp(T.LB[:, 24:36], A("bi"), "bi", "LB1")
+    ms(T.kap[:, 0:12], 1.0, "kap0")
+    ms(T.kap[:, 12:14], 8.0, "kap1")
+    ts(T.abi[:, 0:78], A("ib"), cols["s37"], OP.add, "ib c_s37", "abi", c=80)
+    ts(T.abi[:, 78:156], T.abi[:, 0:78], 2047, OP.bitwise_and, "abi", "abj", c=80)
+    ts(A("AB"), T.abi[:, 78:156], -1023.5, OP.add, "abj", "AB", c=80)
+    ms(T.AB[:, 12:78:13], -1023.5, "AB")
 
-    def masked(j, src, b):
-        ts(T.nmh[0:8, NP * j:NP * j + NP], T.nmi[:, NP * j:NP * j + NP], 1024.0, OP.mult, "nmi%d" % j, "nmh%d" % j)
-        mm(L(b), T.R8n[0:8, :], T.nmh[0:8, NP * j:NP * j + NP], True, False, "R8n nmh%d" % j, "bk%d" % b)
+    def masked(j, src, b, out):
+        ts(T.nmh[0:8, NP * j:NP * j + NP], T.nmi[:, NP * j:NP * j + NP], 1024.0, OP.mult, "nmi%d" % j, "nmh%d" % j, c=200)
+        mm(L(b), R8, T.nmh[0:8, NP * j:NP * j + NP], True, False, "R8n nmh%d" % j, "bk%d" % b)
         mm(L(b), A("CR"), A("ones"), False, True, "CR ones", "bk%d" % b)
-        tt(A("t0"), L(b), A(src), OP.max, "bk%d %s" % (b, src), "t0")
-
-    col("e0", 0, 0.0, OP.is_equal)
-    col("e15", 15, 0.0, OP.is_equal)
-    ts(A("W1"), rp, 0.0, OP.is_equal, "raw", "W1")
-    ts(T.tm[:, 0:272], T.raw[:, 0:272], 16.0, OP.is_ge, "raw raw2", "tm", -200.0, OP.mult)
-    masked(1, "hai", 4)
-    ts(A("Hs"), A("t0"), 3072.0, OP.min, "t0", "Hs", -E, OP.add)
-    ts(HFR, A("Hs"), cols["e0"], OP.mult, "Hs c_e0", "hfr")
-    masked(0, "tri", 5)
-    ts(A("TT0"), A("t0"), 3072.0, OP.min, "t0", "TT0")
-    diag(B[2][:, 292:304], "W1", "DG", 3 * NP, 4 * NP, "hfr", "bk2", first=True)
-    ts(A("bi"), A("iq"), cols["s"], OP.add, "iq c_s", "bi")
-    ms(A("D0"), BIG, "D0a D0b D0c")
-    ms(T.D0[:, 1:36:3], -BIG, "D0b")
-    ms(A("D1"), BIG, "D1a D1b D1c")
-    ms(T.D1[:, 36:37], OFF, "D1a")
-    ts(T.abi[:, 0:12], A("bi"), 37.0, OP.mult, "bi", "abi")
-    ts(T.abi[:, 72:84], T.abi[:, 0:12], 2047, OP.bitwise_and, "abi", "abj")
-    ts(T.D1[:, 0:36:3], T.abi[:, 72:84], OFF, OP.add, "abj", "D1a")
+        tt(A(out), L(b), A(src), OP.max, "bk%d %s" % (b, src), out)
 
     def front():
-        act(T.D1[:, 2:36:3], B[2][:, 292:304], AF.Identity, "bk2", "D1c", bias=E + OFF)
-        act(T.D0[:, 2:36:3], B[2][:, 292:304], AF.Identity, "bk2", "D0c", bias=16384.0 * (E - 0.5), scale=-16384.0)
+        act(T.D1[:, 2:36:3], B[5][:, 256:268], AF.Identity, "bk5", "D1c", bias=E + OFF, c=70)
+        act(T.D0[:, 2:36:3], B[5][:, 256:268], AF.Identity, "bk5", "D0c", bias=16384.0 * (E - 0.5), scale=-16384.0, c=70)
 
-    def choose():
+    def choose(now):
+        now("scan")
         op("V", lambda: g.vector.tensor_tensor_scan(A("cf"), A("D0"), T.D1[:, 0:36], 0.0, OP.max, OP.min),
-           "D0a D0b D0c D1a D1b D1c", "cf")
-
-    def clist():
+           "D0a D0b D0c D1a D1b D1c", "cf", 70)
+        now("cl")
         ts(A("cl"), T.cf[:, 2:36:3], -OFF, OP.add, "cf", "cl")
+        now("crep")
+        act(A("crep"), A("IOT").indirect(A("cl")), AF.Copy, "IOT cl", "crep", c=G192)
 
-    def crep():
-        act(A("crep"), A("IOT").indirect(A("cl")), AF.Copy, "IOT cl", "crep")
+    def hand_flags(now):
+        now("hinv")
+        ts(HINV, A("Hp"), E, OP.is_ge, "Hp", "hinv", 256.0, OP.mult, c=100)
+        now("hfr")
+        ts(HFR, A("Hp"), cols["e0"], OP.mult, "Hp E0", "hfr", c=100)
 
+    masked(0, "tri", 5, "fst")
+    ts(A("TT0"), A("fst"), 3072.0, OP.min, "fst", "TT0", c=200)
+    masked(1, "hai", 4, "RR")
+    ts(A("Hs"), A("RR"), 3072.0, OP.min, "RR", "Hs", -E, OP.add, c=200)
+    ts(HFR, A("Hs"), cols["e0"], OP.mult, "Hs E0", "hfr", c=100)
+    diag(B[5][:, 256:268], "W1", "DG", NP, "hfr", "bk5", first=True)
     front()
-    tt(A("smB"), A("raw"), A("tm"), OP.add, "raw raw2 tm", "smB")
-    choose()
-    clist()
-    ts(A("W1b"), rp, 0.0, OP.is_equal, "raw", "W1b")
-    blk("BAb", 1.0)
-    scaled("NB", "BAb", -8.0)
-    scaled("WN", "W1b", -8.0)
-    scaled("W2", "W1b", 16.0)
-    col("ic", "e15", 3840.0, OP.mult, 256.0, OP.add)
-    col("ip", "e15", -240.0, OP.mult, 256.0, OP.add)
-    eye("Ipen", "s", "ip")
-    ts(T.nmh[0:8, 2 * NP:3 * NP], T.nmi[:, 2 * NP:3 * NP], -2040.0, OP.add, "nmi2", "nmh2")
-    col("s0", "e0", -200.0, OP.mult, -1.0, OP.add)
-    cols["sm"] = T.cols[:, len(cols):len(cols) + 1]
-    tt(cols["sm"], cols["s0"], cols["s"], OP.add, "c_s0 c_s", "c_sm")
-    eye("Sh", "sm")
+    ms(T.D0[:, 0:36:3], BIG, "D0a")
+    ms(T.D0[:, 1:36:3], -BIG, "D0b")
+    ms(T.D1[:, 1:36:3], BIG, "D1b")
+    ts(T.D1[:, 0:39:3], T.AB[:, 0:13], 4096.0, OP.add, "AB", "D1a")
+    choose(len)
+    ms(T.nmh[0:32, 2 * NP:3 * NP], 2040.0 - (OFF - 0.5) / 8, "nmh2", 100)
+    ts(T.nmh[0:8, 2 * NP:3 * NP], T.nmi[:, 2 * NP:3 * NP], -2040.0, OP.add, "nmi2", "nmh2", c=200)
+    mm(L(3), A("Sh"), A("Hs"), True, False, "Sh Hs", "bk3")
+    mm(L(3), A("CE15"), A("ones"), False, True, "CE15 ones", "bk3")
+    cp(A("Hp"), L(3), "bk3", "Hp", 200)
+    hand_flags(len)
 
-    def more_constants():
-        col("m15", "e15", -1.0 / 4096, OP.mult)
-        blk("M15", "m15")
-        col("n15", "e15", -1.0, OP.add)
-        eye("tA", "s", "n15")
-        tt(A("SI"), A("Sh"), A("tA"), OP.add, "Sh tA", "SI")
-        col("sp", "s", 1.0, OP.add)
-        eye("tB", "sp", None, src=sb)
-        tt(A("tA"), A("tA"), A("tB"), OP.add, "tA tB", "tA")
-        ts(A("Moh"), A("tA"), -1.0 / 256, OP.mult, "tA", "Moh")
-        eye("Ih", "s", src=rw2)
-        scaled("C15", "Ib", "e15")
-        scaled("CE15", "C15", E)
-        scaled("CE", "Ib", E)
-        scaled("NIb", "Ib", -1.0)
+    def inside(lo, hi):
+        return [j for j in range(len(PIECES)) if lo <= PIECES[j][0] < hi]
 
-    def late_constants():
-        ts(T.tm[:, 0:256], rw2, 0.0, OP.is_lt, "raw raw2", "tm", 300.0, OP.mult)
-        tt(A("smC"), rw2, T.tm[:, 0:256], OP.add, "raw raw2 tm", "smC")
-        ts(A("TUi"), T.smC[:, 0:128], cols["s"], OP.is_le, "smC c_s", "TUi")
-        ts(A("TUr"), A("smC"), cols["s"], OP.is_lt, "smC c_s", "TUr", -4096.0, OP.mult)
-        blk("BH", 4096.0, src=sb2)
-        col("kc", "e0", -float(NH) - 1, OP.mult, 1.0, OP.add)
-        col("mh", "e0", -512.0 / NH, OP.mult)
-        blk("MH", "mh")
-        for w in range(1, 4):
-            col("a%d" % w, 15 - w, -1.0, OP.mult, 15.0, OP.add)
-            eye("RA%d" % w, "a%d" % w, out=T.RA[:, 128 * w - 128:128 * w])
-        ms(A("KB"), 0.0, "KB")
-        ts(T.KB[:, 0:12], A("bi"), 16.0, OP.mult, "bi KB", "KB0", float(NH), OP.add)
-        cp(T.KB[:, 12:24], A("bi"), "bi KB", "KB1")
-        ms(A("ZB"), -7.5 / 16, "ZB")
-        ms(A("half"), 0.5, "half")
-        cols["w"] = T.cols[:, len(cols):len(cols) + 1]
-        ts(cols["w"], A("wti"), 1.0 / 32, OP.mult, "wti", "c_w")
-        scaled("Ww", "W1b", "w")
-        ts(A("ShN"), A("Sh"), -512.0, OP.mult, "Sh", "ShN")
-        col("ci", "e15", 1.875, OP.mult, -2.0, OP.add)
-        eye("CI", "s", "ci")
-        ms(A("onesq"), 1.0, "onesq")
-        ms(T.kap[:, 0:12], 1.0, "kap0")
-        ms(T.kap[:, 12:14], 8.0, "kap1")
-        for t in range(1, V):
-            ts(T.abi[:, 12 * t:12 * t + 12], A("bi"), 37.0, OP.mult, "bi", "abi%d" % t, float(613 * t), OP.add)
-        ts(T.abi[:, 84:144], T.abi[:, 12:72], 2047, OP.bitwise_and, "abi1 abi2 abi3 abi4 abi5", "abk")
-        ms(A("AB"), -1023.5, "AB")
-        for t in range(1, V):
-            ts(T.AB[:, 13 * t:13 * t + 12], T.abi[:, 72 + 12 * t:84 + 12 * t], -1023.5, OP.add, "abk AB", "AB%d" % t)
+    def xts(lo, hi):
+        return " ".join("XT%d" % j for j in inside(lo, hi))
 
-    def hand_constants():
-        for h in range(4):
-            ts(T.RW[:, 128 * h:128 * h + 128], rw, T.cw[:, 14 - 4 * h:15 - 4 * h], OP.is_equal, "raw cw", "RW%d" % h)
-        blk("B16", 16.0)
-        col("pi", "e15", -15.0, OP.mult, 16.0, OP.add)
-        blk("PI", "pi")
-        col("pk", "e0", -4080.0, OP.mult, 4096.0, OP.add)
-        blk("PK", "pk")
-        col("cp", "s", 4096.0, OP.mult, 2048.0 * 65, OP.add)
-        scaled("CP", "Ib", "cp")
-        col("hc", "e15", -85.0, OP.mult, 99.0, OP.add)
-        ts(A("HQ"), sb, cols["hc"], OP.min, "smB c_hc c_sm", "HQ", cols["sm"], OP.is_equal)
-
-    def last_constants():
-        col("cq", "cp", -4096.0, OP.add)
-        scaled("CPL", "Ib", "cq")
-        eye("IL", "s", -512.0)
-        eye("I3", "s", 3072.0)
-        ts(A("M8"), T.raw[:, 16:144:16], 0.0, OP.is_equal, "raw", "M8")
-
-    def hand_flags():
-        ts(HINV, A("Hp"), E, OP.is_ge, "Hp", "hinv", 256.0, OP.mult)
-        ts(HFR, A("Hp"), cols["e0"], OP.mult, "Hp c_e0", "hfr")
-
-    def hand_merge(nm):
-        tt(A("RR"), L(3), A("Rv"), OP.max, "bk3 Rv", "RR")
-        tt(A(nm), H(5), A("RR"), OP.min, "bk5 RR", nm)
-
-    xt_all = " ".join("XT%d" % j for j in range(len(PIECES)))
+    def cards(nm, j, b, out, to, length):
+        ts(T.VL[:, NP * j:NP * j + NP], A(nm), E, OP.is_lt, nm, "VL%d" % j, c=100)
+        mm(B[b][0:8, NP:2 * NP], A("M8"), T.VL[:, NP * j:NP * j + NP], True, True, "M8 VL%d" % j, "bk%d" % b)
+        mm(L(b), I, A(nm), True, False, "I " + nm, "bk%d" % b)
+        mm(L(b), A("I3"), T.VL[:, NP * j:NP * j + NP], False, True, "I3 VL%d" % j, "bk%d" % b)
+        act(A(out), L(b), AF.Identity, "bk%d" % b, out, bias=-E)
+        act(T.omn[:, NP * j:NP * j + NP], B[b][0:8, NP:2 * NP], AF.Copy, "bk%d" % b, "omn%d" % j)
+        dma("S", "o" + to[1], T[to][:, :], A(out), out, "", 96)
+        dma("S", "o" + length[1], T[length][:, :], T.omn[:, NP * j:NP * j + NP], "omn%d" % j, "", 6)
 
     for t in range(V):
         last = t == V - 1
@@ -314,200 +318,266 @@ def rank_program(g, core, T, topo):
         jj = 0 if last else (2 if t == 3 else 1)
         ro = 128 - 16 * jj
 
+        def now(nm):
+            at[0] = (t, nm)
+
         def rot(nm):
             return T[nm][:, ro:ro + 128] if jj else T[nm][:, 0:128]
 
-        def gather(j):
-            p, n, q = PIECES[j]
+        def turn(mats, src, win, step):
+            now(win)
+            for w in range(4):
+                o = B[6 + w // 2][:, 256 * (w % 2):256 * (w % 2) + NP]
+                mm(o, mats[w][0], A(src), True, True, mats[w][1] + " " + src, "bk%d" % (6 + w // 2))
+            for w in range(4):
+                o = B[6 + w // 2][:, 256 * (w % 2):256 * (w % 2) + NP]
+                act(T[win][:, step * w:step * w + NP], o, AF.Copy, "bk%d" % (6 + w // 2), "%s%d" % (win, w))
+
+        if last:
+            at[0] = None
+            ts(A("ShN"), I, -512.0, OP.mult, "I", "ShN")
+            tt(A("PH"), A("B16"), A("ShN"), OP.add, "B16 ShN", "PH", 270)
+            scaled("CP", "I", "cq")
+        now("xc")
+        cp(A("xc"), A("X").indirect(A("cl")), "X Xp cl", "xc", G192)
+        for j, (p, n, q) in enumerate(PIECES):
+            now("g%d" % j)
             out, src = T.XT[:, 16 * p:16 * (p + n)], A("X").indirect(tab[:, p:p + n])
             if q == "A":
-                act(out, src, AF.Identity, "X Xp " + tn, "XT%d" % j, bias=-2.0)
+                act(out, src, AF.Copy, "X Xp " + tn, "XT%d" % j, c=60 + GATHER * 16 * n)
             else:
-                ts(out, src, -2.0, OP.add, "X Xp " + tn, "XT%d" % j)
-
-        def maxes(j):
-            p, n, q = PIECES[j]
-            b, o = (1, 4 * p) if p < 128 else (2, 4 * (p - 128))
-            for s in range(4):
-                tt(T.MX[:, 16 * p + s:16 * (p + n):4], B[b][:, o:o + 4 * n], T.XT[:, 16 * p + s:16 * (p + n):4], OP.max,
-                   "bk%d XT%d" % (b, j), "MX%d_%d" % (j, s))
-
-        def fours(b, p, n):
-            for s in range(4):
-                mm(B[b][:, s:4 * n:4], A("Ib"), T.xc[:, p:p + n], True, True, "Ib xc", "bk%d" % b)
-
-        def inside(c):
-            return [j for j in range(len(PIECES)) if PIECES[j][0] // 64 == c]
-
-        def sumx(c):
-            for s in range(16):
-                mm(B[0][:, 64 * c:64 * c + 64], T.WN[:, 16 - s:144 - s], T.XT[:, 1024 * c + s:1024 * c + 1024:16], False, False,
-                   "WN " + " ".join("XT%d" % j for j in inside(c)), "bk0")
-
-        def summ(c):
-            for k in range(16):
-                s = k // 4 + 4 * (k % 4)
-                mm(B[0][:, 64 * c:64 * c + 64], T.W2[:, 16 - s:144 - s], T.MX[:, 1024 * c + s:1024 * c + 1024:16], False, c == 2 and k == 15,
-                   "W2 " + " ".join("MX%d_%d" % (j, s % 4) for j in inside(c)), "bk0")
-
-        if t > 0:
-            op("R", None, "", tn, dma="arr%d" % t)
-        ts(A("xc"), A("X").indirect(A("cl")), -2.0, OP.add, "X Xp cl", "xc")
-        gather(0)
-        fours(1, 0, 128)
-        mm(L(0), A("NB"), A("xc"), True, False, "NB xc", "bk0")
-        mm(L(0), T.R8n[0:8, :], T.nmh[0:8, 2 * NP:3 * NP], False, False, "R8n nmh2", "bk0")
-        fours(2, 128, 64)
-        ts(A("Th"), A(tn), -E, OP.add, tn, "Th")
-        ts(INV, A(tn), 3072.0, OP.is_ge, tn + " c_ic", "inv", cols["ic"], OP.mult)
-        if t > 0:
-            hand_merge("Hp")
-            hand_flags()
-        else:
-            more_constants()
-            mm(L(6), A("Sh"), A("Hs"), True, False, "Sh Hs", "bk6")
-            mm(L(6), A("CE15"), A("ones"), False, True, "CE15 ones", "bk6")
-            cp(A("Hp"), L(6), "bk6", "Hp")
-            hand_flags()
-        mm(L(0), A("Ipen"), INV, False, False, "Ipen inv", "bk0")
+                cp(out, src, "X Xp " + tn, "XT%d" % j, 60 + GATHER * 16 * n)
+        now("Th")
+        ts(A("Th"), A(tn), -E, OP.add, tn, "Th", c=100)
+        now("inv")
+        ts(INV, A(tn), 3072.0, OP.is_ge, tn + " c_ic", "inv", cols["ic"], OP.mult, c=100)
+        now("LB")
+        mm(B[5][:, 256:292], I, A("LB"), True, False, "I LB0 LB1", "bk5", 34)
+        diag(B[5][:, 256:292], "W1", "DG", 3 * NP, "inv hinv hfr", "bk5")
+        now("x1")
+        ts(A("x1"), B[5][:, 268:280], 3840.0 if last else 0.0, OP.add, "bk5", "x1")
+        now("x2")
+        tt(T.xi[:, 0:12], B[5][:, 280:292], A("x1"), OP.add, "bk5 x1", "x2", 70)
+        now("x3")
+        ts(T.xi[:, 12:24], T.xi[:, 0:12], 1023, OP.bitwise_and, "x2", "x3")
+        now("x4")
+        ts(T.xi[:, 24:36], T.xi[:, 0:12], 3072 + 255, OP.bitwise_and, "x2", "x4")
+        now("ql")
+        cp(A("ql"), T.xi[:, 12:36], "x3 x4", "ql")
+        if not last:
+            now("front")
+            front()
+        now("oh")
         mm(L(3), A("M15"), INV, True, True, "M15 inv", "bk3")
         mm(H(3), A("Moh"), INV, True, False, "Moh inv", "bk3")
         mm(H(3), A("C15"), A("ones"), False, True, "C15 ones", "bk3")
+        now("fT")
+        tt(A("fT"), L(3), A("Th"), OP.mult, "bk3 Th", "fT")
+        now("ohc")
+        tt(A("ohc"), H(3), A("crep"), OP.mult, "bk3 crep", "ohc")
+        now("pt0")
         mm(L(4), A("Sh"), A("Th"), True, False, "Sh Th", "bk4")
         mm(L(4), A("CE15"), A("ones"), False, False, "CE15 ones", "bk4")
-        gather(1)
-        if t == 0:
-            crep()
-        gather(2)
-        tt(A("fT"), L(3), A("Th"), OP.mult, "bk3 Th", "fT")
-        sumx(0)
-        maxes(0)
+        now("SI")
         mm(L(4), A("SI"), A("fT"), False, True, "SI fT", "bk4")
-        summ(0)
-        tt(A("ohc"), H(3), A("crep"), OP.mult, "bk3 crep", "ohc")
+        now("Tapp")
         tt(A("Tapp"), L(4), A("ohc"), OP.add, "bk4 ohc", "Tapp")
-        if t == 0:
-            late_constants()
-        maxes(2)
-        gather(3)
-        gather(4)
-        mm(L(5), rot("Ih"), A("Tapp"), True, False, "Ih Tapp", "bk5")
-        mm(L(4), rot("Ih"), A("Th"), True, True, "Ih Th", "bk4")
-        mm(L(3), A("Ib"), A("xc"), True, False, "Ib xc", "bk3")
-        for w in range(4):
-            m = T.RA[:, 128 * w - 128:128 * w] if w else T.Ih[:, 0:128]
-            mm(B[6 + w // 2][:, 256 * (w % 2):256 * (w % 2) + NP], m, A("Tapp"), True, True, "Ih RA1 RA2 RA3 Tapp", "bk%d" % (6 + w // 2))
-        sumx(1)
-        maxes(1)
-        summ(1)
-        maxes(3)
-        sumx(2)
-        maxes(4)
-        summ(2)
-        act(A("Trot"), L(4), AF.Copy, "bk4", "Trot")
-        mm(H(4), A("Ib"), T.XT[:, 0:3072:16], True, False, "Ib " + xt_all, "bk4")
-        mm(H(4), A("NIb"), A("xc"), False, True, "NIb xc", "bk4")
-        for w in range(4):
-            act(T.WINA[:, 256 * w:256 * w + NP], B[6 + w // 2][:, 256 * (w % 2):256 * (w % 2) + NP], AF.Copy, "bk%d" % (6 + w // 2), "WINA%d" % w)
-        act(T.XT[:, NH:NH + 3072:16], H(4), AF.Abs, "bk4", "N0", scale=2.0)
+        now("Trot")
+        mm(H(3), rot("I"), A("Th"), True, True, "I I2 Th", "bk3")
+        now("CE")
+        mm(L(3), A("CE"), A("ones"), True, False, "CE ones", "bk3")
+        now("Trot")
+        act(A("Trot"), H(3), AF.Copy, "bk3", "Trot")
+        turn([(I, "I")] + [(T.RA[:, 128 * w:128 * w + 128], "RA%d" % (w + 1)) for w in range(3)], "Tapp", "WINA", 256)
+        now("Tg")
+        cp(A("Tg"), A("WINA").indirect(T.ql[:, 0:12]), "WINA0 WINA1 WINA2 WINA3 ql", "Tg", G192)
+        turn([(T.RW[:, 128 * h:128 * h + 128], "RW%d" % h) for h in range(4)], "Tg", "WIN", 1024)
+        now("Rv")
+        act(A("Rv"), A("WIN").indirect(T.ql[:, 12:24]), AF.Copy, "WIN0 WIN1 WIN2 WIN3 ql", "Rv", c=G192)
 
-        ts(A("ok"), L(0), OFF - 8 * 2040.0, OP.add, "bk0 D1a", "ok", T.D1[:, 36:37], OP.is_le)
-        mm(L(2), A("CE"), A("ones"), True, False, "CE ones", "bk2")
+        now("thr")
+        mm(L(0), T.R8n[0:9, :], T.nmh[0:9, 2 * NP:3 * NP], True, False, "R8n nmh2", "bk0")
+        now("NB")
+        mm(L(0), A("NB"), A("xc"), False, False, "NB xc", "bk0+")
+        now("Ipen")
+        mm(L(0), A("Ipen"), INV, False, False, "Ipen inv", "bk0+")
+        for b, p, n in ((1, 0, 128), (2, 128, 64)):
+            now("four%d" % b)
+            for s in range(4):
+                mm(B[b][:, s:4 * n:4], I, T.xc[:, p:p + n], True, True, "I xc", "bk%d" % b, n // 2 + 2)
+        for j, (p, n, q) in enumerate(PIECES):
+            b, o = (1, 4 * p) if p < 128 else (2, 4 * (p - 128))
+            for s in range(4):
+                now("m%d_%d" % (j, s))
+                tt(T.MX[:, 16 * p + s:16 * (p + n):4], B[b][:, o:o + 4 * n], T.XT[:, 16 * p + s:16 * (p + n):4], OP.max,
+                   "bk%d XT%d" % (b, j), "MX%d_%d" % (j, s), max(70, 4 * n + 10))
+        for c in range(3):
+            o = B[0][:, 64 * c:64 * c + 64]
+            now("sx%d" % c)
+            for s in range(16):
+                mm(o, T.WN[:, 16 - s:144 - s], T.XT[:, 1024 * c + s:1024 * c + 1024:16], False, False,
+                   "WN " + xts(64 * c, 64 * c + 64), "bk0+", 34)
+            for k in range(16):
+                now("sm%d" % c + ("ab"[k // 8] if c == 1 else ""))
+                s = k // 4 + 4 * (k % 4)
+                end = c == 2 and k == 15
+                mm(o, T.W2[:, 16 - s:144 - s], T.MX[:, 1024 * c + s:1024 * c + 1024:16], False, end,
+                   "W2 " + " ".join("MX%d_%d" % (j, s % 4) for j in inside(64 * c, 64 * c + 64)), "bk0" if end else "bk0+", 34)
+        now("d0a")
+        mm(H(4), A("NI"), A("xc"), True, False, "NI xc", "bk4")
+        mm(B[4][:, NP:NP + 128], I, T.XT[:, 0:2048:16], False, False, "I " + xts(0, 128), "bk4", 70)
+        now("d0b")
+        mm(B[4][:, NP + 128:2 * NP], I, T.XT[:, 2048:3072:16], False, True, "I " + xts(128, NP), "bk4", 34)
+        now("ad")
+        act(A("ad"), H(4), AF.Abs, "bk4", "ad", scale=2.0)
+        now("N0")
+        mm(L(4), A("NI"), A("xc"), True, False, "NI xc", "bk4")
+        mm(L(4), I, A("ad"), False, True, "I ad", "bk4")
+        act(T.XT[:, NH:NH + 3072:16], L(4), AF.Identity, "bk4", "N0", bias=0.5)
+
+        now("ok")
+        act(A("ok"), L(0), AF.Relu, "bk0 D1a", "ok", bias=T.D1[:, 36:37], scale=-1.0)
+        now("tri")
         mm(L(1), A("TUi"), A("ok"), True, True, "TUi ok", "bk1")
-        mm(L(2), rot("TUr"), A("ok"), False, True, "TUr ok", "bk2")
-        mm(L(5), rot("BH"), A("ok"), False, True, "BH ok", "bk5")
-        ts(K1, L(1), 0.5, OP.is_ge, "bk1 c_kc", "K1", cols["kc"], OP.mult)
-        kp = B[0][:, 256:304]
-        mm(kp, T.Ih[:, 0:128], A("KB"), True, False, "Ih KB0 KB1", "bk0")
-        mm(L(3), A("MH"), K1, False, True, "MH K1", "bk3")
-        diag(kp, "W1", "DG", 0, 4 * NP, "K1 inv hinv hfr", "bk0")
-        act(A("ac"), L(3), AF.Relu, "bk3", "ac", bias=3.5 - 512)
-        tt(A("fst"), L(2), A("Trot"), OP.max, "bk2 Trot", "fst")
+        now("K1")
+        act(A("K1"), L(1), AF.Sign, "bk1", "K1")
+        kp = B[0][:, 256:268]
+        now("kd")
+        mm(kp, I, A("KB"), True, False, "I KB", "bk0", 34)
+        diag(kp, "Wk", "K1", NP, "K1", "bk0")
+        now("kl")
+        cp(A("kl"), kp, "bk0", "kl")
+        now("pt")
+        mm(L(5), rot("I"), A("Tapp"), True, False, "I I2 Tapp", "bk5")
+        now("ramp")
+        mm(L(3), rot("TUr"), A("ok"), False, True, "TUr0 TUr1 ok", "bk3")
+        mm(L(5), rot("BH"), A("ok"), False, True, "BH0 BH1 ok", "bk5")
+        now("fst")
+        tt(A("fst"), L(3), A("Trot"), OP.max, "bk3 Trot", "fst")
+        now("Tc")
         tt(A("Tc"), L(5), A("fst"), OP.min, "bk5 fst", "Tc")
         if not last:
             to = T["TO%d" % t]
             nxt = T.cores[(rank + 1) % len(T.cores)]
-            ts(to[:, :], A("Tc"), E, OP.add, "Tc", "TO%d" % t)
+            now("to")
+            ts(to[:, :], A("Tc"), E, OP.add, "Tc", "TO%d" % t, c=100)
             rid, pid = topo.addr(nxt, core)
             mask = 0
             for e in send_engines(topo, core, nxt):
                 mask |= 1 << e
             op("G", lambda to=to, t=t, rid=rid, pid=pid, mask=mask: g.remote_dma(
-                T["TT%d" % (t + 1)][:, :], to[:, :], T.sem["arr%d" % (t + 1)], T.sem.snd, pid, rid, mask), "TO%d" % t, "", dma="snd")
-            mm(H(1), A("CI"), INV, True, False, "CI inv", "bk1")
-            mm(H(1), A("MH"), K1, False, False, "MH K1", "bk1")
-            mm(H(1), A("ShN"), K1, False, True, "ShN K1", "bk1")
+                T["TT%d" % (t + 1)][:, :], to[:, :], T.sem["arr%d" % (t + 1)], T.sem.snd, pid, rid, mask),
+               "TO%d" % t, "sent%d" % t, REMOTE * (2 if t == 0 else 1), dma="snd")
+            op("R", None, "sent%d" % t, "TT%d" % (t + 1), 0, dma="arr%d" % (t + 1))
+        else:
+            now("yt")
+            cards("Tc", 0, 3, "oyt", "yt", "yn")
+        now("u")
+        tt(A("u"), A("XT").indirect(A("kl")), A("xc"), OP.add, xts(0, NP) + " N0 kl xc", "u", G192)
+        now("y1")
+        ts(A("y1"), A("u"), 0.5, OP.mult, "u", "y1", 1023.75, OP.add, c=100)
         pz = B[2][:, 256:268]
-        mm(pz, T.Ih[:, 0:128], A("ZB"), True, False, "Ih ZB", "bk2")
-        cp(A("kl"), kp[:, 0:12] if False else B[0][:, 256:268], "bk0", "kl")
+        now("zd")
+        diag(pz, "Ww", "y1", NP, "y1", "bk2", first=True)
+        now("y")
+        ts(A("y"), A("y1"), -1024.0, OP.add, "y1", "y", c=100)
+        now("zf")
+        tt(A("zf"), pz, A("bz"), OP.subtract, "bk2 bz", "zf", 70)
+        now("zt")
+        tt(A("zt"), pz, A("zf"), OP.subtract, "bk2 zf", "zt", 70)
+        now("zl")
+        ts(A("zl"), A("zt"), 16.0, OP.mult, "zt", "zl")
+        now("X")
+        cp(A("X").indirect(A("zl")), A("y"), "y zl Xp", "X", 50 + SCATTER * NP)
         if not last:
-            tt(T.D1[:, 1:36:3], B[0][:, 256:268], T.cf[:, 2:36:3], OP.max, "bk0 cf", "D1b")
-        ts(A("x1"), B[0][:, 280:292], 3840.0 if last else 0.0, OP.add, "bk0", "x1")
-        tt(T.xi[:, 0:12], B[0][:, 268:280], A("x1"), OP.add, "bk0 x1", "x2")
-        tt(A("u"), A("XT").indirect(A("kl")), A("ac"), OP.add, xt_all + " N0 kl ac", "u")
-        if not last:
-            act(T.cap[:, :], H(1), AF.Relu, "bk1", "cap acc", scale=1.0 / 512, acc=T.acc[:, 0:1])
-            act(T.rA[:, 0:13], T.kap[:, 0:13], AF.Identity, "kap0 kap1 acc", "rA", scale=T.acc[:, 0:1])
-            act(T.D0[:, 1:36:3], B[0][:, 256:268], AF.Identity, "bk0", "D0b", bias=NH + 3071.0, scale=-1.0)
-            act(T.D1[:, 2:36:3], B[0][:, 292:304], AF.Identity, "bk0", "D1c", bias=E + OFF)
-            act(T.D0[:, 2:36:3], B[0][:, 292:304], AF.Identity, "bk0", "D0c", bias=16384.0 * (E - 0.5), scale=-16384.0)
-        ts(T.xi[:, 12:24], T.xi[:, 0:12], 1023, OP.bitwise_and, "x2", "x3")
-        ts(A("y2"), A("u"), R2, OP.add, "u", "y2", -R2, OP.add)
-        diag(pz, "Ww", "y2", 0, NP, "y2", "bk2")
-        ts(T.xi[:, 24:36], T.xi[:, 0:12], 3072 + 255, OP.bitwise_and, "x2", "x4")
-        cp(A("ql"), T.xi[:, 12:36], "x3 x4", "ql")
-        if t == 0:
-            hand_constants()
-        if t == V - 2:
-            last_constants()
-        cp(A("Tg"), A("WINA").indirect(T.ql[:, 0:12]), "WINA0 WINA1 WINA2 WINA3 ql", "Tg")
-        pa = B[1][:, 400:413]
-        if not last:
-            mm(pa, T.Ih[:, 0:128], T.AB[:, 13 * t + 13:13 * t + 26], True, False, "Ih AB AB%d" % (t + 1), "bk1")
-            mm(pa, A("onesq"), T.rA[:, 0:13], False, True, "onesq rA", "bk1")
-        for h in range(4):
-            mm(B[6 + h // 2][:, 256 * (h % 2):256 * (h % 2) + NP], T.RW[:, 128 * h:128 * h + 128], A("Tg"), True, True,
-               "RW%d Tg" % h, "bk%d" % (6 + h // 2))
-        for h in range(4):
-            act(T.WIN[:, 1024 * h:1024 * h + NP], B[6 + h // 2][:, 256 * (h % 2):256 * (h % 2) + NP], AF.Copy, "bk%d" % (6 + h // 2), "WIN%d" % h)
-        tt(A("zf"), pz, A("bi"), OP.subtract, "bk2 bi", "zf")
-        if not last:
+            now("D1b")
+            tt(T.D1[:, 1:36:3], kp, T.cf[:, 2:36:3], OP.max, "bk0 cf", "D1b", 70)
+            now("D0b")
+            act(T.D0[:, 1:36:3], kp, AF.Identity, "bk0", "D0b", bias=NH + 3071.0, scale=-1.0, c=70)
+            now("cap")
+            mm(H(1), A("CI"), INV, True, False, "CI inv", "bk1")
+            mm(H(1), A("MC"), A("K1"), False, True, "MC K1", "bk1")
+            act(A("cap"), H(1), AF.Relu, "bk1", "cap acc", scale=1.0 / 512, acc=T.acc[:, 0:1], c=220)
+            act(T.rA[:, 0:13], T.kap[:, 0:13], AF.Identity, "kap0 kap1 acc", "rA", scale=T.acc[:, 0:1], c=70)
+            pa = B[1][:, 400:413]
+            now("pa")
+            mm(pa, I, T.AB[:, 13 * t + 13:13 * t + 26], True, False, "I AB", "bk1", 34)
+            mm(pa, T.ones[:, 0:128], T.rA[:, 0:13], False, True, "ones rA", "bk1", 34)
+            now("rr")
             ts(T.rr[:, 0:13], pa, R2K, OP.add, "bk1", "rr", -R2K - 4096, OP.add)
-        tt(A("zt"), pz, A("zf"), OP.subtract, "bk2 zf", "zt")
+            now("D1a")
+            tt(T.D1[:, 0:39:3], pa, T.rr[:, 0:13], OP.subtract, "bk1 rr", "D1a", 70)
+            choose(now)
+        now("pen")
+        mm(H(5), I if last else A("HQ"), A("Hp"), True, True, "I HQ Hp", "bk5")
+        mm(L(5), A("PH"), HINV, True, False, "PH hinv", "bk5")
+        mm(L(5), A("CP"), A("ones"), False, False, "CP ones", "bk5")
+        mm(L(5), A("PI"), INV, False, False, "PI inv", "bk5")
+        mm(L(5), A("PK"), A("K1"), False, True, "PK K1", "bk5")
+        now("RR")
+        tt(A("RR"), L(5), A("Rv"), OP.max, "bk5 Rv", "RR")
+        now("Hp")
+        tt(A("Hp"), H(5), A("RR"), OP.min, "bk5 RR", "Hp")
         if not last:
-            tt(T.D1[:, 0:39:3], pa, T.rr[:, 0:13], OP.subtract, "bk1 rr", "D1a")
-        ts(A("zl"), A("zt"), 16.0, OP.mult, "zt", "zl", 7.5, OP.add)
-        if not last:
-            choose()
-            clist()
-        tt(A("X").indirect(A("zl")), A("y2"), A("half"), OP.mult, "y2 half zl Xp", "X")
-        act(A("Rv"), A("WIN").indirect(T.ql[:, 12:24]), AF.Copy, "WIN0 WIN1 WIN2 WIN3 ql", "Rv")
-        if not last:
-            crep()
-        mm(L(3), A("B16"), HINV, True, False, "B16 hinv", "bk3")
-        mm(L(3), A("IL" if last else "ShN"), HINV, False, False, "IL ShN hinv", "bk3")
-        mm(L(3), A("CPL" if last else "CP"), A("ones"), False, False, "CP CPL ones", "bk3")
-        mm(L(3), A("PI"), INV, False, False, "PI inv", "bk3")
-        mm(L(3), A("PK"), K1, False, True, "PK K1", "bk3")
-        mm(H(5), T.Ih[:, 0:128] if last else A("HQ"), A("Hp"), True, True, "Ih HQ Hp", "bk5")
+            hand_flags(now)
+        else:
+            now("yh")
+            cards("Hp", 1, 1, "oyh", "yh", "ym")
+    at[0] = None
+    dma("A", "ox", T.yx[:, :], T.X[:, 0:3072], "X", "", 768)
 
-    def cards(nm, j, b, out, name):
-        ts(T.VL[:, NP * j:NP * j + NP], A(nm), E, OP.is_lt, nm, "VL%d" % j)
-        mm(L(b), T.Ih[:, 0:128], A(nm), True, False, "Ih " + nm, "bk%d" % b)
-        mm(L(b), A("I3"), T.VL[:, NP * j:NP * j + NP], False, True, "I3 VL%d" % j, "bk%d" % b)
-        act(A(out), L(b), AF.Identity, "bk%d" % b, out, bias=-E)
-        dma("A", name[1], T[name[0]][:, :], A(out), out, "")
+    emit(g, core, T, topo, plan(ops), rank)
 
-    dma("S", "ox", T.yx[:, :], T.X[:, 0:3072], "X", "")
-    cards("Tc", 0, 0, "oyt", ("yt", "ot"))
-    hand_merge("Hs")
-    cards("Hs", 1, 1, "oyh", ("yh", "oh"))
-    mm(B[2][0:8, 0:2 * NP], A("M8"), A("VL"), True, True, "M8 VL0 VL1", "bk2")
-    cp(A("omn"), B[2][0:8, 0:2 * NP], "bk2", "omn")
-    dma("S", "on", T.yn[:, :], T.omn[:, 0:NP], "omn", "")
-    dma("S", "om", T.ym[:, :], T.omn[:, NP:2 * NP], "omn", "")
 
-    emit(g, core, T, topo, ops, rank)
+def plan(ops):
+    n = len(ops)
+    hold = [60 if o["dma"] else o["c"] for o in ops]
+    for q, names in ORDER.items():
+        place = {nm.rstrip("-+"): ((nm[-1] == "-") - (nm[-1] == "+"), i) for i, nm in enumerate(names.split())}
+        key = {k: (o["at"][0] + place[o["at"][1]][0], place[o["at"][1]][1]) for k, o in enumerate(ops) if o["q"] == q and o["at"]}
+        for k in key:
+            if ops[k]["at"] in LATER:
+                key[k] = (ops[k]["at"][0], place[LATER[ops[k]["at"]][q]][1] + 0.5)
+        mine = sorted(key, key=lambda k: (key[k], k))
+        for a, b in zip(mine, mine[1:]):
+            ops[b]["order"].add(a)
+    for q in "GS":
+        mine = [k for k, o in enumerate(ops) if o["q"] == q]
+        for a, b in zip(mine, mine[1:]):
+            ops[b]["order"].add(a)
+    succ = [[] for _ in ops]
+    left = [0] * n
+    for k, o in enumerate(ops):
+        for d in o["deps"] | o["order"]:
+            succ[d].append((k, WAKE if d in o["deps"] else hold[d] - ops[d]["c"]))
+            left[k] += 1
+    line, wait = [k for k in range(n) if not left[k]], list(left)
+    for k in line:
+        for s, lag in succ[k]:
+            wait[s] -= 1
+            if not wait[s]:
+                line.append(s)
+    assert len(line) == n, [ops[k]["at"] for k in range(n) if wait[k]][:9]
+    tail = [0] * n
+    for k in reversed(line):
+        tail[k] = ops[k]["c"] + max([tail[s] + lag for s, lag in succ[k]] + [0])
+    free, est, out = {}, [0] * n, []
+    ready = [k for k in range(n) if not left[k]]
+    while ready:
+        start = {k: max(est[k], free.get(ops[k]["q"], 0)) for k in ready}
+        first = min(ready, key=lambda k: start[k] + hold[k])
+        lim = start[first] + hold[first]
+        k = max([j for j in ready if ops[j]["q"] == ops[first]["q"] and (start[j] < lim or j == first)], key=lambda j: (tail[j], -j))
+        ready.remove(k)
+        out.append(k)
+        free[ops[k]["q"]] = start[k] + hold[k]
+        for s, lag in succ[k]:
+            est[s] = max(est[s], start[k] + ops[k]["c"] + lag)
+            left[s] -= 1
+            if not left[s]:
+                ready.append(s)
+    new = {k: i for i, k in enumerate(out)}
+    return [dict(ops[k], deps=set(new[d] for d in ops[k]["deps"]) if ops[k]["q"] != "R" else set()) for k in out]
 
 
 def emit(g, core, T, topo, ops, rank):

@@ -10,8 +10,9 @@ NH = 8192
 OFF = 3072.5
 R2K = 1.5 * 2 ** 34
 BIG = 30000.0
-PIECES = ((0, 64, "A"), (64, 48, "A"), (112, 16, "V"), (128, 16, "V"), (144, 32, "A"), (176, 16, "A"))
-WAKE, DMA, REMOTE, GATHER, SCATTER = 100, 1000, 2000, 1.6, 4.0
+PIECES = ((0, 32, "A"), (32, 32, "V"), (64, 64, "A"), (128, 14, "V"), (142, 30, "A"), (172, 20, "A"))
+MAXES = ((0, 32), (32, 32), (64, 64), (128, 44), (172, 20))
+WAKE, DMA, REMOTE, GATHER, SCATTER = 250, 1200, 2000, 1.6, 4.0
 
 
 def _m(*pieces):
@@ -19,21 +20,20 @@ def _m(*pieces):
 
 
 ORDER = {
-    "V": "xc hinv- hfr- fT ohc g2 Tapp g3 m0_0 x1 m0_1 x2 m0_2 x3 x4 m0_3 ql " + _m(2) + _m(1) + _m(3) + _m(4, 5) +
-         "Tg fst Tc to yt kl D1b u y1 y RR Hp zf rr yh zt D1a zl scan cl Th+ inv+ X",
-    "A": "g0 g1 g4 g5 Trot WINA ad front ok N0 K1 WIN cap D0b Rv yt yh crep",
-    "P": "four1 NB SI four2 LB Trot CE WINA sx0 sm0 sx1 d0a sm1a sm1b sx2 d0b sm2 N0 pt tri ramp WIN kd cap pen yt zd pa yh "
-         "thr+ oh+ pt0+ Ipen+",
+    "V": "inv Th xc g1 fT ohc g3 Tapp " + _m(0, 1) + _m(2) + "x1 m3_0 m4_0 m3_1 m4_1 m3_2 m4_2 x2 m4_3 m3_3 "
+         "x3 x4 ql Tg fst Tc to yt kl u rr D1b RR D1a y Hp scan zf cl zt hinv yh zl hfr X",
+    "A": "g0 g2 g4 g5 WINAa okA Trot WINAb front ok K1A xh K1 N0 cap WINa WINb rA Rv D0b yt yh crep",
+    "P": "thr Ipen ff oh LB pt0 four1 NB SI four2 sx0 Trot WINAa WINAb sm0a sx1 CE sm0b sm1a sm1b thrB NBB IpenB sx2 sm2a sm2b "
+         "triA d0c pt d0a CI ramp tri d0b BH kb cap WINa WINb kd pen pa PK zd yt yh",
 }
-LATER = {(0, "ohc"): {"V": "m2_3"}, (0, "Tapp"): {"V": "m2_3"}, (0, "Trot"): {"P": "sx1", "A": "g5"}, (0, "CE"): {"P": "sx1"},
-         (0, "WINA"): {"P": "sx1", "A": "Trot"}, (1, "Th"): {"V": "xc"}, (1, "inv"): {"V": "xc"},
-         (1, "oh"): {"P": "four1"}, (1, "pt0"): {"P": "four1"}, (1, "Ipen"): {"P": "four1"}}
+LATER = {(0, "ohc"): {"V": "m2_3"}, (0, "Tapp"): {"V": "m2_3"}, (0, "Trot"): {"P": "sm1b", "A": "g5"}, (0, "CE"): {"P": "sm1b"},
+         (0, "WINAa"): {"P": "sm1b", "A": "g5"}, (0, "WINAb"): {"P": "sm1b", "A": "g5"}}
 
-F16 = "Th:192 fT:192 Tapp:192 Hs:192 Hp:192 Tg:192 u:192 y1:192 DG:576 KB:12 LB:36 AB:78 nmh:576 Tc:192 VL:384"
+F16 = "Th:192 fT:192 Tapp:192 Hs:192 Hp:192 Tg:192 u:192 DG:576 KB:12 LB:36 AB:78 nmh:576 Tc:192 VL:384"
 B16 = ("raw:144 tm:144 I:256 NI BA NB W1:144 W2:144 Wk:144 WN:144 Ww:144 TUi TUr:256 BH:256 C15 CE15 CE CP CR R8n "
        "Ipen Sh SI Moh M15 MC CI PI PK PH HQ RA:384 RW:512 I3 tA tB tC ShN B16 M8:8 "
-       "ones:192 xc:192 ok:192 K1:192 y:192 ad:192 cap:192 kap:14 rA:14")
-F32 = ("crep:192 ohc:192 Trot:192 fst:192 Rv:192 RR:192 oyt:192 oyh:192 cw:16 SC:16 E0:16 NE:16 cols:16 "
+       "ones:192 xc:192 ok:192 K1:192 y:192 I5 I75 cap:192 kap:14 rA:14")
+F32 = ("crep:192 ohc:192 Trot:192 xh:192 fst:192 Rv:192 RR:192 oyt:192 oyh:192 cw:16 SC:16 E0:16 NE:16 cols:16 "
        "iq:12 ib:78 bi:12 bz:12 D0:36 D1:40 cf:36 rr:14 zt:12 x1:12 acc:2 r8")
 SCRATCH = {
     "X": ("sbuf", [128, CW], "bfloat16"), "XT": ("sbuf", [128, NH + 3072], "bfloat16"), "MX": ("sbuf", [128, 3072], "bfloat16"),
@@ -56,12 +56,13 @@ for _i in range(V):
 for _i in range(V - 1):
     SCRATCH["TO%d" % _i] = ("sbuf", [128, NP], "uint16")
 
-DMAS = ["dx", "dt", "dh", "dn", "dm", "dth", "dw", "ox", "oh", "ot", "om", "on"]
+DMAS = ["dx", "dt", "dh", "dn", "dm", "dth", "dw", "ox0", "ox1", "oh", "ot", "om", "on"]
 SEMAPHORES = ["qV", "qA", "qP", "qG", "snd"] + ["arr%d" % i for i in range(1, V)] + ["d_" + n for n in DMAS]
 
 
 def send_engines(topo, src, dst):
-    return topo.engines(src, dst)[:8]
+    e = topo.engines(src, dst)
+    return e[::len(e) // 8]
 
 
 def rank_program(g, core, T, topo):
@@ -123,7 +124,7 @@ def rank_program(g, core, T, topo):
 
     def dma(q, name, out, in_, r, w, kb):
         e = {"S": g.sync, "A": g.scalar}[q]
-        op(q, lambda: e.dma_start(out, in_), r, w, DMA + 3 * kb, dma="d_" + name)
+        op(q, lambda: e.dma_start(out, in_), r, w, DMA + 3.5 * kb, dma="d_" + name)
 
     def ms(ap, v, w, c=70):
         op("V", lambda: g.vector.memset(ap, v), "", w, c)
@@ -207,7 +208,7 @@ def rank_program(g, core, T, topo):
                           ("zc", "s", -1.0, 128.0), ("s37", "s", 37.0, 0.0)):
         col(nm, src, a, b)
     cols["w"], home["w"] = T.cols[:, 15:16], "c_w"
-    ts(cols["w"], A("wti"), 1.0 / 16, OP.mult, "wti", "c_w")
+    ts(cols["w"], A("wti"), 1.0 / 32, OP.mult, "wti", "c_w")
     eye(A("Sh"), T.SC[:, 0:1], "Sh", "n0")
     eye(A("tA"), cols["s"], "tA", "n15")
     eye(A("tB"), T.SC[:, 14:15], "tB", "n15")
@@ -218,18 +219,19 @@ def rank_program(g, core, T, topo):
     ts(A("M8"), T.raw[:, 16:144:16], 0.0, OP.is_equal, "raw", "M8")
     for nm, src, by in (("CR", "I", "cr"), ("NI", "I", -1.0), ("NB", "BA", -8.0), ("WN", "W1", -8.0), ("W2", "W1", 16.0),
                         ("Ipen", "I", "ip"), ("C15", "I", "e15"), ("CE15", "C15", E), ("CE", "I", E), ("Ww", "W1", "w"),
-                        ("CI", "I", "ci"), ("PI", "BA", "pi"), ("PK", "BA", "pk"), ("I3", "I", 3072.0), ("Wk", "W1", "kc"),
-                        ("CP", "I", "cp")):
+                        ("CI", "I", "ci"), ("PI", "BA", "pi"), ("PK", "BA", "pk"), ("I3", "I", 3072.0),
+                        ("CP", "I", "cp"), ("I5", "I", -0.5), ("I75", "I", -0.75)):
         scaled(nm, src, by)
     ts(A("M15"), A("BA"), cols["e15"], OP.mult, "BA E0", "M15", -1.0 / 4096, OP.mult)
-    ts(A("tC"), A("BA"), cols["e0"], OP.mult, "BA E0", "tC", 512.0, OP.mult)
+    ts(A("tC"), A("BA"), 2.0 ** -12, OP.mult, "BA", "tC")
     ts(A("ShN"), A("Sh"), -512.0, OP.mult, "Sh", "ShN")
     ts(A("B16"), A("BA"), 16.0, OP.mult, "BA", "B16")
-    tt(A("MC"), A("tC"), A("ShN"), OP.add, "tC ShN", "MC", 270)
     tt(A("PH"), A("B16"), A("ShN"), OP.add, "B16 ShN", "PH", 270)
     tt(A("HQ"), A("Sh"), A("C15"), OP.add, "Sh C15", "HQ", 270)
     less("SI", "Sh", "tA", 1.0, 6)
     less("Moh", "tA", "tB", 1.0 / 256, 7)
+    ts(A("tB"), I, -512.0, OP.mult, "I", "tB")
+    tt(A("tA"), A("B16"), A("tB"), OP.add, "B16 tB", "tA", 270)
     for h in range(2):
         scaled("BH%d" % h, "BA", 8192.0, out=T.BH[:, 128 * h:128 * h + 128])
     mm(B[1][:, 0:128], R8, R8, True, False, "R8n", "bk1", 70)
@@ -239,13 +241,14 @@ def rank_program(g, core, T, topo):
     ts(A("TUi"), T.oyh[:, 0:128], cols["zc"], OP.is_ge, "oyh c_zc", "TUi", c=140)
     ts(T.TUr[:, 0:128], T.oyh[:, 0:128], cols["zc"], OP.is_gt, "oyh c_zc", "TUr0", -8192.0, OP.mult, c=140)
     cp(T.TUr[:, 128:256], T.TUr[:, 0:128], "TUr0", "TUr1")
+    tt(A("MC"), A("tC"), T.TUr[:, 0:128], OP.add, "tC TUr0", "MC", 270)
     ts(A("bi"), A("iq"), cols["s"], OP.add, "iq SC", "bi")
     ts(A("bz"), A("bi"), 7.5 / 16, OP.add, "bi", "bz")
     ts(A("KB"), A("bi"), 16.0, OP.mult, "bi", "KB", float(NH), OP.add)
     ms(T.LB[:, 0:24], 0.0, "LB0")
     cp(T.LB[:, 24:36], A("bi"), "bi", "LB1")
-    ms(T.kap[:, 0:12], 1.0, "kap0")
-    ms(T.kap[:, 12:14], 8.0, "kap1")
+    ms(T.kap[:, 0:12], 0.5, "kap0")
+    ms(T.kap[:, 12:14], 4.0, "kap1")
     ts(T.abi[:, 0:78], A("ib"), cols["s37"], OP.add, "ib c_s37", "abi", c=80)
     ts(T.abi[:, 78:156], T.abi[:, 0:78], 2047, OP.bitwise_and, "abi", "abj", c=80)
     ts(A("AB"), T.abi[:, 78:156], -1023.5, OP.add, "abj", "AB", c=80)
@@ -280,9 +283,12 @@ def rank_program(g, core, T, topo):
     ts(A("TT0"), A("fst"), 3072.0, OP.min, "fst", "TT0", c=200)
     masked(1, "hai", 4, "RR")
     ts(A("Hs"), A("RR"), 3072.0, OP.min, "RR", "Hs", -E, OP.add, c=200)
-    ts(HFR, A("Hs"), cols["e0"], OP.mult, "Hs E0", "hfr", c=100)
-    diag(B[5][:, 256:268], "W1", "DG", NP, "hfr", "bk5", first=True)
+    ts(A("Wk"), A("raw"), 0.0, OP.is_equal, "raw E0", "Wk", cols["e0"], OP.mult)
+    diag(B[5][:, 256:268], "Wk", "Hs", NP, "Hs", "bk5", first=True)
+    scaled("Wk", "W1", "kc")
+    at[0] = (-1, "crep")
     front()
+    at[0] = None
     ms(T.D0[:, 0:36:3], BIG, "D0a")
     ms(T.D0[:, 1:36:3], -BIG, "D0b")
     ms(T.D1[:, 1:36:3], BIG, "D1b")
@@ -294,9 +300,10 @@ def rank_program(g, core, T, topo):
     mm(L(3), A("CE15"), A("ones"), False, True, "CE15 ones", "bk3")
     cp(A("Hp"), L(3), "bk3", "Hp", 200)
     hand_flags(len)
+    scaled("CR", "I", "cq")
 
-    def inside(lo, hi):
-        return [j for j in range(len(PIECES)) if lo <= PIECES[j][0] < hi]
+    def inside(lo, hi, parts=None):
+        return [j for j, p in enumerate(parts or PIECES) if lo <= p[0] < hi]
 
     def xts(lo, hi):
         return " ".join("XT%d" % j for j in inside(lo, hi))
@@ -325,19 +332,18 @@ def rank_program(g, core, T, topo):
             return T[nm][:, ro:ro + 128] if jj else T[nm][:, 0:128]
 
         def turn(mats, src, win, step):
-            now(win)
             for w in range(4):
+                now(win + "ab"[w // 2])
                 o = B[6 + w // 2][:, 256 * (w % 2):256 * (w % 2) + NP]
                 mm(o, mats[w][0], A(src), True, True, mats[w][1] + " " + src, "bk%d" % (6 + w // 2))
             for w in range(4):
+                now(win + "ab"[w // 2])
                 o = B[6 + w // 2][:, 256 * (w % 2):256 * (w % 2) + NP]
                 act(T[win][:, step * w:step * w + NP], o, AF.Copy, "bk%d" % (6 + w // 2), "%s%d" % (win, w))
 
         if last:
             at[0] = None
-            ts(A("ShN"), I, -512.0, OP.mult, "I", "ShN")
-            tt(A("PH"), A("B16"), A("ShN"), OP.add, "B16 ShN", "PH", 270)
-            scaled("CP", "I", "cq")
+            ts(T.bz[:, 6:12], T.bi[:, 6:12], 7.5 / 16 - 96, OP.add, "bi", "bz")
         now("xc")
         cp(A("xc"), A("X").indirect(A("cl")), "X Xp cl", "xc", G192)
         for j, (p, n, q) in enumerate(PIECES):
@@ -347,6 +353,8 @@ def rank_program(g, core, T, topo):
                 act(out, src, AF.Copy, "X Xp " + tn, "XT%d" % j, c=60 + GATHER * 16 * n)
             else:
                 cp(out, src, "X Xp " + tn, "XT%d" % j, 60 + GATHER * 16 * n)
+        now("xh")
+        act(A("xh"), A("xc"), AF.Identity, "xc", "xh", bias=2079.5)
         now("Th")
         ts(A("Th"), A(tn), -E, OP.add, tn, "Th", c=100)
         now("inv")
@@ -367,8 +375,9 @@ def rank_program(g, core, T, topo):
         if not last:
             now("front")
             front()
-        now("oh")
+        now("ff")
         mm(L(3), A("M15"), INV, True, True, "M15 inv", "bk3")
+        now("oh")
         mm(H(3), A("Moh"), INV, True, False, "Moh inv", "bk3")
         mm(H(3), A("C15"), A("ones"), False, True, "C15 ones", "bk3")
         now("fT")
@@ -395,63 +404,79 @@ def rank_program(g, core, T, topo):
         now("Rv")
         act(A("Rv"), A("WIN").indirect(T.ql[:, 12:24]), AF.Copy, "WIN0 WIN1 WIN2 WIN3 ql", "Rv", c=G192)
 
-        now("thr")
-        mm(L(0), T.R8n[0:9, :], T.nmh[0:9, 2 * NP:3 * NP], True, False, "R8n nmh2", "bk0")
-        now("NB")
-        mm(L(0), A("NB"), A("xc"), False, False, "NB xc", "bk0+")
-        now("Ipen")
-        mm(L(0), A("Ipen"), INV, False, False, "Ipen inv", "bk0+")
-        for b, p, n in ((1, 0, 128), (2, 128, 64)):
+        def opening(b, lo, hi, nm):
+            o, c, bk = B[b][:, 0:hi - lo], (hi - lo) // 2 + 3, "bk%d" % b
+            now("thr" + nm)
+            mm(o, T.R8n[0:9, :], T.nmh[0:9, 2 * NP + lo:2 * NP + hi], True, False, "R8n nmh2", bk, c)
+            now("NB" + nm)
+            mm(o, A("NB"), T.xc[:, lo:hi], False, False, "NB xc", bk + "+", c)
+            now("Ipen" + nm)
+            mm(o, A("Ipen"), T.DG[:, 2 * NP + lo:2 * NP + hi], False, False, "Ipen inv", bk + "+", c)
+
+        opening(0, 0, 128, "")
+        for b, p, n, r in ((1, 0, 128, 2), (2, 128, 64, 4)):
             now("four%d" % b)
-            for s in range(4):
-                mm(B[b][:, s:4 * n:4], I, T.xc[:, p:p + n], True, True, "I xc", "bk%d" % b, n // 2 + 2)
-        for j, (p, n, q) in enumerate(PIECES):
-            b, o = (1, 4 * p) if p < 128 else (2, 4 * (p - 128))
-            for s in range(4):
-                now("m%d_%d" % (j, s))
-                tt(T.MX[:, 16 * p + s:16 * (p + n):4], B[b][:, o:o + 4 * n], T.XT[:, 16 * p + s:16 * (p + n):4], OP.max,
-                   "bk%d XT%d" % (b, j), "MX%d_%d" % (j, s), max(70, 4 * n + 10))
+            for s in range(r):
+                mm(B[b][:, s:r * n:r], I, T.xc[:, p:p + n], True, True, "I xc", "bk%d" % b, n // 2 + 2)
+        for j, (p, n) in enumerate(MAXES):
+            b, r = (1, 2) if p < 128 else (2, 4)
+            o, st = r * (p % 128), 16 // r
+            for s in range(st):
+                now("m%d_%d" % (j, s % 4))
+                tt(T.MX[:, 16 * p + s:16 * (p + n):st], B[b][:, o:o + r * n], T.XT[:, 16 * p + s:16 * (p + n):st], OP.max,
+                   "bk%d " % b + xts(p, p + n), "MX%d_%d" % (j, s), max(70, r * n + 10))
         for c in range(3):
-            o = B[0][:, 64 * c:64 * c + 64]
+            b = c // 2
+            o, bk = B[b][:, 64 * (c % 2):64 * (c % 2) + 64], "bk%d" % b
+            if b:
+                opening(1, 128, NP, "B")
             now("sx%d" % c)
             for s in range(16):
                 mm(o, T.WN[:, 16 - s:144 - s], T.XT[:, 1024 * c + s:1024 * c + 1024:16], False, False,
-                   "WN " + xts(64 * c, 64 * c + 64), "bk0+", 34)
+                   "WN " + xts(64 * c, 64 * c + 64), bk + "+", 34)
             for k in range(16):
-                now("sm%d" % c + ("ab"[k // 8] if c == 1 else ""))
+                now("sm%d" % c + "ab"[k // 8])
                 s = k // 4 + 4 * (k % 4)
-                end = c == 2 and k == 15
+                end = c > 0 and k == 15
                 mm(o, T.W2[:, 16 - s:144 - s], T.MX[:, 1024 * c + s:1024 * c + 1024:16], False, end,
-                   "W2 " + " ".join("MX%d_%d" % (j, s % 4) for j in inside(64 * c, 64 * c + 64)), "bk0" if end else "bk0+", 34)
-        now("d0a")
-        mm(H(4), A("NI"), A("xc"), True, False, "NI xc", "bk4")
-        mm(B[4][:, NP:NP + 128], I, T.XT[:, 0:2048:16], False, False, "I " + xts(0, 128), "bk4", 70)
-        now("d0b")
-        mm(B[4][:, NP + 128:2 * NP], I, T.XT[:, 2048:3072:16], False, True, "I " + xts(128, NP), "bk4", 34)
-        now("ad")
-        act(A("ad"), H(4), AF.Abs, "bk4", "ad", scale=2.0)
+                   "W2 " + " ".join("MX%d_%d" % (j, s % (4 if b else 8)) for j in inside(64 * c, 64 * c + 64, MAXES)), bk if end else bk + "+", 34)
+        now("d0c")
+        mm(L(4), A("I75"), A("xc"), True, False, "I75 xc", "bk4")
+        for nm, lo, hi in (("d0a", 0, 128), ("d0b", 128, NP)):
+            now(nm)
+            mm(B[4][:, lo:hi], A("I5"), T.XT[:, 16 * lo:16 * hi:16], False, False, "I5 " + xts(lo, hi), "bk4", (hi - lo) // 2 + 3)
+            mm(B[4][:, lo:hi], I, T.MX[:, 16 * lo:16 * hi:16], False, hi == NP,
+               "I " + " ".join("MX%d_0" % j for j in inside(lo, hi, MAXES)), "bk4", (hi - lo) // 2 + 3)
         now("N0")
-        mm(L(4), A("NI"), A("xc"), True, False, "NI xc", "bk4")
-        mm(L(4), I, A("ad"), False, True, "I ad", "bk4")
-        act(T.XT[:, NH:NH + 3072:16], L(4), AF.Identity, "bk4", "N0", bias=0.5)
+        act(T.XT[:, NH:NH + 3072:16], L(4), AF.Identity, "bk4", "N0", bias=0.5, scale=4.0)
 
-        now("ok")
-        act(A("ok"), L(0), AF.Relu, "bk0 D1a", "ok", bias=T.D1[:, 36:37], scale=-1.0)
-        now("tri")
-        mm(L(1), A("TUi"), A("ok"), True, True, "TUi ok", "bk1")
-        now("K1")
-        act(A("K1"), L(1), AF.Sign, "bk1", "K1")
+        for b, lo, hi, nm in ((0, 0, 128, "A"), (1, 128, NP, "")):
+            n, bk = hi - lo, "bk%d" % b
+            now("ok" + nm)
+            act(T.ok[:, lo:hi], B[b][:, 0:n], AF.Relu, bk + " D1a", "ok" + nm, bias=T.D1[:, 36:37], scale=-1.0, c=n + 5)
+            now("tri" + nm)
+            mm(B[b][:, 128:128 + n], A("TUi"), T.ok[:, lo:hi], True, True, "TUi ok" + nm, bk, n // 2 + 3)
+            now("K1" + nm)
+            act(T.K1[:, lo:hi], B[b][:, 128:128 + n], AF.Sign, bk, "K1" + nm, c=n + 5)
+        if not last:
+            now("CI")
+            mm(L(2), A("CI"), INV, True, False, "CI inv", "bk2")
+            now("cap")
+            mm(L(2), A("MC"), A("ok"), False, True, "MC ok okA", "bk2")
+            act(A("cap"), L(2), AF.Sign, "bk2", "cap acc", bias=-2.0 ** -14, acc=T.acc[:, 0:1], c=220)
         kp = B[0][:, 256:268]
-        now("kd")
+        now("kb")
         mm(kp, I, A("KB"), True, False, "I KB", "bk0", 34)
-        diag(kp, "Wk", "K1", NP, "K1", "bk0")
+        now("kd")
+        diag(kp, "Wk", "K1", NP, "K1 K1A", "bk0")
         now("kl")
         cp(A("kl"), kp, "bk0", "kl")
         now("pt")
         mm(L(5), rot("I"), A("Tapp"), True, False, "I I2 Tapp", "bk5")
         now("ramp")
-        mm(L(3), rot("TUr"), A("ok"), False, True, "TUr0 TUr1 ok", "bk3")
-        mm(L(5), rot("BH"), A("ok"), False, True, "BH0 BH1 ok", "bk5")
+        mm(L(3), rot("TUr"), A("ok"), False, True, "TUr0 TUr1 ok okA", "bk3")
+        now("BH")
+        mm(L(5), rot("BH"), A("ok"), False, True, "BH0 BH1 ok okA", "bk5")
         now("fst")
         tt(A("fst"), L(3), A("Trot"), OP.max, "bk3 Trot", "fst")
         now("Tc")
@@ -473,14 +498,12 @@ def rank_program(g, core, T, topo):
             now("yt")
             cards("Tc", 0, 3, "oyt", "yt", "yn")
         now("u")
-        tt(A("u"), A("XT").indirect(A("kl")), A("xc"), OP.add, xts(0, NP) + " N0 kl xc", "u", G192)
-        now("y1")
-        ts(A("y1"), A("u"), 0.5, OP.mult, "u", "y1", 1023.75, OP.add, c=100)
+        tt(A("u"), A("XT").indirect(A("kl")), A("xh"), OP.add, xts(0, NP) + " N0 kl xh", "u", G192)
         pz = B[2][:, 256:268]
         now("zd")
-        diag(pz, "Ww", "y1", NP, "y1", "bk2", first=True)
+        diag(pz, "Ww", "u", NP, "u", "bk2", first=True)
         now("y")
-        ts(A("y"), A("y1"), -1024.0, OP.add, "y1", "y", c=100)
+        ts(A("y"), A("u"), -2080.0, OP.add, "u", "y", 0.5, OP.mult, c=100)
         now("zf")
         tt(A("zf"), pz, A("bz"), OP.subtract, "bk2 bz", "zf", 70)
         now("zt")
@@ -488,16 +511,19 @@ def rank_program(g, core, T, topo):
         now("zl")
         ts(A("zl"), A("zt"), 16.0, OP.mult, "zt", "zl")
         now("X")
-        cp(A("X").indirect(A("zl")), A("y"), "y zl Xp", "X", 50 + SCATTER * NP)
+        if last:
+            for h in range(2):
+                now("X")
+                cp(T.X[:, 1536 * h:1536 * h + 1536].indirect(T.zl[:, 6 * h:6 * h + 6]), T.y[:, 96 * h:96 * h + 96],
+                   "y zl X", "X%d" % h, 50 + SCATTER * 96)
+        else:
+            cp(A("X").indirect(A("zl")), A("y"), "y zl Xp", "X", 50 + SCATTER * NP)
         if not last:
             now("D1b")
             tt(T.D1[:, 1:36:3], kp, T.cf[:, 2:36:3], OP.max, "bk0 cf", "D1b", 70)
             now("D0b")
             act(T.D0[:, 1:36:3], kp, AF.Identity, "bk0", "D0b", bias=NH + 3071.0, scale=-1.0, c=70)
-            now("cap")
-            mm(H(1), A("CI"), INV, True, False, "CI inv", "bk1")
-            mm(H(1), A("MC"), A("K1"), False, True, "MC K1", "bk1")
-            act(A("cap"), H(1), AF.Relu, "bk1", "cap acc", scale=1.0 / 512, acc=T.acc[:, 0:1], c=220)
+            now("rA")
             act(T.rA[:, 0:13], T.kap[:, 0:13], AF.Identity, "kap0 kap1 acc", "rA", scale=T.acc[:, 0:1], c=70)
             pa = B[1][:, 400:413]
             now("pa")
@@ -510,10 +536,12 @@ def rank_program(g, core, T, topo):
             choose(now)
         now("pen")
         mm(H(5), I if last else A("HQ"), A("Hp"), True, True, "I HQ Hp", "bk5")
-        mm(L(5), A("PH"), HINV, True, False, "PH hinv", "bk5")
-        mm(L(5), A("CP"), A("ones"), False, False, "CP ones", "bk5")
+        ph, cst = ("tA", "CR") if last else ("PH", "CP")
+        mm(L(5), A(ph), HINV, True, False, ph + " hinv", "bk5")
+        mm(L(5), A(cst), A("ones"), False, False, cst + " ones", "bk5")
         mm(L(5), A("PI"), INV, False, False, "PI inv", "bk5")
-        mm(L(5), A("PK"), A("K1"), False, True, "PK K1", "bk5")
+        now("PK")
+        mm(L(5), A("PK"), A("K1"), False, True, "PK K1 K1A", "bk5")
         now("RR")
         tt(A("RR"), L(5), A("Rv"), OP.max, "bk5 Rv", "RR")
         now("Hp")
@@ -524,7 +552,8 @@ def rank_program(g, core, T, topo):
             now("yh")
             cards("Hp", 1, 1, "oyh", "yh", "ym")
     at[0] = None
-    dma("A", "ox", T.yx[:, :], T.X[:, 0:3072], "X", "", 768)
+    for h in range(2):
+        dma("SA"[h], "ox%d" % h, T.yx[:, 1536 * h:1536 * h + 1536], T.X[:, 1536 * h:1536 * h + 1536], "X%d" % h, "", 384)
 
     emit(g, core, T, topo, plan(ops), rank)
 

@@ -1,4 +1,4 @@
-from concourse.mybir import AluOpType, ActivationFunctionType
+from concourse.mybir import AluOpType, ActivationFunctionType, AxisListType
 
 OP = AluOpType
 AF = ActivationFunctionType
@@ -7,12 +7,23 @@ NP = 192
 CW = 3088
 E = 1536.0
 NH = 8192
+XB = 10240
 OFF = 3072.5
 R2K = 1.5 * 2 ** 34
+R16 = 1.5 * 2 ** 27
+R1 = 1.5 * 2 ** 23
 BIG = 30000.0
-PIECES = ((0, 32, "A"), (32, 32, "V"), (64, 64, "A"), (128, 14, "V"), (142, 30, "A"), (172, 20, "A"))
-MAXES = ((0, 32), (32, 32), (64, 64), (128, 44), (172, 20))
-WAKE, DMA, REMOTE, GATHER, SCATTER = 250, 1200, 2000, 1.6, 4.0
+SINE = (-2.679189617679568e-07, 62.462959736501446, 113.70776756960623, 10536.242908533108)
+SP = 96
+PARTS = (("A", 0, SP, 0), ("B", SP, NP, 1))
+PIECES = ((0, 48, "A"), (48, 48, "V"), (96, 56, "A"), (152, 40, "A"))
+MAXES = ((0, 96), (96, 56), (152, 40))
+ON = {"inv": "V", "cl": "A", "ql": "A", "hinv": "A", "Th": "V", "y": "A", "x1": "A", "RR": "A", "hfr": "A", "D0b": "A", "xh": "A"}
+WE = E if ON["RR"] == "A" else 0.0
+REP = (2, 2)
+ZR = (1, 1)
+SX = SM = ((0, SP), (SP, NP - SP))
+WAKE, DMA, REMOTE, GATHER, SCATTER = 200, 1700, 2000, 1.6, 4.0
 
 
 def _m(*pieces):
@@ -20,44 +31,109 @@ def _m(*pieces):
 
 
 ORDER = {
-    "V": "inv Th xc g1 fT ohc g3 Tapp " + _m(0, 1) + _m(2) + "x1 m3_0 m4_0 m3_1 m4_1 m3_2 m4_2 x2 m4_3 m3_3 "
-         "x3 x4 ql Tg fst Tc to yt kl u rr D1b RR D1a y Hp scan zf cl zt hinv yh zl hfr X",
-    "A": "g0 g2 g4 g5 WINAa okA Trot WINAb front ok K1A xh K1 N0 cap WINa WINb rA Rv D0b yt yh crep",
-    "P": "thr Ipen ff oh LB pt0 four1 NB SI four2 sx0 Trot WINAa WINAb sm0a sx1 CE sm0b sm1a sm1b thrB NBB IpenB sx2 sm2a sm2b "
-         "triA d0c pt d0a CI ramp tri d0b BH kb cap WINa WINb kd pen pa PK zd yt yh",
+    "V": "xc g1 Q m0_0 m0_1 Tapp m0_3 m0_2 m1_0 m1_2 m1_1 m1_3 Hp- m2_2 m2_1 m2_0 m2_3 fstA kA TcA uA fstB TcB kB zrA uB D1b zfA rr ql zlA D1a zrB XA scan zfB U0 cl zlB U1 XB inv+ yt yh",
+    "A": "g0 g2 g3 xh hfr- okA hinv- Trot K1A N0A okB N0B K1B yA cap rA D0b x1 yB front Gt wall RR crep Th+ yt yh",
+    "P": "Tc Tapp IpenA four1 Rv1- Trot wall- four2 NBA sx0 sm0a sm0b CEA sx1 ptA sm0c d0A sm0d sm1c sm1a sm1b thrB sm1d sx2 triA BHA sm2c sm2b rampA sm2a kA IpenB NBB sm2d d0B CI ptB zcA triB BHB CEB rampB cap zA kB LB pa zcB thrA+ zB pen F PK Rv0 yt yh",
 }
-LATER = {(0, "ohc"): {"V": "m2_3"}, (0, "Tapp"): {"V": "m2_3"}, (0, "Trot"): {"P": "sm1b", "A": "g5"}, (0, "CE"): {"P": "sm1b"},
-         (0, "WINAa"): {"P": "sm1b", "A": "g5"}, (0, "WINAb"): {"P": "sm1b", "A": "g5"}}
+LAST = {
+    "V": "xc g1 Q m0_0 m0_1 Tapp m0_3 m0_2 m1_0 m1_2 m1_1 m1_3 Hp- m2_2 m2_1 m2_0 m2_3 kA uA fstA TcA ql kB zrA uB zfA fstB zlA TcB XA zrB U0 zfB U1 zlB yt XB Hp yh",
+    "A": "g0 g2 g3 xh hfr- okA hinv- Trot K1A N0A okB N0B x1 K1B yA Gt yB wall RR yt yh",
+    "P": "Tc Tapp IpenA four1 Rv1- Trot wall- four2 NBA sx0 sm0a sm0b CEA sx1 ptA sm0c d0A sm0d sm1c sm1a sm1b thrB sm1d sx2 triA BHA sm2c sm2b rampA sm2a kA IpenB NBB sm2d d0B LB ptB zcA triB BHB CEB rampB zA kB F zcB zB pen PK Rv0 Rv1 wall yt yh",
+}
+ORDER = {
+    "V": "xc U1- g1 inv m0_2 m0_3 m0_1 m1_0 m1_1 m0_0 m1_3 m1_2 Q Hp- Tapp m2_2 m2_0 m2_1 m2_3 fstA TcA kA uA fstB kB TcB uB zrA D1b rr zfA ql zrB zlA D1a zfB XA scan zlB cl XB U0 yt yh",
+    "A": "g0 g2 Th g3 Trot xh okA hinv- hfr- N0A K1A okB N0B K1B cap yA rA D0b yB x1 front Gt RR wall crep yt yh",
+    "P": "Tc NBA Rv0- Rv1- four2 four1 wall- sx0 sm0c IpenA sm0d sx1 sm0b Tapp sm1b d0A Trot sm1a sm0a sm1c thrB NBB sm1d sx2 CEA triA rampA IpenB sm2c ptA BHA sm2a sm2b sm2d kA d0B ptB triB BHB CI cap CEB rampB zcA kB zA LB pa zcB zB F pen thrA+ PK yt yh",
+}
+LAST = {
+    "V": "xc U1- g1 inv m0_3 m0_2 m0_1 m1_1 m1_3 m1_2 m1_0 m0_0 Q Hp- m2_0 m2_1 m2_2 m2_3 Tapp kA ql fstA uA kB TcA uB U0 zrA fstB zrB zfA U1 zfB zlA TcB zlB XA yt Hp XB yh",
+    "A": "g0 g2 Th g3 xh N0A hfr- hinv- Trot okA K1A okB x1 K1B N0B Gt yA wall RR yB yt yh",
+    "P": "Rv0- four2 Rv1- wall- NBA four1 Tc sx0 sm0d sx1 IpenA Tapp sm0c sm0b sm1c d0A thrB sm0a sm1a NBB Trot sm1b sm1d sx2 sm2a sm2b sm2c triA IpenB sm2d LB kA triB ptB CEA rampA ptA BHA d0B kB zcA F CEB zA zcB rampB zB BHB pen PK Rv0 Rv1 wall yt yh",
+}
+ORDER = {
+    "V": "xc g1 m0_1 m0_3 m0_2 inv m1_0 m0_0 Hp- m1_1 m1_2 m1_3 Q Tapp m2_1 m2_0 m2_2 m2_3 kA fstA uA TcA zrA kB ztA zfA uB zlA D1b rr ql XA zrB D1a zfB ztB scan fstB zlB cl TcB U0 XB U1 yt yh",
+    "A": "g2 Th g3 xh N0A hfr- hinv- okA Trot K1A okB N0B K1B yA cap rA D0b x1 yB front Gt wall crep RR g0+ yt yh",
+    "P": "Rv1- Tc four1 wall- NBA four2 sx0 sm0b sm0d sx1 Tapp sm0a d0A sm0c sm1a IpenA Trot sm1b sm1c sm1d thrB sx2 IpenB CEA ptA triA sm2a sm2c sm2b kA NBB rampA sm2d d0B BHA zcA triB CI cap zA kB LB pa F zcB zB pen ptB CEB rampB PK BHB thrA+ Rv0 yt yh",
+}
+LAST = {
+    "V": "xc g1 m0_1 m0_3 m0_2 inv m1_0 m0_0 Hp- m1_1 m1_2 m1_3 Q Tapp m2_1 m2_0 m2_2 m2_3 kA fstA uA TcA zrA kB ztA zfA uB zlA ql XA zrB zfB ztB fstB zlB TcB U0 XB U1 yt Hp yh",
+    "A": "g2 Th g3 xh N0A hfr- hinv- okA Trot K1A okB N0B K1B yA x1 yB Gt wall RR yt yh",
+    "P": "Rv1- Tc four1 wall- NBA four2 sx0 sm0b sm0d sx1 Tapp sm0a d0A sm0c sm1a IpenA Trot sm1b sm1c sm1d thrB sx2 IpenB CEA ptA triA sm2a sm2c sm2b kA NBB rampA sm2d d0B BHA zcA triB zA kB LB F zcB zB pen ptB CEB rampB PK BHB Rv0 Rv1 wall yt yh",
+}
+ORDER = {
+    "V": "xc g1 invA U1- m0_3 m0_1 m0_0 QA m0_2 m1_0 m1_1 m1_2 m1_3 TappA Hp- invB okA m2_2 m2_1 m2_0 m2_3 kA uA okB QB fstA TappB TcA zrA ztA zfA kB zlA uB XA ql D1b zrB rr ztB D1a zfB fstB scan zlB TcB cl XB U0 yt yh",
+    "A": "g0 ThA g2 g3 N0A ThB hinv- xh K1A hfr- TrotA yA K1B N0B TrotB cap x1 D0b rA yB wall RR front Gt SD+ crep yt yh",
+    "P": "Rv0- four1 TpA NBA four2 TappA Rv1- IpenA TrotA wall- sx0d sx0a sx0c sm0a sx0b d0A sm0b sm0c sm0d thrB CEA NBB IpenB sx1a triA sx1d sx1b sx1c TpB kA sm1b sm1c sm1a sm1d TappB rampA ptA BHA zcA zA triB d0B CI LBa TrotB kB cap LBb pen PK ptB LT thrA+ zcB zB pa BHB Fa CEB rampB Fb yt yh",
+}
+LAST = {
+    "V": "U1- xc g1 invA Hp- m0_1 m0_0 m0_2 m1_0 m1_1 m1_2 m1_3 m0_3 invB m2_0 okA m2_1 QB m2_2 m2_3 TappB QA TappA kA okB uA fstA ql zrA TcA kB fstB ztA zfA uB zlA U0 U1 zrB XA ztB zfB TcB zlB yt Hp XB yh",
+    "A": "g0 ThA g2 g3 ThB hfr- xh N0A TrotA K1A hinv- x1 TrotB N0B K1B yA Gt wall yB RR yt yh",
+    "P": "Rv0- Rv1- four1 wall- IpenA TpA TpB NBA TrotA TappA four2 sx0a d0A sx0b sx0d sm0a sm0b sx0c sm0c sm0d thrB TappB NBB IpenB sx1b sx1d sm1a triA sx1c sx1a d0B sm1b sm1c kA sm1d TrotB LBa LBb zcA CEA triB ptA rampA BHA ptB LT zA Fa kB CEB rampB BHB Fb pen zcB zB PK Rv0 Rv1 wall yt yh",
+}
+ORDER = {
+    "V": "xc g1 invA U1- m0_3 m0_1 m0_0 QA m0_2 m1_0 m1_1 m1_2 m1_3 TappA Hp- invB okA m2_2 m2_1 m2_0 m2_3 kA uA okB QB fstA TappB TcA zrA ztA zfA kB zlA uB XA ql D1b zrB rr ztB D1a zfB fstB scan zlB TcB cl XB U0 yt yh",
+    "A": "g0 ThA g2 g3 ThB hinv- xh K1A N0A hfr- TrotA yA K1B N0B TrotB cap x1 D0b rA yB wall RR front Gt SD+ crep yt yh",
+    "P": "Rv0- four1 TpA NBA four2 TappA Rv1- IpenA TrotA wall- sx0d sx0a sx0c sm0a sx0b sm0b sm0c sm0d thrB CEA NBB IpenB sx1a triA d0A sx1d sx1b sx1c TpB kA sm1b sm1c sm1a sm1d TappB rampA ptA BHA zcA zA triB d0B CI LBa TrotB kB cap LBb pen PK ptB LT zcB zB pa BHB Fa CEB rampB Fb thrA+ yt yh",
+}
+LAST = {
+    "V": "xc g1 U1- invA m0_3 m0_2 m0_0 invB m0_1 m1_1 m1_0 m1_2 m1_3 Hp- QA okA m2_1 QB m2_2 m2_0 TappB m2_3 TappA kA okB uA kB zrA ql fstA uB ztA TcA fstB zfA U0 zlA TcB zrB U1 ztB zfB XA zlB yt Hp XB yh",
+    "A": "ThA g0 g2 ThB g3 hinv- xh TrotA K1A hfr- N0A N0B K1B x1 yA TrotB Gt yB wall RR yt yh",
+    "P": "Rv0- TpA four1 Rv1- TappA TrotA NBA IpenA wall- four2 sx0d sx0c sm0b sx0a sm0a sx0b sm0c sm0d TpB thrB TappB NBB sx1c sx1a IpenB triA d0A sx1d sx1b sm1c sm1b sm1a kA sm1d LBa d0B ptA triB LBb CEA zcA kB zA TrotB CEB LT rampA ptB rampB BHB zcB BHA Fa Fb zB pen PK Rv0 Rv1 wall yt yh",
+}
+ORDER = {
+    "V": "xc g1 invA U1- m0_2 m0_0 m0_1 QA m0_3 Hp- m1_0 m1_1 m1_2 m1_3 TappA invB okA m2_2 m2_0 m2_3 m2_1 fstA kA TcA uA okB QB TappB zrA zfA ztA kB zlA uB XA zrB fstB D1b rr ztB zfB TcB D1a zlB scan XB U0 yt yh",
+    "A": "g0 g2 g3 N0A hfr- xh TrotA ThB K1A hinv- yA TrotB N0B K1B cap D0b rA x1 yB wall RR ql front Gt SD+ cl ThA+ crep yt yh",
+    "P": "Rv0- four1 four2 TpA NBA TappA Rv1- IpenA wall- TrotA sx0b sx0a sx0d sx0c d0A sm0b sm0a sm0c sm0d ptA thrB sx1d triA sx1c CEA sx1b sm1c IpenB sm1a rampA kA NBB BHA sx1a sm1b sm1d TpB TappB d0B TrotB zcA zA triB CI LBa kB cap LBb pen PK zcB zB CEB rampB pa ptB LT BHB Fa Fb thrA+ yt yh",
+}
+ORDER = {
+    "V": "invA U0- xc g1 U1- m0_2 m0_1 QA m0_0 m0_3 TappA invB m1_1 okA m1_2 m2_1 m2_2 m1_3 m2_0 m1_0 m2_3 Hp- fstA kA TcA okB uA QB TappB zrA kB zfA ztA uB fstB D1b zlA TcB zrB rr XA ztB zfB D1a zlB scan XB yt yh",
+    "A": "SD cl- ThA crep- g0 g2 g3 N0A xh wall- ThB RR- K1A TrotA hinv- K1B N0B yA hfr- TrotB cap rA yB x1 ql front D0b Gt yt yh",
+    "P": "thrA four1 PK- TpA IpenA Rv0- NBA TappA sx0a sx0b sx0c sx0d Rv1- four2 sm0c TrotA d0A sm0b sm0a sm0d CEA thrB NBB ptA IpenB sx1c triA sx1d sx1b sm1b wall- sx1a rampA BHA kA sm1c sm1a sm1d TpB zcA TappB triB d0B CI zA TrotB kB cap CEB ptB rampB BHB LBa zcB LBb zB pa LT Fa pen Fb yt yh",
+}
+LAST = {
+    "V": "U1- U0- xc g1 invA invB m0_0 m0_1 m0_2 QA m0_3 m1_2 TappA m1_0 okA m2_2 m1_1 m2_1 m2_0 m1_3 m2_3 kA Hp- uA okB QB TappB zrA kB zfA uB ztA fstB fstA zlA TcA XA zrB U0 U1 zfB ztB TcB zlB yt XB Hp yh",
+    "A": "SD cl- ThA crep- g0 g2 g3 TrotA wall- N0A RR- K1A ThB xh hinv- TrotB N0B hfr- K1B x1 yB yA ql Gt wall RR yt yh",
+    "P": "Rv0- TrotA thrA four1 TpA Rv1- sx0a sx0d four2 sx0b PK- IpenA TappA sm0b d0A NBA sx0c sm0a sm0c thrB sm0d NBB IpenB CEA sx1c sx1a sx1b triA sm1c wall- sm1b kA sm1a sx1d sm1d d0B TrotB TpB TappB triB zcA CEB ptA rampA zA kB LBa LBb ptB rampB BHB BHA LT zcB Fa zB Fb pen PK Rv0 Rv1 wall yt yh",
+}
+ORDER = {
+    "V": "U0- xc U1- g1 ThA ThB invA invB m0_0 m0_1 QA m0_2 TappA m0_3 m1_0 m1_1 okA m1_2 m2_2 m2_0 m2_1 m1_3 m2_3 fstA QB Hp- TcA okB kA TappB uA fstB kB TcB uB zrA D1b ztA zrB rr zfA zfB D1a ztB zlA scan zlB XA XB yt yh",
+    "A": "SD wall- crep- RR- g0 g2 g3 N0A K1A xh TrotA hinv- K1B N0B TrotB hfr- yA cap D0b rA x1 yB front ql Gt cl yt yh",
+    "P": "thrA Fb- four2 Rv0- four1 Rv1- TpB wall- NBA TpA sx0d sx0c TappB TappA d0A sm0a IpenA sx0b TrotA sx0a sm0b CEA ptA sm0c sm0d thrB NBB IpenB sx1a triA sx1b sx1c sx1d rampA BHA sm1a sm1b sm1c sm1d kA d0B CI triB CEB zcA TrotB ptB rampB BHB kB cap LBa zA LBb zcB zB pa LT pen PK Fa yt yh",
+}
+LAST = {
+    "V": "U1- U0- xc g1 invA ThB ThA m0_0 m0_2 m0_1 m0_3 QA invB m1_1 TappA Hp- okA m1_0 m2_0 m2_1 m1_3 m2_2 m1_2 m2_3 QB kA TappB okB uA zrA fstA zfA ztA kB zlA uB XA zrB U0 ztB U1 zfB fstB zlB TcA TcB XB yt Hp yh",
+    "A": "SD RR- wall- crep- g0 g2 g3 N0A hfr- hinv- K1A xh TrotA K1B x1 N0B TrotB yA ql Gt wall RR yB yt yh",
+    "P": "Fb- Rv0- TpA Rv1- thrA four1 sx0a TappA sx0c four2 sx0d wall- sm0a sm0c d0A NBA TpB sm0b sx0b IpenA thrB sm0d IpenB TappB CEA ptA NBB TrotA sx1c sx1a triA sx1d sm1b sm1a rampA sx1b kA sm1c sm1d d0B LBa zcA triB LBb zA BHA CEB TrotB kB pen ptB LT rampB PK zcB Fa zB Fb BHB Rv0 Rv1 wall yt yh",
+}
+LATER = {(0, "first"): {"A": "g2"}, (0, "TpA"): {"P": "sm0d"}, (0, "TappA"): {"P": "sm0d", "V": "m1_2"}, (0, "QA"): {"V": "okA"},
+         (0, "TpB"): {"P": "IpenB"}, (0, "TappB"): {"P": "IpenB", "V": "kA"}, (0, "CEA"): {"P": "IpenB"}, (0, "ptA"): {"P": "IpenB"}}
 
-F16 = "Th:192 fT:192 Tapp:192 Hs:192 Hp:192 Tg:192 u:192 DG:576 KB:12 LB:36 AB:78 nmh:576 Tc:192 VL:384"
-B16 = ("raw:144 tm:144 I:256 NI BA NB W1:144 W2:144 Wk:144 WN:144 Ww:144 TUi TUr:256 BH:256 C15 CE15 CE CP CR R8n "
-       "Ipen Sh SI Moh M15 MC CI PI PK PH HQ RA:384 RW:512 I3 tA tB tC ShN B16 M8:8 "
-       "ones:192 xc:192 ok:192 K1:192 y:192 I5 I75 cap:192 kap:14 rA:14")
-F32 = ("crep:192 ohc:192 Trot:192 xh:192 fst:192 Rv:192 RR:192 oyt:192 oyh:192 cw:16 SC:16 E0:16 NE:16 cols:16 "
-       "iq:12 ib:78 bi:12 bz:12 D0:36 D1:40 cf:36 rr:14 zt:12 x1:12 acc:2 r8")
+F16 = "Th:192 Q:192 Tapp:192 crep:192 Hs:192 Hp:192 u:192 DG:576 AB:78 nmh:576 Tc:192 VL:384 MK KM ZM LT SQA SQB FH:64"
+B16 = ("raw:144 tm:144 I:256 BA NB S8:8 S16:8 SL:8 RL:24 Wk:144 TUr:256 BH:256 C15 CE15 CE CR R8n "
+       "Ipen Sh MF Mx I12 I8 BAk BAw MC CI PI PK PH HQ I3 tA tB tC ShN B16 M8:8 jt i2 zero "
+       "ones:192 xc:192 K1:192 y:192 I5 I75 cap:192 kap:14 rA:14 wall:192")
+F32 = ("Trot:192 xh:192 fst:192 Gt:192 U:384 RR:192 oyt:192 oyh:192 cw:16 SC:16 E0:16 NE:16 cols:32 M8f:8 "
+       "ib:78 D0:36 D1:40 cf:36 rr:14 zr:24 zf:12 bz:8 acc:2 r8 SD TAB ta tb tw tq")
 SCRATCH = {
-    "X": ("sbuf", [128, CW], "bfloat16"), "XT": ("sbuf", [128, NH + 3072], "bfloat16"), "MX": ("sbuf", [128, 3072], "bfloat16"),
-    "IOT": ("sbuf", [128, 3072], "float32"), "WIN": ("sbuf", [128, 4096], "float32"), "WINA": ("sbuf", [128, 1024], "float32"),
+    "X": ("sbuf", [128, CW], "bfloat16"), "XT": ("sbuf", [128, XB + NH + 2048], "bfloat16"), "MX": ("sbuf", [128, 3072], "bfloat16"),
+    "IOT": ("sbuf", [128, 3072], "float32"), "FE": ("sbuf", [128, 4, 128], "float16"), "ME": ("sbuf", [128, 2, 128], "float32"),
     "nmi": ("sbuf", [8, 576], "int32"), "omn": ("sbuf", [8, 2 * NP], "float32"),
     "tri": ("sbuf", [128, NP], "int32"), "hai": ("sbuf", [128, NP], "int32"), "wti": ("sbuf", [128, 1], "int32"),
-    "cwi": ("sbuf", [128, 32], "int32"), "abi": ("sbuf", [128, 156], "int32"), "zf": ("sbuf", [128, 12], "int32"),
-    "xi": ("sbuf", [128, 36], "int32"),
+    "cwi": ("sbuf", [128, 32], "int32"), "abi": ("sbuf", [128, 156], "int32"), "TI": ("sbuf", [128, 128], "int32"),
     "cl": ("sbuf", [128, 12], "uint16"), "kl": ("sbuf", [128, 12], "uint16"), "zl": ("sbuf", [128, 12], "uint16"),
-    "ql": ("sbuf", [128, 24], "uint16"),
+    "ql": ("sbuf", [128, 12], "uint16"),
+    "TO": ("sbuf", [128, NP * (V - 1)], "uint16"), "TT": ("sbuf", [128, NP * V], "uint16"),
 }
 for _names, _dt in ((F16, "float16"), (B16, "bfloat16"), (F32, "float32")):
     for _n in _names.split():
         _n, _w = (_n.split(":") + ["128"])[:2]
         SCRATCH[_n] = ("sbuf", [128, int(_w)], _dt)
 for _i in range(8):
-    SCRATCH["bk%d" % _i] = ("psum", [128, 512], "float32")
-for _i in range(V):
-    SCRATCH["TT%d" % _i] = ("sbuf", [128, NP], "uint16")
-for _i in range(V - 1):
-    SCRATCH["TO%d" % _i] = ("sbuf", [128, NP], "uint16")
+    SCRATCH["bk%d" % _i] = ("psum", [128, 32, 16] if _i in (0, 2) else [128, 512], "float32")
 
-DMAS = ["dx", "dt", "dh", "dn", "dm", "dth", "dw", "ox0", "ox1", "oh", "ot", "om", "on"]
-SEMAPHORES = ["qV", "qA", "qP", "qG", "snd"] + ["arr%d" % i for i in range(1, V)] + ["d_" + n for n in DMAS]
+DMAS = ["dx", "dt", "dh", "dn", "dm", "dth", "dw", "oxA", "oxB", "oh", "ot", "om", "on"]
+SEMAPHORES = (["qV", "qA", "qP", "qG", "snd"] + ["arr%s%d" % (p[0], i) for i in range(1, V) for p in PARTS]
+              + ["d_" + n for n in DMAS])
 
 
 def send_engines(topo, src, dst):
@@ -102,7 +178,7 @@ def rank_program(g, core, T, topo):
                     order.update(a[q])
                 a[q] = a[q] + [k] if lastq.get(n) == q and q != "P" else [k]
                 lastq[n] = q
-        ops.append({"q": q, "f": f, "deps": deps, "order": order, "dma": dma, "c": c, "at": at[0]})
+        ops.append({"q": q, "f": f, "deps": deps, "order": order, "dma": dma, "c": c, "at": None if q == "S" else at[0]})
 
     def ts(out, in0, s1, o1, r, w, s2=None, o2=None, c=70):
         if o2 is None:
@@ -116,8 +192,17 @@ def rank_program(g, core, T, topo):
     def cp(out, a, r, w, c=70):
         op("V", lambda: g.vector.tensor_copy(out, a), r, w, c)
 
+    def pick(out, a, r, w, c):
+        op("V", lambda: g.vector.tensor_reduce(out, a, AxisListType.X, OP.max), r, w, c)
+
     def act(out, a, fn, r, w, bias=0.0, scale=1.0, acc=None, c=200):
         op("A", lambda: g.scalar.activation(out, a, fn, bias=bias, scale=scale, accum_out=acc), r, w, c)
+
+    def lin(q, out, a, scale, bias, r, w, c):
+        if q == "A":
+            act(out, a, AF.Identity, r, w, bias=bias, scale=scale, c=max(70, c))
+        else:
+            ts(out, a, scale, OP.mult, r, w, bias, OP.add, c=max(70, c // 2))
 
     def mm(out, l, rr, st, sp, r, w, c=100):
         op("P", lambda: g.tensor.matmul(out, l, rr, st, sp), r, w, c)
@@ -138,11 +223,14 @@ def rank_program(g, core, T, topo):
 
     B = [T["bk%d" % i] for i in range(8)]
 
+    def R(b, lo, hi, first=0, step=1):
+        return B[b][:, lo // 16:hi // 16, first:16:step] if b in (0, 2) else B[b][:, lo + first:hi:step]
+
     def L(b):
-        return B[b][:, 0:NP]
+        return R(b, 0, NP)
 
     def H(b):
-        return B[b][:, NP:2 * NP]
+        return R(b, NP, 2 * NP)
 
     def A(nm):
         return T[nm][:, :]
@@ -155,18 +243,24 @@ def rank_program(g, core, T, topo):
     dma("A", "dm", T.nmi[:, NP:2 * NP], T.mh[:, :], "", "nmi1", 6)
     dma("S", "dt", A("tri"), T.trains[:, :], "", "tri", 96)
     dma("A", "dh", A("hai"), T.hands[:, :], "", "hai", 96)
-    dma("S", "dx", T.X[:, 0:3072], T.x0[:, :], "", "X", 960)
-    dma("A", "dth", T.nmi[:, 2 * NP:3 * NP], T.th[:, :], "", "nmi2", 6)
+    dma("S", "dth", T.nmi[:, 2 * NP:3 * NP], T.th[:, :], "", "nmi2", 6)
+    dma("S", "dx", T.X[:, 0:3072], T.x0[:, :], "", "XA XB", 960)
     dma("A", "dw", A("wti"), T.wt[:, :], "", "wti", 1)
 
     op("G", lambda: g.iota(T.cwi[:, 0:16], [[1, 16]], 128, -1), "", "cwi", 160)
     iota(A("tm"), [[1, 144]], -16, -1, "tm", 144)
     iota(T.r8[0:8, :], [[1, 8], [0, 16]], 0, -1, "r8", 128)
-    iota(A("iq"), [[16, 12]], 0, 0, "iq", 12)
     iota(A("ib"), [[613, V], [16 * 37, 13]], 0, 0, "ib", 78)
-    iota(A("IOT"), [[1, 3072]], -3072, 0, "IOT", 3072)
+    iota(A("IOT"), [[1, 3072]], -1536, 0, "IOT", 3072)
+    iota(A("jt"), [[0, 8], [1, 16]], 0, 0, "jt", 128)
+    ts(T.cols[:, 30:31], T.cwi[:, 0:1], -1.0, OP.mult, "cwi", "c_p", 144.0, OP.add)
+    ts(A("i2"), T.tm[:, 0:128], T.cols[:, 30:31], OP.add, "tm c_p", "i2", 2.0, OP.mult)
+    ms(A("zero"), 0.0, "zero")
+    for nm, by in (("CE", E), ("I3", 3072.0), ("I8", 8.0)):
+        op("G", lambda nm=nm, by=by: g.affine_select(A(nm), A("zero"), [[-1, 128]], OP.not_equal, by, 0, 1), "zero", nm, 440)
     ms(A("ones"), 1.0, "ones", 100)
     ms(T.X[:, 3072:CW], 0.0, "Xp")
+    ms(A("SD"), -BIG, "SD", 140)
     ts(T.cwi[:, 16:32], T.cwi[:, 0:16], 15, OP.bitwise_and, "cwi", "cwj")
     cp(A("cw"), T.cwi[:, 16:32], "cwj", "cw")
     ts(A("SC"), A("cw"), -1.0, OP.mult, "cw", "SC", 15.0, OP.add)
@@ -189,70 +283,92 @@ def rank_program(g, core, T, topo):
         act(A(nm) if out is None else out, I if src == "I" else A(src), AF.Identity, src + " " + home.get(by, ""), nm,
             scale=cols.get(by, by), c=140)
 
-    def less(nm, a, b, scale, bk):
-        mm(B[bk][:, 0:128], I, A(a), True, False, "I " + a, "bk%d" % bk, 70)
-        mm(B[bk][:, 0:128], A("NI"), A(b), False, True, "NI " + b, "bk%d" % bk, 70)
-        act(A(nm), B[bk][:, 0:128], AF.Identity, "bk%d" % bk, nm, scale=scale, c=140)
-
     eye(I, cols["s"], "I")
     eye(T.I[:, 128:256], cols["s"], "I2")
     ms(T.R8n[0:32, :], -8.0, "R8n")
     ts(T.R8n[0:8, :], T.r8[0:8, :], 0.0, OP.is_equal, "r8", "R8n", -8.0, OP.mult, c=140)
-    ts(A("W1"), A("raw"), 0.0, OP.is_equal, "raw", "W1")
+    ts(A("S8"), T.raw[:, 16:144:16], 0.0, OP.is_equal, "raw", "S8", -8.0, OP.mult)
+    act(T.RL[:, 0:12], T.I[:, 0:12], AF.Copy, "I", "RL0", c=70)
+    tt(T.RL[:, 12:24], T.I[:, 12:24], T.I[:, 24:36], OP.add, "I", "RL1", 70)
     R8 = T.R8n[0:8, :]
     mm(B[7][:, 0:128], R8, R8, True, True, "R8n", "bk7", 70)
     act(A("BA"), B[7][:, 0:128], AF.Identity, "bk7", "BA", scale=1.0 / 64, c=140)
     for nm, src, a, b in (("cr", "s", 8192.0, 4096.0), ("ic", "e15", 3840.0, 256.0), ("ip", "e15", -240.0, 256.0),
                           ("ci", "e15", 1.875, -2.0), ("pi", "e15", -15.0, 16.0), ("kc", "e0", -NH - 1.0, 1.0),
-                          ("pk", "e0", -135168.0, 4096.0), ("cp", "s", 4096.0, 2048.0 * 65), ("cq", "s", 4096.0, 2048.0 * 63),
-                          ("zc", "s", -1.0, 128.0), ("s37", "s", 37.0, 0.0)):
+                          ("pk", "e0", -135168.0, 4096.0), ("cp", "s", 4096.0, 2048.0 * 65 + WE), ("cq", "s", 4096.0, 2048.0 * 63 + WE),
+                          ("s37", "s", 37.0, 0.0), ("ib", "ic", -3071.0, 0.0), ("n2", "n15", 2.0, 0.0)):
         col(nm, src, a, b)
-    cols["w"], home["w"] = T.cols[:, 15:16], "c_w"
-    ts(cols["w"], A("wti"), 1.0 / 32, OP.mult, "wti", "c_w")
+    cols["w"], home["w"] = T.cols[:, 31:32], "c_w"
+    ts(cols["w"], A("wti"), 0.5, OP.mult, "wti", "c_w")
     eye(A("Sh"), T.SC[:, 0:1], "Sh", "n0")
-    eye(A("tA"), cols["s"], "tA", "n15")
-    eye(A("tB"), T.SC[:, 14:15], "tB", "n15")
-    for w in range(1, 4):
-        eye(T.RA[:, 128 * w - 128:128 * w], T.SC[:, 15 - w:16 - w], "RA%d" % w)
-    for h in range(4):
-        eye(T.RW[:, 128 * h:128 * h + 128], T.cw[:, 14 - 4 * h:15 - 4 * h], "RW%d" % h)
-    ts(A("M8"), T.raw[:, 16:144:16], 0.0, OP.is_equal, "raw", "M8")
-    for nm, src, by in (("CR", "I", "cr"), ("NI", "I", -1.0), ("NB", "BA", -8.0), ("WN", "W1", -8.0), ("W2", "W1", 16.0),
-                        ("Ipen", "I", "ip"), ("C15", "I", "e15"), ("CE15", "C15", E), ("CE", "I", E), ("Ww", "W1", "w"),
-                        ("CI", "I", "ci"), ("PI", "BA", "pi"), ("PK", "BA", "pk"), ("I3", "I", 3072.0),
-                        ("CP", "I", "cp"), ("I5", "I", -0.5), ("I75", "I", -0.75)):
+    eye(A("tB"), T.SC[:, 14:15], "tB", "n2")
+    for nm, by in (("M8", -0.125), ("M8f", -0.125), ("S16", -2.0), ("SL", -1.0 / 2048)):
+        act(A(nm), A("S8"), AF.Identity, "S8", nm, scale=by, c=70)
+    c = T.cols
+    ts(c[:, 20:21], cols["s"], 9.0, OP.is_ge, "SC", "c_sg")
+    cols.update(sg=c[:, 20:21], fh=c[:, 21:22], og=c[:, 22:23], al=c[:, 23:24])
+    home.update(sg="c_sg", fh="c_fh", og="c_og", al="c_al")
+    for j, (nm, src, a, b) in enumerate((("sh", "s", 0.5, 0.0), ("o1", "sg", -4.0, 1024.0), ("be", "sg", 0.25, -0.125))):
+        cols[nm], home[nm] = c[:, 24 + j:25 + j], "c_" + nm
+        act(cols[nm], cols[src], AF.Identity, home[src], home[nm], bias=b, scale=a, c=70)
+    ts(cols["fh"], cols["sg"], -4.0, OP.mult, "c_sg c_sh", "c_fh", cols["sh"], OP.add)
+    ts(cols["og"], cols["fh"], 28.0, OP.mult, "c_fh c_o1", "c_og", cols["o1"], OP.add)
+    act(c[:, 27:28], cols["fh"], AF.Identity, "c_fh", "c_nf", scale=-1.0, c=70)
+    ts(c[:, 28:29], cols["e0"], T.E0[:, 8:9], OP.add, "E0", "c_a0", -1.0 / 16, OP.mult)
+    act(cols["al"], c[:, 28:29], AF.Identity, "c_a0", "c_al", bias=0.125, c=70)
+    ts(T.TI[:, 0:64], T.i2[:, 0:64], c[:, 27:28], OP.mult, "i2 c_nf c_og", "TI0", cols["og"], OP.add)
+    for j, (o, a, b, by, k) in enumerate(((64, 0, 9, "sh", 0), (73, 1, 8, "sh", 4), (80, 0, 9, "sh", 4), (89, 1, 8, "sh", 0),
+                                          (96, 0, 16, "fh", 0), (112, 0, 16, "fh", 4))):
+        ts(T.TI[:, o:o + b - a], T.i2[:, a:b], cols[by], OP.mult, "i2 " + home[by], "TI%d" % (j + 1), 1024.0 - k, OP.add)
+    ts(A("TI"), A("TI"), 15, OP.bitwise_and, "TI0 TI1 TI2 TI3 TI4 TI5 TI6", "TI", c=140)
+    act(A("ta"), A("TI"), AF.Abs, "TI", "ta", bias=-8.0, c=140)
+    act(A("tb"), A("ta"), AF.Identity, "ta", "tb", bias=-4.0, c=140)
+    act(A("tw"), A("tb"), AF.Square, "tb", "tw", c=140)
+    act(A("tq"), A("tw"), AF.Square, "tw", "tq", bias=-SINE[2], c=140)
+    act(A("ta"), A("tw"), AF.Identity, "tw", "ta", bias=-SINE[1], c=140)
+    act(A("tw"), A("tq"), AF.Identity, "tq", "tw", bias=SINE[0] * SINE[3], scale=SINE[0], c=140)
+    tt(A("tq"), A("ta"), A("tb"), OP.mult, "ta tb", "tq", 270)
+    tt(A("TAB"), A("tq"), A("tw"), OP.mult, "tq tw", "TAB", 270)
+    act(T.FH[:, 0:32], T.TAB[:, 64:96], AF.Copy, "TAB", "FH0", c=70)
+    tt(T.FH[:, 32:64], T.TAB[:, 64:96], T.FH[:, 0:32], OP.subtract, "TAB FH0", "FH1", 70)
+    for j, by in enumerate(("al", "be")):
+        act(T.ta[:, 16 * j:16 * j + 16], T.TAB[:, 96 + 16 * j:112 + 16 * j], AF.Identity, "TAB tq " + home[by], "ta%d" % j,
+            scale=cols[by], c=70)
+    for j in range(8):
+        act(T.FE[:, :, 16 * j:16 * j + 16], A("FH"), AF.Identity, "FH0 FH1 M8f", "FE%d" % j, scale=T.M8f[:, j:j + 1], c=70)
+        act(T.ME[:, :, 16 * j:16 * j + 16], T.ta[:, 0:32], AF.Identity, "ta0 ta1 M8f", "ME%d" % j, scale=T.M8f[:, j:j + 1], c=70)
+    FE, ME = (" ".join(nm + str(j) for j in range(8)) for nm in ("FE", "ME"))
+    for nm, src, by in (("CR", "I", "cr"), ("NB", "BA", -8.0), ("tC", "BA", "e0"),
+                        ("Ipen", "I", "ip"), ("C15", "I", "e15"), ("CE15", "C15", E), ("BAw", "BA", "w"),
+                        ("CI", "I", "ci"), ("PI", "BA", "pi"), ("PK", "BA", "pk"), ("BAk", "BA", "kc"), ("I5", "I", -0.5), ("I12", "I", -12288.0),
+                        ("I75", "I", -0.75)):
         scaled(nm, src, by)
-    ts(A("M15"), A("BA"), cols["e15"], OP.mult, "BA E0", "M15", -1.0 / 4096, OP.mult)
-    ts(A("tC"), A("BA"), 2.0 ** -12, OP.mult, "BA", "tC")
-    ts(A("ShN"), A("Sh"), -512.0, OP.mult, "Sh", "ShN")
-    ts(A("B16"), A("BA"), 16.0, OP.mult, "BA", "B16")
-    tt(A("PH"), A("B16"), A("ShN"), OP.add, "B16 ShN", "PH", 270)
-    tt(A("HQ"), A("Sh"), A("C15"), OP.add, "Sh C15", "HQ", 270)
-    less("SI", "Sh", "tA", 1.0, 6)
-    less("Moh", "tA", "tB", 1.0 / 256, 7)
-    ts(A("tB"), I, -512.0, OP.mult, "I", "tB")
-    tt(A("tA"), A("B16"), A("tB"), OP.add, "B16 tB", "tA", 270)
+    ts(A("MF"), A("BA"), cols["e15"], OP.mult, "BA E0", "MF", -1.0, OP.mult)
+    scaled("ShN", "Sh", -512.0)
+    scaled("B16", "BA", 16.0)
+
+    def both(out, nm, a, b, r):
+        mm(B[7][:, 0:128], I, a, True, False, "I " + r, "bk7", 70)
+        mm(B[7][:, 0:128], I, b, False, True, "I " + r, "bk7", 70)
+        act(out, B[7][:, 0:128], AF.Copy, "bk7", nm, c=140)
+    mm(B[6][:, 0:128], I, A("CI"), True, False, "I CI", "bk6", 70)
+    mm(B[6][:, 0:128], I, A("tB"), False, False, "I tB", "bk6", 70)
+    mm(B[6][:, 0:128], A("I5"), A("MF"), False, True, "I5 MF", "bk6", 70)
+    act(A("Mx"), B[6][:, 0:128], AF.Identity, "bk6", "Mx", scale=8.0, c=140)
+    op("G", lambda: g.affine_select(A("tA"), A("B16"), [[-1, 128]], OP.not_equal, -496.0, 0, 1), "B16", "tA", 440)
     for h in range(2):
-        scaled("BH%d" % h, "BA", 8192.0, out=T.BH[:, 128 * h:128 * h + 128])
-    mm(B[1][:, 0:128], R8, R8, True, False, "R8n", "bk1", 70)
-    mm(B[1][:, 0:128], R8, R8, False, False, "R8n", "bk1", 70)
-    mm(B[1][:, 0:128], A("NI"), rw, False, True, "NI raw", "bk1", 70)
-    act(T.oyh[:, 0:128], B[1][:, 0:128], AF.Copy, "bk1", "oyh", c=140)
-    ts(A("TUi"), T.oyh[:, 0:128], cols["zc"], OP.is_ge, "oyh c_zc", "TUi", c=140)
-    ts(T.TUr[:, 0:128], T.oyh[:, 0:128], cols["zc"], OP.is_gt, "oyh c_zc", "TUr0", -8192.0, OP.mult, c=140)
-    cp(T.TUr[:, 128:256], T.TUr[:, 0:128], "TUr0", "TUr1")
-    tt(A("MC"), A("tC"), T.TUr[:, 0:128], OP.add, "tC TUr0", "MC", 270)
-    ts(A("bi"), A("iq"), cols["s"], OP.add, "iq SC", "bi")
-    ts(A("bz"), A("bi"), 7.5 / 16, OP.add, "bi", "bz")
-    ts(A("KB"), A("bi"), 16.0, OP.mult, "bi", "KB", float(NH), OP.add)
-    ms(T.LB[:, 0:24], 0.0, "LB0")
-    cp(T.LB[:, 24:36], A("bi"), "bi", "LB1")
-    ms(T.kap[:, 0:12], 0.5, "kap0")
-    ms(T.kap[:, 12:14], 4.0, "kap1")
+        scaled("BH%d" % h, "tC", 8192.0, out=T.BH[:, 128 * h:128 * h + 128])
+        scaled("TUr%d" % h, "Sh", -8192.0, out=T.TUr[:, 128 * h:128 * h + 128])
+    act(T.kap[:, 0:12], T.ones[:, 0:12], AF.Identity, "ones", "kap0", scale=0.5, c=70)
+    act(T.kap[:, 12:14], T.ones[:, 0:2], AF.Identity, "ones", "kap1", scale=4.0, c=70)
     ts(T.abi[:, 0:78], A("ib"), cols["s37"], OP.add, "ib c_s37", "abi", c=80)
     ts(T.abi[:, 78:156], T.abi[:, 0:78], 2047, OP.bitwise_and, "abi", "abj", c=80)
     ts(A("AB"), T.abi[:, 78:156], -1023.5, OP.add, "abj", "AB", c=80)
     ms(T.AB[:, 12:78:13], -1023.5, "AB")
+    ts(A("MK"), A("jt"), cols["s"], OP.not_equal, "jt SC", "MK", -60000.0, OP.mult)
+    act(A("ZM"), A("MK"), AF.Identity, "MK", "ZM", bias=-7.5 / 8, c=140)
+    act(T.cols[:, 29:30], cols["s"], AF.Identity, "SC", "c_s16", bias=7.5, scale=16.0, c=70)
+    act(A("bz"), T.i2[:, 0:128:16], AF.Identity, "i2 c_s16", "bz", bias=T.cols[:, 29:30], scale=8.0, c=70)
 
     def masked(j, src, b, out):
         ts(T.nmh[0:8, NP * j:NP * j + NP], T.nmi[:, NP * j:NP * j + NP], 1024.0, OP.mult, "nmi%d" % j, "nmh%d" % j, c=200)
@@ -260,47 +376,56 @@ def rank_program(g, core, T, topo):
         mm(L(b), A("CR"), A("ones"), False, True, "CR ones", "bk%d" % b)
         tt(A(out), L(b), A(src), OP.max, "bk%d %s" % (b, src), out)
 
-    def front():
-        act(T.D1[:, 2:36:3], B[5][:, 256:268], AF.Identity, "bk5", "D1c", bias=E + OFF, c=70)
-        act(T.D0[:, 2:36:3], B[5][:, 256:268], AF.Identity, "bk5", "D0c", bias=16384.0 * (E - 0.5), scale=-16384.0, c=70)
+    def front(by):
+        act(T.D1[:, 2:36:3], B[7][:, 448:460], AF.Identity, "bk7", "D1c", bias=E + OFF, scale=by, c=70)
+        act(T.D0[:, 2:36:3], B[7][:, 448:460], AF.Identity, "bk7", "D0c", bias=16384.0 * (E - 0.5), scale=-16384.0 * by, c=70)
 
     def choose(now):
         now("scan")
         op("V", lambda: g.vector.tensor_tensor_scan(A("cf"), A("D0"), T.D1[:, 0:36], 0.0, OP.max, OP.min),
            "D0a D0b D0c D1a D1b D1c", "cf", 70)
         now("cl")
-        ts(A("cl"), T.cf[:, 2:36:3], -OFF, OP.add, "cf", "cl")
+        lin(ON["cl"] if at[0] else "V", A("cl"), T.cf[:, 2:36:3], 1.0, 0.25 - OFF, "cf", "cl", 12)
         now("crep")
+        at[0] = at[0] or (0, "first")
         act(A("crep"), A("IOT").indirect(A("cl")), AF.Copy, "IOT cl", "crep", c=G192)
 
-    def hand_flags(now):
+    def hand_flags(now, on):
         now("hinv")
-        ts(HINV, A("Hp"), E, OP.is_ge, "Hp", "hinv", 256.0, OP.mult, c=100)
+        if on["hinv"] == "A":
+            act(HINV, A("Hp"), AF.Relu, "Hp", "hinv", bias=256.0 * (1 - E), scale=256.0)
+        else:
+            ts(HINV, A("Hp"), E - 0.5, OP.is_ge, "Hp", "hinv", 256.0, OP.mult, c=100)
         now("hfr")
-        ts(HFR, A("Hp"), cols["e0"], OP.mult, "Hp E0", "hfr", c=100)
+        lin(on["hfr"], HFR, A("Hp"), cols["e0"], 0.0, "Hp E0", "hfr", NP)
 
     masked(0, "tri", 5, "fst")
-    ts(A("TT0"), A("fst"), 3072.0, OP.min, "fst", "TT0", c=200)
+    ts(T.TT[:, 0:NP], A("fst"), 3072.0, OP.min, "fst", "TTA0 TTB0", c=200)
     masked(1, "hai", 4, "RR")
     ts(A("Hs"), A("RR"), 3072.0, OP.min, "RR", "Hs", -E, OP.add, c=200)
     ts(A("Wk"), A("raw"), 0.0, OP.is_equal, "raw E0", "Wk", cols["e0"], OP.mult)
-    diag(B[5][:, 256:268], "Wk", "Hs", NP, "Hs", "bk5", first=True)
-    scaled("Wk", "W1", "kc")
+    diag(B[7][:, 448:460], "Wk", "Hs", NP, "Hs", "bk7", first=True)
     at[0] = (-1, "crep")
-    front()
+    front(1.0)
     at[0] = None
     ms(T.D0[:, 0:36:3], BIG, "D0a")
     ms(T.D0[:, 1:36:3], -BIG, "D0b")
     ms(T.D1[:, 1:36:3], BIG, "D1b")
     ts(T.D1[:, 0:39:3], T.AB[:, 0:13], 4096.0, OP.add, "AB", "D1a")
     choose(len)
+    at[0] = None
     ms(T.nmh[0:32, 2 * NP:3 * NP], 2040.0 - (OFF - 0.5) / 8, "nmh2", 100)
     ts(T.nmh[0:8, 2 * NP:3 * NP], T.nmi[:, 2 * NP:3 * NP], -2040.0, OP.add, "nmi2", "nmh2", c=200)
     mm(L(3), A("Sh"), A("Hs"), True, False, "Sh Hs", "bk3")
     mm(L(3), A("CE15"), A("ones"), False, True, "CE15 ones", "bk3")
     cp(A("Hp"), L(3), "bk3", "Hp", 200)
-    hand_flags(len)
-    scaled("CR", "I", "cq")
+    hand_flags(len, ON)
+    mm(B[7][:, 0:128], I, A("MK"), True, False, "I MK", "bk7", 70)
+    mm(B[7][:, 0:128], I, A("i2"), False, True, "I i2", "bk7", 70)
+    act(A("KM"), B[7][:, 0:128], AF.Identity, "bk7", "KM", bias=NH / 8.0, c=140)
+    both(A("MC"), "MC", A("tC"), T.TUr[:, 0:128], "tC TUr0")
+    both(A("PH"), "PH", A("B16"), A("ShN"), "B16 ShN")
+    both(A("HQ"), "HQ", A("Sh"), A("C15"), "Sh C15")
 
     def inside(lo, hi, parts=None):
         return [j for j, p in enumerate(parts or PIECES) if lo <= p[0] < hi]
@@ -308,20 +433,32 @@ def rank_program(g, core, T, topo):
     def xts(lo, hi):
         return " ".join("XT%d" % j for j in inside(lo, hi))
 
-    def cards(nm, j, b, out, to, length):
-        ts(T.VL[:, NP * j:NP * j + NP], A(nm), E, OP.is_lt, nm, "VL%d" % j, c=100)
+    def xt(p):
+        return 16 * p if p < SP else XB + 16 * (p - SP)
+
+    def cards(nm, r, j, b, out, to, length):
+        ts(T.VL[:, NP * j:NP * j + NP], A(nm), E - 0.5, OP.is_lt, r, "VL%d" % j, c=100)
         mm(B[b][0:8, NP:2 * NP], A("M8"), T.VL[:, NP * j:NP * j + NP], True, True, "M8 VL%d" % j, "bk%d" % b)
-        mm(L(b), I, A(nm), True, False, "I " + nm, "bk%d" % b)
+        mm(L(b), I, A(nm), True, False, "I " + r, "bk%d" % b)
         mm(L(b), A("I3"), T.VL[:, NP * j:NP * j + NP], False, True, "I3 VL%d" % j, "bk%d" % b)
-        act(A(out), L(b), AF.Identity, "bk%d" % b, out, bias=-E)
+        if j:
+            ts(A(out), L(b), R1 - E, OP.add, "bk%d" % b, out, -R1, OP.add, c=200)
+        else:
+            act(A(out), L(b), AF.Identity, "bk%d" % b, out, bias=-E)
         act(T.omn[:, NP * j:NP * j + NP], B[b][0:8, NP:2 * NP], AF.Copy, "bk%d" % b, "omn%d" % j)
         dma("S", "o" + to[1], T[to][:, :], A(out), out, "", 96)
         dma("S", "o" + length[1], T[length][:, :], T.omn[:, NP * j:NP * j + NP], "omn%d" % j, "", 6)
 
+    nxt = T.cores[(rank + 1) % len(T.cores)]
+    rid, pid = topo.addr(nxt, core)
+    mask = 0
+    for e in send_engines(topo, core, nxt):
+        mask |= 1 << e
+
     for t in range(V):
         last = t == V - 1
-        tn = "TT%d" % t
-        tab = T[tn]
+        tn = "TTA%d TTB%d" % (t, t)
+        tab = T.TT[:, NP * t:NP * t + NP]
         jj = 0 if last else (2 if t == 3 else 1)
         ro = 128 - 16 * jj
 
@@ -331,229 +468,229 @@ def rank_program(g, core, T, topo):
         def rot(nm):
             return T[nm][:, ro:ro + 128] if jj else T[nm][:, 0:128]
 
-        def turn(mats, src, win, step):
-            for w in range(4):
-                now(win + "ab"[w // 2])
-                o = B[6 + w // 2][:, 256 * (w % 2):256 * (w % 2) + NP]
-                mm(o, mats[w][0], A(src), True, True, mats[w][1] + " " + src, "bk%d" % (6 + w // 2))
-            for w in range(4):
-                now(win + "ab"[w // 2])
-                o = B[6 + w // 2][:, 256 * (w % 2):256 * (w % 2) + NP]
-                act(T[win][:, step * w:step * w + NP], o, AF.Copy, "bk%d" % (6 + w // 2), "%s%d" % (win, w))
-
-        if last:
-            at[0] = None
-            ts(T.bz[:, 6:12], T.bi[:, 6:12], 7.5 / 16 - 96, OP.add, "bi", "bz")
         now("xc")
-        cp(A("xc"), A("X").indirect(A("cl")), "X Xp cl", "xc", G192)
+        cp(A("xc"), A("X").indirect(A("cl")), "XA XB Xp cl", "xc", G192)
         for j, (p, n, q) in enumerate(PIECES):
             now("g%d" % j)
-            out, src = T.XT[:, 16 * p:16 * (p + n)], A("X").indirect(tab[:, p:p + n])
+            out, src = T.XT[:, xt(p):xt(p) + 16 * n], A("X").indirect(T.TT[:, NP * t + p:NP * t + p + n])
+            r = "XA XB Xp TT%s%d" % ("AB"[p >= SP], t)
             if q == "A":
-                act(out, src, AF.Copy, "X Xp " + tn, "XT%d" % j, c=60 + GATHER * 16 * n)
+                act(out, src, AF.Copy, r, "XT%d" % j, c=60 + GATHER * 16 * n)
             else:
-                cp(out, src, "X Xp " + tn, "XT%d" % j, 60 + GATHER * 16 * n)
+                cp(out, src, r, "XT%d" % j, 60 + GATHER * 16 * n)
         now("xh")
-        act(A("xh"), A("xc"), AF.Identity, "xc", "xh", bias=2079.5)
-        now("Th")
-        ts(A("Th"), A(tn), -E, OP.add, tn, "Th", c=100)
-        now("inv")
-        ts(INV, A(tn), 3072.0, OP.is_ge, tn + " c_ic", "inv", cols["ic"], OP.mult, c=100)
-        now("LB")
-        mm(B[5][:, 256:292], I, A("LB"), True, False, "I LB0 LB1", "bk5", 34)
-        diag(B[5][:, 256:292], "W1", "DG", 3 * NP, "inv hinv hfr", "bk5")
+        lin(ON["xh"], A("xh"), A("xc"), 1.0, 2079.5, "xc", "xh", NP)
+        for nm, lo, hi, b in PARTS:
+            n, c2, bk, tn = hi - lo, (hi - lo) // 2 + 3, "bk%d" % (3 + 2 * b), "TT%s%d" % (nm, t)
+            tab, th, inv, crep = T.TT[:, NP * t + lo:NP * t + hi], T.Th[:, lo:hi], T.DG[:, 2 * NP + lo:2 * NP + hi], T.crep[:, lo:hi]
+            p3, p2 = B[3 + 2 * b][:, 0:n], B[3 + 2 * b][:, 128:128 + n]
+            now("Th" + nm)
+            lin(ON["Th"], th, tab, 1.0, -E, tn, "Th" + nm, n)
+            now("inv" + nm)
+            if ON["inv"] == "A":
+                act(inv, tab, AF.Relu, tn + " c_ic c_ib", "inv" + nm, bias=cols["ib"], scale=cols["ic"], c=n + 5)
+            else:
+                ts(inv, tab, 3072.0, OP.is_ge, tn + " c_ic", "inv" + nm, cols["ic"], OP.mult)
+            now("Tp" + nm)
+            mm(p3, A("I12"), T.ones[:, 0:n], True, False, "I12 ones", bk, c2)
+            mm(p2, A("C15"), crep, False, False, "C15 crep", bk, c2)
+            mm(p3, I, crep, False, False, "I crep", bk, c2)
+            now("Tapp" + nm)
+            mm(p3, A("Mx"), inv, False, False, "Mx inv" + nm, bk, c2)
+            mm(p2, A("MF"), inv, False, False, "MF inv" + nm, bk, c2)
+            mm(p2, A("Sh"), th, False, True, "Sh Th" + nm, bk, c2)
+            now("Q" + nm)
+            tt(T.Q[:, lo:hi], p3, th, OP.min, bk + " Th" + nm, "Q" + nm, n + 5)
+            now("Tapp" + nm)
+            tt(T.Tapp[:, lo:hi], p2, T.Q[:, lo:hi], OP.max, bk + " Q" + nm, "Tapp" + nm, n + 5)
+            now("Trot" + nm)
+            mm(B[6][:, lo:hi], rot("I"), th, True, True, "I I2 Th" + nm, "bk6", c2)
+            act(T.Trot[:, lo:hi], B[6][:, lo:hi], AF.Identity, "bk6", "Trot" + nm, bias=0.0 if last else E, c=n + 5)
+        for j in range(16):
+            now("LB" + "ab"[j // 8])
+            mm(B[7][0:36, 256 + j:384:16], T.DG[:, j:3 * NP:16], A("SL"), j == 0, j == 15, "SL invA invB hinv hfr", "bk7", 20)
         now("x1")
-        ts(A("x1"), B[5][:, 268:280], 3840.0 if last else 0.0, OP.add, "bk5", "x1")
-        now("x2")
-        tt(T.xi[:, 0:12], B[5][:, 280:292], A("x1"), OP.add, "bk5 x1", "x2", 70)
-        now("x3")
-        ts(T.xi[:, 12:24], T.xi[:, 0:12], 1023, OP.bitwise_and, "x2", "x3")
-        now("x4")
-        ts(T.xi[:, 24:36], T.xi[:, 0:12], 3072 + 255, OP.bitwise_and, "x2", "x4")
+        act(T.LT[0:36, :], B[7][0:36, 256:384], AF.Copy, "bk7", "LT", c=140)
+        now("LT")
+        mm(B[7][:, 448:472], T.LT[0:36, :], T.RL[0:36, :], True, True, "LT RL0 RL1", "bk7", 34)
         now("ql")
-        cp(A("ql"), T.xi[:, 12:36], "x3 x4", "ql")
+        lin(ON["ql"], A("ql"), B[7][:, 460:472], 1.0, 15.0 if last else 0.0, "bk7", "ql", 12)
         if not last:
             now("front")
-            front()
-        now("ff")
-        mm(L(3), A("M15"), INV, True, True, "M15 inv", "bk3")
-        now("oh")
-        mm(H(3), A("Moh"), INV, True, False, "Moh inv", "bk3")
-        mm(H(3), A("C15"), A("ones"), False, True, "C15 ones", "bk3")
-        now("fT")
-        tt(A("fT"), L(3), A("Th"), OP.mult, "bk3 Th", "fT")
-        now("ohc")
-        tt(A("ohc"), H(3), A("crep"), OP.mult, "bk3 crep", "ohc")
-        now("pt0")
-        mm(L(4), A("Sh"), A("Th"), True, False, "Sh Th", "bk4")
-        mm(L(4), A("CE15"), A("ones"), False, False, "CE15 ones", "bk4")
-        now("SI")
-        mm(L(4), A("SI"), A("fT"), False, True, "SI fT", "bk4")
-        now("Tapp")
-        tt(A("Tapp"), L(4), A("ohc"), OP.add, "bk4 ohc", "Tapp")
-        now("Trot")
-        mm(H(3), rot("I"), A("Th"), True, True, "I I2 Th", "bk3")
-        now("CE")
-        mm(L(3), A("CE"), A("ones"), True, False, "CE ones", "bk3")
-        now("Trot")
-        act(A("Trot"), H(3), AF.Copy, "bk3", "Trot")
-        turn([(I, "I")] + [(T.RA[:, 128 * w:128 * w + 128], "RA%d" % (w + 1)) for w in range(3)], "Tapp", "WINA", 256)
-        now("Tg")
-        cp(A("Tg"), A("WINA").indirect(T.ql[:, 0:12]), "WINA0 WINA1 WINA2 WINA3 ql", "Tg", G192)
-        turn([(T.RW[:, 128 * h:128 * h + 128], "RW%d" % h) for h in range(4)], "Tg", "WIN", 1024)
-        now("Rv")
-        act(A("Rv"), A("WIN").indirect(T.ql[:, 12:24]), AF.Copy, "WIN0 WIN1 WIN2 WIN3 ql", "Rv", c=G192)
+            front(256.0)
+        for j in range(4):
+            now("F" + "ab"[j // 2])
+            mm(B[6][:, NP * (j % 2):NP * (j % 2) + NP], T.FE[:, j, :], A("Tapp"), j == 0, j == 3, FE + " TappA TappB", "bk6")
+        now("Gt")
+        act(A("Gt"), T.TAB[:, 0:64].indirect(A("ql")), AF.Copy, "TAB ql", "Gt", c=G192)
+        for j in range(2):
+            now("U%d" % j)
+            tt(T.U[:, NP * j:NP * j + NP], B[6][:, NP * j:NP * j + NP], A("Gt"), OP.mult, "bk6 Gt", "U%d" % j)
 
         def opening(b, lo, hi, nm):
-            o, c, bk = B[b][:, 0:hi - lo], (hi - lo) // 2 + 3, "bk%d" % b
+            o, c, bk = B[b][0:hi - lo, 0:128], 67, "bk%d" % b
             now("thr" + nm)
-            mm(o, T.R8n[0:9, :], T.nmh[0:9, 2 * NP + lo:2 * NP + hi], True, False, "R8n nmh2", bk, c)
+            mm(o, T.nmh[0:9, 2 * NP + lo:2 * NP + hi], T.R8n[0:9, :], True, False, "R8n nmh2", bk, c)
             now("NB" + nm)
-            mm(o, A("NB"), T.xc[:, lo:hi], False, False, "NB xc", bk + "+", c)
+            mm(o, T.xc[:, lo:hi], A("NB"), False, False, "NB xc", bk + "+", c)
             now("Ipen" + nm)
-            mm(o, A("Ipen"), T.DG[:, 2 * NP + lo:2 * NP + hi], False, False, "Ipen inv", bk + "+", c)
+            mm(o, T.DG[:, 2 * NP + lo:2 * NP + hi], A("Ipen"), False, False, "Ipen inv" + nm, bk + "+", c)
 
-        opening(0, 0, 128, "")
-        for b, p, n, r in ((1, 0, 128, 2), (2, 128, 64, 4)):
+        now("SD")
+        act(T.SD[:, 0:128:16], T.ones[:, 0:8], AF.Identity, "ones D1a", "SD", bias=3.5, scale=T.D1[:, 36:37], c=70)
+
+        opening(4, 0, SP, "A")
+        for b, p, n, r in ((1, 0, SP, REP[0]), (2, SP, NP - SP, REP[1])):
             now("four%d" % b)
             for s in range(r):
-                mm(B[b][:, s:r * n:r], I, T.xc[:, p:p + n], True, True, "I xc", "bk%d" % b, n // 2 + 2)
+                mm(R(b, 0, r * n, s, r), I, T.xc[:, p:p + n], True, True, "I xc", "bk%d" % b, n // 2 + 2)
         for j, (p, n) in enumerate(MAXES):
-            b, r = (1, 2) if p < 128 else (2, 4)
-            o, st = r * (p % 128), 16 // r
+            b, r = (1, REP[0]) if p < SP else (2, REP[1])
+            o, st = r * (p - SP * (b - 1)), 16 // r
             for s in range(st):
                 now("m%d_%d" % (j, s % 4))
-                tt(T.MX[:, 16 * p + s:16 * (p + n):st], B[b][:, o:o + r * n], T.XT[:, 16 * p + s:16 * (p + n):st], OP.max,
+                tt(T.MX[:, 16 * p + s:16 * (p + n):st], R(b, o, o + r * n), T.XT[:, xt(p) + s:xt(p) + 16 * n:st], OP.max,
                    "bk%d " % b + xts(p, p + n), "MX%d_%d" % (j, s), max(70, r * n + 10))
-        for c in range(3):
-            b = c // 2
-            o, bk = B[b][:, 64 * (c % 2):64 * (c % 2) + 64], "bk%d" % b
+        for b in range(2):
+            bk, D = "bk%d" % (4, 1)[b], B[(4, 1)[b]]
             if b:
-                opening(1, 128, NP, "B")
-            now("sx%d" % c)
-            for s in range(16):
-                mm(o, T.WN[:, 16 - s:144 - s], T.XT[:, 1024 * c + s:1024 * c + 1024:16], False, False,
-                   "WN " + xts(64 * c, 64 * c + 64), bk + "+", 34)
-            for k in range(16):
-                now("sm%d" % c + "ab"[k // 8])
-                s = k // 4 + 4 * (k % 4)
-                end = c > 0 and k == 15
-                mm(o, T.W2[:, 16 - s:144 - s], T.MX[:, 1024 * c + s:1024 * c + 1024:16], False, end,
-                   "W2 " + " ".join("MX%d_%d" % (j, s % (4 if b else 8)) for j in inside(64 * c, 64 * c + 64, MAXES)), bk if end else bk + "+", 34)
-        now("d0c")
-        mm(L(4), A("I75"), A("xc"), True, False, "I75 xc", "bk4")
-        for nm, lo, hi in (("d0a", 0, 128), ("d0b", 128, NP)):
-            now(nm)
-            mm(B[4][:, lo:hi], A("I5"), T.XT[:, 16 * lo:16 * hi:16], False, False, "I5 " + xts(lo, hi), "bk4", (hi - lo) // 2 + 3)
-            mm(B[4][:, lo:hi], I, T.MX[:, 16 * lo:16 * hi:16], False, hi == NP,
-               "I " + " ".join("MX%d_0" % j for j in inside(lo, hi, MAXES)), "bk4", (hi - lo) // 2 + 3)
-        now("N0")
-        act(T.XT[:, NH:NH + 3072:16], L(4), AF.Identity, "bk4", "N0", bias=0.5, scale=4.0)
+                opening(1, SP, NP, "B")
+            for c, (p, n) in enumerate(SX):
+                for s in range(16 * (c == b)):
+                    now("sx%d" % c + "abcd"[s // 4])
+                    mm(D[0:n, s:128:16], T.XT[:, xt(p) + s:xt(p) + 16 * n:16], A("S8"), False, False,
+                       "S8 " + xts(p, p + n), bk + "+", 34)
+            for c, (p, n) in enumerate(SM):
+                for k in range(16 * (c == b)):
+                    now("sm%d" % c + "abcd"[k // 4])
+                    s = k // 4 + 4 * (k % 4)
+                    end = k == 15
+                    mm(D[0:n, s:128:16], T.MX[:, 16 * p + s:16 * (p + n):16], A("S16"), False, end,
+                       "S16 " + " ".join("MX%d_%d" % (j, s % (16 // REP[b])) for j in inside(p, p + n, MAXES)),
+                       bk if end else bk + "+", 34)
 
-        for b, lo, hi, nm in ((0, 0, 128, "A"), (1, 128, NP, "")):
-            n, bk = hi - lo, "bk%d" % b
+        for nm, lo, hi, b in PARTS:
+            n, bk, c2, pb = hi - lo, "bk%d" % (2 * b), (hi - lo) // 2 + 3, 2 * b
+            x0, q0, q1 = xt(lo), lo // 16, hi // 16
             now("ok" + nm)
-            act(T.ok[:, lo:hi], B[b][:, 0:n], AF.Relu, bk + " D1a", "ok" + nm, bias=T.D1[:, 36:37], scale=-1.0, c=n + 5)
+            op("V", lambda n=n, b=b: g.vector.tensor_tensor_scan(T["SQ" + "AB"[b]][0:n, 127::-1], T.SD[0:n, :], B[(4, 1)[b]][0:n, 127::-1],
+                                                                 0.0, OP.max, OP.min), "bk%d SD" % (4, 1)[b], "ok" + nm, 140)
+            now("d0" + nm)
+            o, bo = R(4 * b, 384, 384 + n), "bk%d" % (4 * b)
+            mm(o, A("I75"), T.xc[:, lo:hi], True, False, "I75 xc", bo, c2)
+            mm(o, A("I5"), T.XT[:, x0:x0 + 16 * n:16], False, False, "I5 " + xts(lo, hi), bo, c2)
+            mm(o, I, T.MX[:, 16 * lo:16 * hi:16], False, True, "I " + " ".join("MX%d_0" % j for j in inside(lo, hi, MAXES)), bo, c2)
+            now("N0" + nm)
+            act(T.XT[:, x0 + NH:x0 + NH + 16 * n:16], o, AF.Identity, bo, "N0" + nm, bias=0.5, scale=4.0, c=n + 5)
             now("tri" + nm)
-            mm(B[b][:, 128:128 + n], A("TUi"), T.ok[:, lo:hi], True, True, "TUi ok" + nm, bk, n // 2 + 3)
+            mm(R(pb, 128, 128 + n), T["SQ" + nm][0:n, :], T.I[0:n, 0:n], True, True, "I ok" + nm, bk, c2)
             now("K1" + nm)
-            act(T.K1[:, lo:hi], B[b][:, 128:128 + n], AF.Sign, bk, "K1" + nm, c=n + 5)
-        if not last:
-            now("CI")
-            mm(L(2), A("CI"), INV, True, False, "CI inv", "bk2")
-            now("cap")
-            mm(L(2), A("MC"), A("ok"), False, True, "MC ok okA", "bk2")
-            act(A("cap"), L(2), AF.Sign, "bk2", "cap acc", bias=-2.0 ** -14, acc=T.acc[:, 0:1], c=220)
-        kp = B[0][:, 256:268]
-        now("kb")
-        mm(kp, I, A("KB"), True, False, "I KB", "bk0", 34)
-        now("kd")
-        diag(kp, "Wk", "K1", NP, "K1 K1A", "bk0")
-        now("kl")
-        cp(A("kl"), kp, "bk0", "kl")
-        now("pt")
-        mm(L(5), rot("I"), A("Tapp"), True, False, "I I2 Tapp", "bk5")
-        now("ramp")
-        mm(L(3), rot("TUr"), A("ok"), False, True, "TUr0 TUr1 ok okA", "bk3")
-        now("BH")
-        mm(L(5), rot("BH"), A("ok"), False, True, "BH0 BH1 ok okA", "bk5")
-        now("fst")
-        tt(A("fst"), L(3), A("Trot"), OP.max, "bk3 Trot", "fst")
-        now("Tc")
-        tt(A("Tc"), L(5), A("fst"), OP.min, "bk5 fst", "Tc")
-        if not last:
-            to = T["TO%d" % t]
-            nxt = T.cores[(rank + 1) % len(T.cores)]
-            now("to")
-            ts(to[:, :], A("Tc"), E, OP.add, "Tc", "TO%d" % t, c=100)
-            rid, pid = topo.addr(nxt, core)
-            mask = 0
-            for e in send_engines(topo, core, nxt):
-                mask |= 1 << e
-            op("G", lambda to=to, t=t, rid=rid, pid=pid, mask=mask: g.remote_dma(
-                T["TT%d" % (t + 1)][:, :], to[:, :], T.sem["arr%d" % (t + 1)], T.sem.snd, pid, rid, mask),
-               "TO%d" % t, "sent%d" % t, REMOTE * (2 if t == 0 else 1), dma="snd")
-            op("R", None, "sent%d" % t, "TT%d" % (t + 1), 0, dma="arr%d" % (t + 1))
-        else:
-            now("yt")
-            cards("Tc", 0, 3, "oyt", "yt", "yn")
-        now("u")
-        tt(A("u"), A("XT").indirect(A("kl")), A("xh"), OP.add, xts(0, NP) + " N0 kl xh", "u", G192)
-        pz = B[2][:, 256:268]
-        now("zd")
-        diag(pz, "Ww", "u", NP, "u", "bk2", first=True)
-        now("y")
-        ts(A("y"), A("u"), -2080.0, OP.add, "u", "y", 0.5, OP.mult, c=100)
-        now("zf")
-        tt(A("zf"), pz, A("bz"), OP.subtract, "bk2 bz", "zf", 70)
-        now("zt")
-        tt(A("zt"), pz, A("zf"), OP.subtract, "bk2 zf", "zt", 70)
-        now("zl")
-        ts(A("zl"), A("zt"), 16.0, OP.mult, "zt", "zl")
-        now("X")
+            act(T.K1[:, lo:hi], R(pb, 128, 128 + n), AF.Sign, bk + " SD", "K1" + nm, bias=T.SD[:, 0:1], scale=-1.0, c=n + 5)
+            now("k" + nm)
+            mm(R(pb, 256, 256 + n), A("I8"), T.KM[:, 0:n], True, False, "I8 KM", bk, c2)
+            mm(R(pb, 256, 256 + n), A("BAk"), T.K1[:, lo:hi], False, True, "BAk K1" + nm, bk, c2)
+            pick(T.kl[:, q0:q1], R(pb, 256, 256 + n), bk, "kl" + nm, n + 5)
+            br = bp = (3, 1)[b]
+            pr, pp = B[br][:, NP + lo:NP + hi], B[bp][:, lo:hi]
+            now("CE" + nm)
+            mm(pr, A("CE" if last else "I3"), T.ones[:, 0:n], True, False, "CE I3 ones", "bk%d" % br, c2)
+            now("pt" + nm)
+            mm(pp, rot("I"), T.Tapp[:, lo:hi], False, False, "I I2 Tapp" + nm, "bk%d" % bp, c2)
+            if not last:
+                mm(pp, A("CE"), T.ones[:, 0:n], False, False, "CE ones", "bk%d" % bp, c2)
+            now("ramp" + nm)
+            mm(pr, rot("TUr"), T.K1[:, lo:hi], False, False, "TUr0 TUr1 K1" + nm, "bk%d" % br, c2)
+            now("BH" + nm)
+            mm(pp, rot("BH"), T.K1[:, lo:hi], False, True, "BH0 BH1 K1" + nm, "bk%d" % bp, c2)
+            now("fst" + nm)
+            tt(T.fst[:, lo:hi], pr, T.Trot[:, lo:hi], OP.max, "bk%d Trot%s fst" % (br, nm), "fst" + nm, n + 5)
+            now("Tc" + nm)
+            if last:
+                tt(T.Tc[:, lo:hi], pp, T.fst[:, lo:hi], OP.min, "bk%d fst%s" % (bp, nm), "Tc" + nm, n + 5)
+            else:
+                to, there, arr = T.TO[:, NP * t + lo:NP * t + hi], T.TT[:, NP * (t + 1) + lo:NP * (t + 1) + hi], "arr%s%d" % (nm, t + 1)
+                tt(to, pp, T.fst[:, lo:hi], OP.min, "bk%d fst%s" % (bp, nm), "TO" + arr, n + 5)
+                op("G", lambda to=to, there=there, arr=arr: g.remote_dma(there, to, T.sem[arr], T.sem.snd, pid, rid, mask),
+                   "TO" + arr, "sent" + arr, REMOTE * (2 if t == 0 and b == 0 else 1), dma="snd")
+                op("R", None, "sent" + arr, "TT%s%d" % (nm, t + 1), 0, dma=arr)
+            now("u" + nm)
+            tt(T.u[:, lo:hi], T.XT[:, x0:x0 + NH + 16 * n].indirect(T.kl[:, q0:q1]), T.xh[:, lo:hi], OP.add,
+               xts(lo, hi) + " N0%s kl%s xh" % (nm, nm), "u" + nm, 60 + GATHER * n)
+            z0 = 384 * b
+            k = ZR[b]
+            now("zc" + nm)
+            mm(R(pb, z0, z0 + n), A("I8"), T.ZM[:, 0:n], True, False, "I8 ZM", bk, c2)
+            now("z" + nm)
+            for h in range(k):
+                mm(R(pb, z0 + h * n, z0 + h * n + n), A("BAw"), T.u[:, lo:hi], False, h == k - 1, "BAw u" + nm, bk, c2)
+            now("y" + nm)
+            lin(ON["y"], T.y[:, lo:hi], T.u[:, lo:hi], 0.5, -1040.0, "u" + nm, "y" + nm, n)
+            now("zr" + nm)
+            pick(T.zr[:, 2 * q0:2 * q0 + k * (q1 - q0)], R(pb, z0, z0 + k * n), bk, "zr" + nm, k * n + 5)
+            if k == 1:
+                now("zt" + nm)
+                tt(T.zr[:, q0 + q1:2 * q1], T.zr[:, 2 * q0:q0 + q1], T.bz[:, 0:q1 - q0], OP.add, "bz zr" + nm, "zt" + nm, 70)
+            now("zf" + nm)
+            ts(T.zf[:, q0:q1], T.zr[:, 2 * q0:q0 + q1], R16, OP.add, "zr" + nm, "zf" + nm, -R16, OP.add)
+            now("zl" + nm)
+            tt(T.zl[:, q0:q1], T.zr[:, q0 + q1:2 * q1], T.zf[:, q0:q1], OP.subtract, "zr%s zf%s zt%s" % (nm, nm, nm), "zl" + nm, 70)
+            now("X" + nm)
+            cp(T.X[:, 16 * lo:16 * hi].indirect(T.zl[:, q0:q1]), T.y[:, lo:hi], "y%s zl%s" % (nm, nm), "X" + nm, 50 + SCATTER * n)
         if last:
-            for h in range(2):
-                now("X")
-                cp(T.X[:, 1536 * h:1536 * h + 1536].indirect(T.zl[:, 6 * h:6 * h + 6]), T.y[:, 96 * h:96 * h + 96],
-                   "y zl X", "X%d" % h, 50 + SCATTER * 96)
+            now("yt")
+            cards("Tc", "TcA TcB", 0, 3, "oyt", "yt", "yn")
         else:
-            cp(A("X").indirect(A("zl")), A("y"), "y zl Xp", "X", 50 + SCATTER * NP)
-        if not last:
+            now("CI")
+            mm(L(3), A("CI"), INV, True, False, "CI invA invB", "bk3")
+            now("cap")
+            mm(L(3), A("MC"), A("K1"), False, True, "MC K1A K1B", "bk3")
+            act(A("cap"), L(3), AF.Sign, "bk3", "cap acc", bias=-0.5, acc=T.acc[:, 0:1], c=220)
             now("D1b")
-            tt(T.D1[:, 1:36:3], kp, T.cf[:, 2:36:3], OP.max, "bk0 cf", "D1b", 70)
+            tt(T.D1[:, 1:36:3], A("kl"), T.cf[:, 2:36:3], OP.max, "klA klB cf", "D1b", 70)
             now("D0b")
-            act(T.D0[:, 1:36:3], kp, AF.Identity, "bk0", "D0b", bias=NH + 3071.0, scale=-1.0, c=70)
+            lin(ON["D0b"], T.D0[:, 1:36:3], A("kl"), -1.0, NH + 3071.0, "klA klB", "D0b", 12)
             now("rA")
             act(T.rA[:, 0:13], T.kap[:, 0:13], AF.Identity, "kap0 kap1 acc", "rA", scale=T.acc[:, 0:1], c=70)
-            pa = B[1][:, 400:413]
+            pa = B[3][:, 400:413]
             now("pa")
-            mm(pa, I, T.AB[:, 13 * t + 13:13 * t + 26], True, False, "I AB", "bk1", 34)
-            mm(pa, T.ones[:, 0:128], T.rA[:, 0:13], False, True, "ones rA", "bk1", 34)
+            mm(pa, I, T.AB[:, 13 * t + 13:13 * t + 26], True, False, "I AB", "bk3", 34)
+            mm(pa, T.ones[:, 0:128], T.rA[:, 0:13], False, True, "ones rA", "bk3", 34)
             now("rr")
-            ts(T.rr[:, 0:13], pa, R2K, OP.add, "bk1", "rr", -R2K - 4096, OP.add)
+            ts(T.rr[:, 0:13], pa, R2K, OP.add, "bk3", "rr", -R2K - 4096, OP.add)
             now("D1a")
-            tt(T.D1[:, 0:39:3], pa, T.rr[:, 0:13], OP.subtract, "bk1 rr", "D1a", 70)
+            tt(T.D1[:, 0:39:3], pa, T.rr[:, 0:13], OP.subtract, "bk3 rr", "D1a", 70)
             choose(now)
         now("pen")
         mm(H(5), I if last else A("HQ"), A("Hp"), True, True, "I HQ Hp", "bk5")
-        ph, cst = ("tA", "CR") if last else ("PH", "CP")
+        ph, cst = ("tA", "cq") if last else ("PH", "cp")
         mm(L(5), A(ph), HINV, True, False, ph + " hinv", "bk5")
-        mm(L(5), A(cst), A("ones"), False, False, cst + " ones", "bk5")
-        mm(L(5), A("PI"), INV, False, False, "PI inv", "bk5")
+        mm(L(5), A("PI"), INV, False, False, "PI invA invB", "bk5")
         now("PK")
-        mm(L(5), A("PK"), A("K1"), False, True, "PK K1 K1A", "bk5")
-        now("RR")
-        tt(A("RR"), L(5), A("Rv"), OP.max, "bk5 Rv", "RR")
-        now("Hp")
-        tt(A("Hp"), H(5), A("RR"), OP.min, "bk5 RR", "Hp")
+        mm(L(5), A("PK"), A("K1"), False, True, "PK K1A K1B", "bk5")
+        for j in range(2):
+            now("Rv%d" % j)
+            mm(L(7), T.ME[:, j, :], T.U[:, NP * j:NP * j + NP], j == 0, j == 1 and ON["RR"] == "V", ME + " U%d" % j, "bk7", 400)
+        now("wall")
+        if ON["RR"] == "V":
+            act(A("wall"), L(5), AF.Identity, "bk5 c_" + cst, "wall", bias=cols[cst])
+            now("RR")
+            tt(A("RR"), L(7), A("wall"), OP.max, "bk7 wall", "RR")
+            now("Hp")
+            tt(A("Hp"), H(5), A("RR"), OP.min, "bk5 RR", "Hp")
+        else:
+            act(A("wall"), L(5), AF.Relu, "bk5 c_" + cst, "wall", bias=cols[cst], scale=1.0)
+            mm(L(7), I, A("wall"), False, True, "I wall", "bk7")
+            now("RR")
+            act(A("RR"), H(5), AF.Copy, "bk5", "RR")
+            now("Hp")
+            tt(A("Hp"), L(7), A("RR"), OP.min, "bk7 RR", "Hp")
         if not last:
-            hand_flags(now)
+            hand_flags(now, ON)
         else:
             now("yh")
-            cards("Hp", 1, 1, "oyh", "yh", "ym")
-    at[0] = None
-    for h in range(2):
-        dma("SA"[h], "ox%d" % h, T.yx[:, 1536 * h:1536 * h + 1536], T.X[:, 1536 * h:1536 * h + 1536], "X%d" % h, "", 384)
+            cards("Hp", "Hp", 1, 6, "oyh", "yh", "ym")
+    for nm, lo, hi, b in PARTS:
+        dma("S", "ox" + nm, T.yx[:, 16 * lo:16 * hi], T.X[:, 16 * lo:16 * hi], "X" + nm, "", 4 * (hi - lo))
 
     emit(g, core, T, topo, plan(ops), rank)
 
@@ -563,15 +700,18 @@ def plan(ops):
     hold = [60 if o["dma"] else o["c"] for o in ops]
     for q, names in ORDER.items():
         place = {nm.rstrip("-+"): ((nm[-1] == "-") - (nm[-1] == "+"), i) for i, nm in enumerate(names.split())}
+        place["first"] = (0, 0)
         key = {k: (o["at"][0] + place[o["at"][1]][0], place[o["at"][1]][1]) for k, o in enumerate(ops) if o["q"] == q and o["at"]}
         for k in key:
+            if key[k][0] >= V - 1:
+                key[k] = (V - 1, LAST[q].split().index(ops[k]["at"][1] + "-" * (ops[k]["at"][0] < V - 1)))
             if ops[k]["at"] in LATER:
                 key[k] = (ops[k]["at"][0], place[LATER[ops[k]["at"]][q]][1] + 0.5)
         mine = sorted(key, key=lambda k: (key[k], k))
         for a, b in zip(mine, mine[1:]):
             ops[b]["order"].add(a)
     for q in "GS":
-        mine = [k for k, o in enumerate(ops) if o["q"] == q]
+        mine = [k for k, o in enumerate(ops) if o["q"] == q and (q == "G" or not o["deps"])]
         for a, b in zip(mine, mine[1:]):
             ops[b]["order"].add(a)
     succ = [[] for _ in ops]

from concourse.mybir import AluOpType, ActivationFunctionType, AxisListType

OP = AluOpType
AF = ActivationFunctionType
V = 6
NP = 192
CW = 3088
E = 1536.0
NH = 8192
XB = 10240
OFF = 3072.5
R2K = 1.5 * 2 ** 34
R16 = 1.5 * 2 ** 27
R1 = 1.5 * 2 ** 23
BIG = 30000.0
SINE = (-2.679189617679568e-07, 62.462959736501446, 113.70776756960623, 10536.242908533108)
SP = 96
PARTS = (("A", 0, SP, 0), ("B", SP, NP, 1))
PIECES = ((0, 48, "A"), (48, 48, "V"), (96, 56, "A"), (152, 40, "A"))
MAXES = ((0, 96), (96, 56), (152, 40))
ON = {"inv": "V", "cl": "A", "ql": "A", "hinv": "A", "Th": "V", "y": "A", "x1": "A", "RR": "A", "hfr": "A", "D0b": "A", "xh": "A"}
WE = E if ON["RR"] == "A" else 0.0
REP = (2, 2)
ZR = (1, 1)
SX = SM = ((0, SP), (SP, NP - SP))
WAKE, DMA, REMOTE, GATHER, SCATTER = 200, 1700, 2000, 1.6, 4.0


def _m(*pieces):
    return "".join("m%d_%d " % (j, s) for s in range(4) for j in pieces)


ORDER = {
    "V": "xc g1 Q m0_0 m0_1 Tapp m0_3 m0_2 m1_0 m1_2 m1_1 m1_3 Hp- m2_2 m2_1 m2_0 m2_3 fstA kA TcA uA fstB TcB kB zrA uB D1b zfA rr ql zlA D1a zrB XA scan zfB U0 cl zlB U1 XB inv+ yt yh",
    "A": "g0 g2 g3 xh hfr- okA hinv- Trot K1A N0A okB N0B K1B yA cap rA D0b x1 yB front Gt wall RR crep Th+ yt yh",
    "P": "Tc Tapp IpenA four1 Rv1- Trot wall- four2 NBA sx0 sm0a sm0b CEA sx1 ptA sm0c d0A sm0d sm1c sm1a sm1b thrB sm1d sx2 triA BHA sm2c sm2b rampA sm2a kA IpenB NBB sm2d d0B CI ptB zcA triB BHB CEB rampB cap zA kB LB pa zcB thrA+ zB pen F PK Rv0 yt yh",
}
LAST = {
    "V": "xc g1 Q m0_0 m0_1 Tapp m0_3 m0_2 m1_0 m1_2 m1_1 m1_3 Hp- m2_2 m2_1 m2_0 m2_3 kA uA fstA TcA ql kB zrA uB zfA fstB zlA TcB XA zrB U0 zfB U1 zlB yt XB Hp yh",
    "A": "g0 g2 g3 xh hfr- okA hinv- Trot K1A N0A okB N0B x1 K1B yA Gt yB wall RR yt yh",
    "P": "Tc Tapp IpenA four1 Rv1- Trot wall- four2 NBA sx0 sm0a sm0b CEA sx1 ptA sm0c d0A sm0d sm1c sm1a sm1b thrB sm1d sx2 triA BHA sm2c sm2b rampA sm2a kA IpenB NBB sm2d d0B LB ptB zcA triB BHB CEB rampB zA kB F zcB zB pen PK Rv0 Rv1 wall yt yh",
}
ORDER = {
    "V": "xc U1- g1 inv m0_2 m0_3 m0_1 m1_0 m1_1 m0_0 m1_3 m1_2 Q Hp- Tapp m2_2 m2_0 m2_1 m2_3 fstA TcA kA uA fstB kB TcB uB zrA D1b rr zfA ql zrB zlA D1a zfB XA scan zlB cl XB U0 yt yh",
    "A": "g0 g2 Th g3 Trot xh okA hinv- hfr- N0A K1A okB N0B K1B cap yA rA D0b yB x1 front Gt RR wall crep yt yh",
    "P": "Tc NBA Rv0- Rv1- four2 four1 wall- sx0 sm0c IpenA sm0d sx1 sm0b Tapp sm1b d0A Trot sm1a sm0a sm1c thrB NBB sm1d sx2 CEA triA rampA IpenB sm2c ptA BHA sm2a sm2b sm2d kA d0B ptB triB BHB CI cap CEB rampB zcA kB zA LB pa zcB zB F pen thrA+ PK yt yh",
}
LAST = {
    "V": "xc U1- g1 inv m0_3 m0_2 m0_1 m1_1 m1_3 m1_2 m1_0 m0_0 Q Hp- m2_0 m2_1 m2_2 m2_3 Tapp kA ql fstA uA kB TcA uB U0 zrA fstB zrB zfA U1 zfB zlA TcB zlB XA yt Hp XB yh",
    "A": "g0 g2 Th g3 xh N0A hfr- hinv- Trot okA K1A okB x1 K1B N0B Gt yA wall RR yB yt yh",
    "P": "Rv0- four2 Rv1- wall- NBA four1 Tc sx0 sm0d sx1 IpenA Tapp sm0c sm0b sm1c d0A thrB sm0a sm1a NBB Trot sm1b sm1d sx2 sm2a sm2b sm2c triA IpenB sm2d LB kA triB ptB CEA rampA ptA BHA d0B kB zcA F CEB zA zcB rampB zB BHB pen PK Rv0 Rv1 wall yt yh",
}
ORDER = {
    "V": "xc g1 m0_1 m0_3 m0_2 inv m1_0 m0_0 Hp- m1_1 m1_2 m1_3 Q Tapp m2_1 m2_0 m2_2 m2_3 kA fstA uA TcA zrA kB ztA zfA uB zlA D1b rr ql XA zrB D1a zfB ztB scan fstB zlB cl TcB U0 XB U1 yt yh",
    "A": "g2 Th g3 xh N0A hfr- hinv- okA Trot K1A okB N0B K1B yA cap rA D0b x1 yB front Gt wall crep RR g0+ yt yh",
    "P": "Rv1- Tc four1 wall- NBA four2 sx0 sm0b sm0d sx1 Tapp sm0a d0A sm0c sm1a IpenA Trot sm1b sm1c sm1d thrB sx2 IpenB CEA ptA triA sm2a sm2c sm2b kA NBB rampA sm2d d0B BHA zcA triB CI cap zA kB LB pa F zcB zB pen ptB CEB rampB PK BHB thrA+ Rv0 yt yh",
}
LAST = {
    "V": "xc g1 m0_1 m0_3 m0_2 inv m1_0 m0_0 Hp- m1_1 m1_2 m1_3 Q Tapp m2_1 m2_0 m2_2 m2_3 kA fstA uA TcA zrA kB ztA zfA uB zlA ql XA zrB zfB ztB fstB zlB TcB U0 XB U1 yt Hp yh",
    "A": "g2 Th g3 xh N0A hfr- hinv- okA Trot K1A okB N0B K1B yA x1 yB Gt wall RR yt yh",
    "P": "Rv1- Tc four1 wall- NBA four2 sx0 sm0b sm0d sx1 Tapp sm0a d0A sm0c sm1a IpenA Trot sm1b sm1c sm1d thrB sx2 IpenB CEA ptA triA sm2a sm2c sm2b kA NBB rampA sm2d d0B BHA zcA triB zA kB LB F zcB zB pen ptB CEB rampB PK BHB Rv0 Rv1 wall yt yh",
}
ORDER = {
    "V": "xc g1 invA U1- m0_3 m0_1 m0_0 QA m0_2 m1_0 m1_1 m1_2 m1_3 TappA Hp- invB okA m2_2 m2_1 m2_0 m2_3 kA uA okB QB fstA TappB TcA zrA ztA zfA kB zlA uB XA ql D1b zrB rr ztB D1a zfB fstB scan zlB TcB cl XB U0 yt yh",
    "A": "g0 ThA g2 g3 N0A ThB hinv- xh K1A hfr- TrotA yA K1B N0B TrotB cap x1 D0b rA yB wall RR front Gt SD+ crep yt yh",
    "P": "Rv0- four1 TpA NBA four2 TappA Rv1- IpenA TrotA wall- sx0d sx0a sx0c sm0a sx0b d0A sm0b sm0c sm0d thrB CEA NBB IpenB sx1a triA sx1d sx1b sx1c TpB kA sm1b sm1c sm1a sm1d TappB rampA ptA BHA zcA zA triB d0B CI LBa TrotB kB cap LBb pen PK ptB LT thrA+ zcB zB pa BHB Fa CEB rampB Fb yt yh",
}
LAST = {
    "V": "U1- xc g1 invA Hp- m0_1 m0_0 m0_2 m1_0 m1_1 m1_2 m1_3 m0_3 invB m2_0 okA m2_1 QB m2_2 m2_3 TappB QA TappA kA okB uA fstA ql zrA TcA kB fstB ztA zfA uB zlA U0 U1 zrB XA ztB zfB TcB zlB yt Hp XB yh",
    "A": "g0 ThA g2 g3 ThB hfr- xh N0A TrotA K1A hinv- x1 TrotB N0B K1B yA Gt wall yB RR yt yh",
    "P": "Rv0- Rv1- four1 wall- IpenA TpA TpB NBA TrotA TappA four2 sx0a d0A sx0b sx0d sm0a sm0b sx0c sm0c sm0d thrB TappB NBB IpenB sx1b sx1d sm1a triA sx1c sx1a d0B sm1b sm1c kA sm1d TrotB LBa LBb zcA CEA triB ptA rampA BHA ptB LT zA Fa kB CEB rampB BHB Fb pen zcB zB PK Rv0 Rv1 wall yt yh",
}
ORDER = {
    "V": "xc g1 invA U1- m0_3 m0_1 m0_0 QA m0_2 m1_0 m1_1 m1_2 m1_3 TappA Hp- invB okA m2_2 m2_1 m2_0 m2_3 kA uA okB QB fstA TappB TcA zrA ztA zfA kB zlA uB XA ql D1b zrB rr ztB D1a zfB fstB scan zlB TcB cl XB U0 yt yh",
    "A": "g0 ThA g2 g3 ThB hinv- xh K1A N0A hfr- TrotA yA K1B N0B TrotB cap x1 D0b rA yB wall RR front Gt SD+ crep yt yh",
    "P": "Rv0- four1 TpA NBA four2 TappA Rv1- IpenA TrotA wall- sx0d sx0a sx0c sm0a sx0b sm0b sm0c sm0d thrB CEA NBB IpenB sx1a triA d0A sx1d sx1b sx1c TpB kA sm1b sm1c sm1a sm1d TappB rampA ptA BHA zcA zA triB d0B CI LBa TrotB kB cap LBb pen PK ptB LT zcB zB pa BHB Fa CEB rampB Fb thrA+ yt yh",
}
LAST = {
    "V": "xc g1 U1- invA m0_3 m0_2 m0_0 invB m0_1 m1_1 m1_0 m1_2 m1_3 Hp- QA okA m2_1 QB m2_2 m2_0 TappB m2_3 TappA kA okB uA kB zrA ql fstA uB ztA TcA fstB zfA U0 zlA TcB zrB U1 ztB zfB XA zlB yt Hp XB yh",
    "A": "ThA g0 g2 ThB g3 hinv- xh TrotA K1A hfr- N0A N0B K1B x1 yA TrotB Gt yB wall RR yt yh",
    "P": "Rv0- TpA four1 Rv1- TappA TrotA NBA IpenA wall- four2 sx0d sx0c sm0b sx0a sm0a sx0b sm0c sm0d TpB thrB TappB NBB sx1c sx1a IpenB triA d0A sx1d sx1b sm1c sm1b sm1a kA sm1d LBa d0B ptA triB LBb CEA zcA kB zA TrotB CEB LT rampA ptB rampB BHB zcB BHA Fa Fb zB pen PK Rv0 Rv1 wall yt yh",
}
ORDER = {
    "V": "xc g1 invA U1- m0_2 m0_0 m0_1 QA m0_3 Hp- m1_0 m1_1 m1_2 m1_3 TappA invB okA m2_2 m2_0 m2_3 m2_1 fstA kA TcA uA okB QB TappB zrA zfA ztA kB zlA uB XA zrB fstB D1b rr ztB zfB TcB D1a zlB scan XB U0 yt yh",
    "A": "g0 g2 g3 N0A hfr- xh TrotA ThB K1A hinv- yA TrotB N0B K1B cap D0b rA x1 yB wall RR ql front Gt SD+ cl ThA+ crep yt yh",
    "P": "Rv0- four1 four2 TpA NBA TappA Rv1- IpenA wall- TrotA sx0b sx0a sx0d sx0c d0A sm0b sm0a sm0c sm0d ptA thrB sx1d triA sx1c CEA sx1b sm1c IpenB sm1a rampA kA NBB BHA sx1a sm1b sm1d TpB TappB d0B TrotB zcA zA triB CI LBa kB cap LBb pen PK zcB zB CEB rampB pa ptB LT BHB Fa Fb thrA+ yt yh",
}
ORDER = {
    "V": "invA U0- xc g1 U1- m0_2 m0_1 QA m0_0 m0_3 TappA invB m1_1 okA m1_2 m2_1 m2_2 m1_3 m2_0 m1_0 m2_3 Hp- fstA kA TcA okB uA QB TappB zrA kB zfA ztA uB fstB D1b zlA TcB zrB rr XA ztB zfB D1a zlB scan XB yt yh",
    "A": "SD cl- ThA crep- g0 g2 g3 N0A xh wall- ThB RR- K1A TrotA hinv- K1B N0B yA hfr- TrotB cap rA yB x1 ql front D0b Gt yt yh",
    "P": "thrA four1 PK- TpA IpenA Rv0- NBA TappA sx0a sx0b sx0c sx0d Rv1- four2 sm0c TrotA d0A sm0b sm0a sm0d CEA thrB NBB ptA IpenB sx1c triA sx1d sx1b sm1b wall- sx1a rampA BHA kA sm1c sm1a sm1d TpB zcA TappB triB d0B CI zA TrotB kB cap CEB ptB rampB BHB LBa zcB LBb zB pa LT Fa pen Fb yt yh",
}
LAST = {
    "V": "U1- U0- xc g1 invA invB m0_0 m0_1 m0_2 QA m0_3 m1_2 TappA m1_0 okA m2_2 m1_1 m2_1 m2_0 m1_3 m2_3 kA Hp- uA okB QB TappB zrA kB zfA uB ztA fstB fstA zlA TcA XA zrB U0 U1 zfB ztB TcB zlB yt XB Hp yh",
    "A": "SD cl- ThA crep- g0 g2 g3 TrotA wall- N0A RR- K1A ThB xh hinv- TrotB N0B hfr- K1B x1 yB yA ql Gt wall RR yt yh",
    "P": "Rv0- TrotA thrA four1 TpA Rv1- sx0a sx0d four2 sx0b PK- IpenA TappA sm0b d0A NBA sx0c sm0a sm0c thrB sm0d NBB IpenB CEA sx1c sx1a sx1b triA sm1c wall- sm1b kA sm1a sx1d sm1d d0B TrotB TpB TappB triB zcA CEB ptA rampA zA kB LBa LBb ptB rampB BHB BHA LT zcB Fa zB Fb pen PK Rv0 Rv1 wall yt yh",
}
ORDER = {
    "V": "U0- xc U1- g1 ThA ThB invA invB m0_0 m0_1 QA m0_2 TappA m0_3 m1_0 m1_1 okA m1_2 m2_2 m2_0 m2_1 m1_3 m2_3 fstA QB Hp- TcA okB kA TappB uA fstB kB TcB uB zrA D1b ztA zrB rr zfA zfB D1a ztB zlA scan zlB XA XB yt yh",
    "A": "SD wall- crep- RR- g0 g2 g3 N0A K1A xh TrotA hinv- K1B N0B TrotB hfr- yA cap D0b rA x1 yB front ql Gt cl yt yh",
    "P": "thrA Fb- four2 Rv0- four1 Rv1- TpB wall- NBA TpA sx0d sx0c TappB TappA d0A sm0a IpenA sx0b TrotA sx0a sm0b CEA ptA sm0c sm0d thrB NBB IpenB sx1a triA sx1b sx1c sx1d rampA BHA sm1a sm1b sm1c sm1d kA d0B CI triB CEB zcA TrotB ptB rampB BHB kB cap LBa zA LBb zcB zB pa LT pen PK Fa yt yh",
}
LAST = {
    "V": "U1- U0- xc g1 invA ThB ThA m0_0 m0_2 m0_1 m0_3 QA invB m1_1 TappA Hp- okA m1_0 m2_0 m2_1 m1_3 m2_2 m1_2 m2_3 QB kA TappB okB uA zrA fstA zfA ztA kB zlA uB XA zrB U0 ztB U1 zfB fstB zlB TcA TcB XB yt Hp yh",
    "A": "SD RR- wall- crep- g0 g2 g3 N0A hfr- hinv- K1A xh TrotA K1B x1 N0B TrotB yA ql Gt wall RR yB yt yh",
    "P": "Fb- Rv0- TpA Rv1- thrA four1 sx0a TappA sx0c four2 sx0d wall- sm0a sm0c d0A NBA TpB sm0b sx0b IpenA thrB sm0d IpenB TappB CEA ptA NBB TrotA sx1c sx1a triA sx1d sm1b sm1a rampA sx1b kA sm1c sm1d d0B LBa zcA triB LBb zA BHA CEB TrotB kB pen ptB LT rampB PK zcB Fa zB Fb BHB Rv0 Rv1 wall yt yh",
}
LATER = {(0, "first"): {"A": "g2"}, (0, "TpA"): {"P": "sm0d"}, (0, "TappA"): {"P": "sm0d", "V": "m1_2"}, (0, "QA"): {"V": "okA"},
         (0, "TpB"): {"P": "IpenB"}, (0, "TappB"): {"P": "IpenB", "V": "kA"}, (0, "CEA"): {"P": "IpenB"}, (0, "ptA"): {"P": "IpenB"}}

F16 = "Th:192 Q:192 Tapp:192 crep:192 Hs:192 Hp:192 u:192 DG:576 AB:78 nmh:576 Tc:192 VL:384 MK KM ZM LT SQA SQB FH:64"
B16 = ("raw:144 tm:144 I:256 BA NB S8:8 S16:8 SL:8 RL:24 Wk:144 TUr:256 BH:256 C15 CE15 CE CR R8n "
       "Ipen Sh MF Mx I12 I8 BAk BAw MC CI PI PK PH HQ I3 tA tB tC ShN B16 M8:8 jt i2 zero "
       "ones:192 xc:192 K1:192 y:192 I5 I75 cap:192 kap:14 rA:14 wall:192")
F32 = ("Trot:192 xh:192 fst:192 Gt:192 U:384 RR:192 oyt:192 oyh:192 cw:16 SC:16 E0:16 NE:16 cols:32 M8f:8 "
       "ib:78 D0:36 D1:40 cf:36 rr:14 zr:24 zf:12 bz:8 acc:2 r8 SD TAB ta tb tw tq")
SCRATCH = {
    "X": ("sbuf", [128, CW], "bfloat16"), "XT": ("sbuf", [128, XB + NH + 2048], "bfloat16"), "MX": ("sbuf", [128, 3072], "bfloat16"),
    "IOT": ("sbuf", [128, 3072], "float32"), "FE": ("sbuf", [128, 4, 128], "float16"), "ME": ("sbuf", [128, 2, 128], "float32"),
    "nmi": ("sbuf", [8, 576], "int32"), "omn": ("sbuf", [8, 2 * NP], "float32"),
    "tri": ("sbuf", [128, NP], "int32"), "hai": ("sbuf", [128, NP], "int32"), "wti": ("sbuf", [128, 1], "int32"),
    "cwi": ("sbuf", [128, 32], "int32"), "abi": ("sbuf", [128, 156], "int32"), "TI": ("sbuf", [128, 128], "int32"),
    "cl": ("sbuf", [128, 12], "uint16"), "kl": ("sbuf", [128, 12], "uint16"), "zl": ("sbuf", [128, 12], "uint16"),
    "ql": ("sbuf", [128, 12], "uint16"),
    "TO": ("sbuf", [128, NP * (V - 1)], "uint16"), "TT": ("sbuf", [128, NP * V], "uint16"),
}
for _names, _dt in ((F16, "float16"), (B16, "bfloat16"), (F32, "float32")):
    for _n in _names.split():
        _n, _w = (_n.split(":") + ["128"])[:2]
        SCRATCH[_n] = ("sbuf", [128, int(_w)], _dt)
for _i in range(8):
    SCRATCH["bk%d" % _i] = ("psum", [128, 32, 16] if _i in (0, 2) else [128, 512], "float32")

DMAS = ["dx", "dt", "dh", "dn", "dm", "dth", "dw", "oxA", "oxB", "oh", "ot", "om", "on"]
SEMAPHORES = (["qV", "qA", "qP", "qG", "snd"] + ["arr%s%d" % (p[0], i) for i in range(1, V) for p in PARTS]
              + ["d_" + n for n in DMAS])


def send_engines(topo, src, dst):
    e = topo.engines(src, dst)
    return e[::len(e) // 8]


def rank_program(g, core, T, topo):
    rank = T.rank_of(core)
    if rank is None:
        return
    ops = []
    writer, readers, bank, lastq = {}, {}, {}, {}
    at = [None]

    def op(q, f, r, w, c, dma=None):
        k = len(ops)
        r, w = r.split(), w.split()
        deps, order = set(), set()
        for n in r:
            if n[:2] != "bk":
                if n in writer:
                    deps.add(writer[n])
                readers.setdefault(n, []).append(k)
        for n in w:
            if n[:2] != "bk":
                if n in writer:
                    deps.add(writer[n])
                deps.update(i for i in readers.get(n, []) if i != k)
                writer[n] = k
                readers[n] = []
        for n in r + w:
            if n[-1] == "+":
                order.add(bank[n[:-1]]["P"][0])
                bank[n[:-1]]["P"].append(k)
            elif n[:2] == "bk":
                a = bank.setdefault(n, {})
                for q2 in a:
                    if q2 != q:
                        deps.update(a[q2])
                if q == "P" and q in a:
                    order.update(a[q])
                a[q] = a[q] + [k] if lastq.get(n) == q and q != "P" else [k]
                lastq[n] = q
        ops.append({"q": q, "f": f, "deps": deps, "order": order, "dma": dma, "c": c, "at": None if q == "S" else at[0]})

    def ts(out, in0, s1, o1, r, w, s2=None, o2=None, c=70):
        if o2 is None:
            op("V", lambda: g.vector.tensor_scalar(out, in0, s1, None, o1), r, w, c)
        else:
            op("V", lambda: g.vector.tensor_scalar(out, in0, s1, s2, o1, o2), r, w, c)

    def tt(out, a, b, o, r, w, c=200):
        op("V", lambda: g.vector.tensor_tensor(out, a, b, o), r, w, c)

    def cp(out, a, r, w, c=70):
        op("V", lambda: g.vector.tensor_copy(out, a), r, w, c)

    def pick(out, a, r, w, c):
        op("V", lambda: g.vector.tensor_reduce(out, a, AxisListType.X, OP.max), r, w, c)

    def act(out, a, fn, r, w, bias=0.0, scale=1.0, acc=None, c=200):
        op("A", lambda: g.scalar.activation(out, a, fn, bias=bias, scale=scale, accum_out=acc), r, w, c)

    def lin(q, out, a, scale, bias, r, w, c):
        if q == "A":
            act(out, a, AF.Identity, r, w, bias=bias, scale=scale, c=max(70, c))
        else:
            ts(out, a, scale, OP.mult, r, w, bias, OP.add, c=max(70, c // 2))

    def mm(out, l, rr, st, sp, r, w, c=100):
        op("P", lambda: g.tensor.matmul(out, l, rr, st, sp), r, w, c)

    def dma(q, name, out, in_, r, w, kb):
        e = {"S": g.sync, "A": g.scalar}[q]
        op(q, lambda: e.dma_start(out, in_), r, w, DMA + 3.5 * kb, dma="d_" + name)

    def ms(ap, v, w, c=70):
        op("V", lambda: g.vector.memset(ap, v), "", w, c)

    def iota(out, pat, base, cm, w, n):
        op("G", lambda: g.iota(out, pat, base, cm, allow_small_or_imprecise_dtypes=True), "", w, 130 + 2 * n)

    def diag(o, mat, src, hi, r, wb, first=False):
        for j in range(16):
            mm(o, T[mat][:, 16 - j:144 - j], T[src][:, j:hi:16], first and j == 0, j == 15, r + " " + mat, wb, 34)

    B = [T["bk%d" % i] for i in range(8)]

    def R(b, lo, hi, first=0, step=1):
        return B[b][:, lo // 16:hi // 16, first:16:step] if b in (0, 2) else B[b][:, lo + first:hi:step]

    def L(b):
        return R(b, 0, NP)

    def H(b):
        return R(b, NP, 2 * NP)

    def A(nm):
        return T[nm][:, :]

    HFR, HINV, INV = (T.DG[:, NP * j:NP * j + NP] for j in range(3))
    I = T.I[:, 0:128]
    G192 = 60 + GATHER * NP

    dma("S", "dn", T.nmi[:, 0:NP], T.nt[:, :], "", "nmi0", 6)
    dma("A", "dm", T.nmi[:, NP:2 * NP], T.mh[:, :], "", "nmi1", 6)
    dma("S", "dt", A("tri"), T.trains[:, :], "", "tri", 96)
    dma("A", "dh", A("hai"), T.hands[:, :], "", "hai", 96)
    dma("S", "dth", T.nmi[:, 2 * NP:3 * NP], T.th[:, :], "", "nmi2", 6)
    dma("S", "dx", T.X[:, 0:3072], T.x0[:, :], "", "XA XB", 960)
    dma("A", "dw", A("wti"), T.wt[:, :], "", "wti", 1)

    op("G", lambda: g.iota(T.cwi[:, 0:16], [[1, 16]], 128, -1), "", "cwi", 160)
    iota(A("tm"), [[1, 144]], -16, -1, "tm", 144)
    iota(T.r8[0:8, :], [[1, 8], [0, 16]], 0, -1, "r8", 128)
    iota(A("ib"), [[613, V], [16 * 37, 13]], 0, 0, "ib", 78)
    iota(A("IOT"), [[1, 3072]], -1536, 0, "IOT", 3072)
    iota(A("jt"), [[0, 8], [1, 16]], 0, 0, "jt", 128)
    ts(T.cols[:, 30:31], T.cwi[:, 0:1], -1.0, OP.mult, "cwi", "c_p", 144.0, OP.add)
    ts(A("i2"), T.tm[:, 0:128], T.cols[:, 30:31], OP.add, "tm c_p", "i2", 2.0, OP.mult)
    ms(A("zero"), 0.0, "zero")
    for nm, by in (("CE", E), ("I3", 3072.0), ("I8", 8.0)):
        op("G", lambda nm=nm, by=by: g.affine_select(A(nm), A("zero"), [[-1, 128]], OP.not_equal, by, 0, 1), "zero", nm, 440)
    ms(A("ones"), 1.0, "ones", 100)
    ms(T.X[:, 3072:CW], 0.0, "Xp")
    ms(A("SD"), -BIG, "SD", 140)
    ts(T.cwi[:, 16:32], T.cwi[:, 0:16], 15, OP.bitwise_and, "cwi", "cwj")
    cp(A("cw"), T.cwi[:, 16:32], "cwj", "cw")
    ts(A("SC"), A("cw"), -1.0, OP.mult, "cw", "SC", 15.0, OP.add)
    ts(A("E0"), A("cw"), 0.0, OP.is_equal, "cw", "E0")
    ts(A("NE"), A("cw"), 0.0, OP.not_equal, "cw", "NE")
    cols = {"s": T.SC[:, 15:16], "e0": T.E0[:, 0:1], "e15": T.E0[:, 15:16], "n0": T.NE[:, 0:1], "n15": T.NE[:, 15:16]}
    home = {"s": "SC", "e0": "E0", "e15": "E0", "n0": "NE", "n15": "NE"}

    def col(nm, src, a, b):
        cols[nm], home[nm] = T.cols[:, len(cols) - 5:len(cols) - 4], "c_" + nm
        act(cols[nm], cols[src], AF.Identity, home[src], home[nm], bias=b, scale=a, c=70)

    ts(A("raw"), A("tm"), cols["s"], OP.add, "tm SC", "raw")
    rw = T.raw[:, 16:144]

    def eye(out, where, nm, by=None):
        ts(out, rw, where, OP.is_equal, "raw cw SC " + home.get(by, ""), nm, cols.get(by), OP.mult if by else None)

    def scaled(nm, src, by, out=None):
        act(A(nm) if out is None else out, I if src == "I" else A(src), AF.Identity, src + " " + home.get(by, ""), nm,
            scale=cols.get(by, by), c=140)

    eye(I, cols["s"], "I")
    eye(T.I[:, 128:256], cols["s"], "I2")
    ms(T.R8n[0:32, :], -8.0, "R8n")
    ts(T.R8n[0:8, :], T.r8[0:8, :], 0.0, OP.is_equal, "r8", "R8n", -8.0, OP.mult, c=140)
    ts(A("S8"), T.raw[:, 16:144:16], 0.0, OP.is_equal, "raw", "S8", -8.0, OP.mult)
    act(T.RL[:, 0:12], T.I[:, 0:12], AF.Copy, "I", "RL0", c=70)
    tt(T.RL[:, 12:24], T.I[:, 12:24], T.I[:, 24:36], OP.add, "I", "RL1", 70)
    R8 = T.R8n[0:8, :]
    mm(B[7][:, 0:128], R8, R8, True, True, "R8n", "bk7", 70)
    act(A("BA"), B[7][:, 0:128], AF.Identity, "bk7", "BA", scale=1.0 / 64, c=140)
    for nm, src, a, b in (("cr", "s", 8192.0, 4096.0), ("ic", "e15", 3840.0, 256.0), ("ip", "e15", -240.0, 256.0),
                          ("ci", "e15", 1.875, -2.0), ("pi", "e15", -15.0, 16.0), ("kc", "e0", -NH - 1.0, 1.0),
                          ("pk", "e0", -135168.0, 4096.0), ("cp", "s", 4096.0, 2048.0 * 65 + WE), ("cq", "s", 4096.0, 2048.0 * 63 + WE),
                          ("s37", "s", 37.0, 0.0), ("ib", "ic", -3071.0, 0.0), ("n2", "n15", 2.0, 0.0)):
        col(nm, src, a, b)
    cols["w"], home["w"] = T.cols[:, 31:32], "c_w"
    ts(cols["w"], A("wti"), 0.5, OP.mult, "wti", "c_w")
    eye(A("Sh"), T.SC[:, 0:1], "Sh", "n0")
    eye(A("tB"), T.SC[:, 14:15], "tB", "n2")
    for nm, by in (("M8", -0.125), ("M8f", -0.125), ("S16", -2.0), ("SL", -1.0 / 2048)):
        act(A(nm), A("S8"), AF.Identity, "S8", nm, scale=by, c=70)
    c = T.cols
    ts(c[:, 20:21], cols["s"], 9.0, OP.is_ge, "SC", "c_sg")
    cols.update(sg=c[:, 20:21], fh=c[:, 21:22], og=c[:, 22:23], al=c[:, 23:24])
    home.update(sg="c_sg", fh="c_fh", og="c_og", al="c_al")
    for j, (nm, src, a, b) in enumerate((("sh", "s", 0.5, 0.0), ("o1", "sg", -4.0, 1024.0), ("be", "sg", 0.25, -0.125))):
        cols[nm], home[nm] = c[:, 24 + j:25 + j], "c_" + nm
        act(cols[nm], cols[src], AF.Identity, home[src], home[nm], bias=b, scale=a, c=70)
    ts(cols["fh"], cols["sg"], -4.0, OP.mult, "c_sg c_sh", "c_fh", cols["sh"], OP.add)
    ts(cols["og"], cols["fh"], 28.0, OP.mult, "c_fh c_o1", "c_og", cols["o1"], OP.add)
    act(c[:, 27:28], cols["fh"], AF.Identity, "c_fh", "c_nf", scale=-1.0, c=70)
    ts(c[:, 28:29], cols["e0"], T.E0[:, 8:9], OP.add, "E0", "c_a0", -1.0 / 16, OP.mult)
    act(cols["al"], c[:, 28:29], AF.Identity, "c_a0", "c_al", bias=0.125, c=70)
    ts(T.TI[:, 0:64], T.i2[:, 0:64], c[:, 27:28], OP.mult, "i2 c_nf c_og", "TI0", cols["og"], OP.add)
    for j, (o, a, b, by, k) in enumerate(((64, 0, 9, "sh", 0), (73, 1, 8, "sh", 4), (80, 0, 9, "sh", 4), (89, 1, 8, "sh", 0),
                                          (96, 0, 16, "fh", 0), (112, 0, 16, "fh", 4))):
        ts(T.TI[:, o:o + b - a], T.i2[:, a:b], cols[by], OP.mult, "i2 " + home[by], "TI%d" % (j + 1), 1024.0 - k, OP.add)
    ts(A("TI"), A("TI"), 15, OP.bitwise_and, "TI0 TI1 TI2 TI3 TI4 TI5 TI6", "TI", c=140)
    act(A("ta"), A("TI"), AF.Abs, "TI", "ta", bias=-8.0, c=140)
    act(A("tb"), A("ta"), AF.Identity, "ta", "tb", bias=-4.0, c=140)
    act(A("tw"), A("tb"), AF.Square, "tb", "tw", c=140)
    act(A("tq"), A("tw"), AF.Square, "tw", "tq", bias=-SINE[2], c=140)
    act(A("ta"), A("tw"), AF.Identity, "tw", "ta", bias=-SINE[1], c=140)
    act(A("tw"), A("tq"), AF.Identity, "tq", "tw", bias=SINE[0] * SINE[3], scale=SINE[0], c=140)
    tt(A("tq"), A("ta"), A("tb"), OP.mult, "ta tb", "tq", 270)
    tt(A("TAB"), A("tq"), A("tw"), OP.mult, "tq tw", "TAB", 270)
    act(T.FH[:, 0:32], T.TAB[:, 64:96], AF.Copy, "TAB", "FH0", c=70)
    tt(T.FH[:, 32:64], T.TAB[:, 64:96], T.FH[:, 0:32], OP.subtract, "TAB FH0", "FH1", 70)
    for j, by in enumerate(("al", "be")):
        act(T.ta[:, 16 * j:16 * j + 16], T.TAB[:, 96 + 16 * j:112 + 16 * j], AF.Identity, "TAB tq " + home[by], "ta%d" % j,
            scale=cols[by], c=70)
    for j in range(8):
        act(T.FE[:, :, 16 * j:16 * j + 16], A("FH"), AF.Identity, "FH0 FH1 M8f", "FE%d" % j, scale=T.M8f[:, j:j + 1], c=70)
        act(T.ME[:, :, 16 * j:16 * j + 16], T.ta[:, 0:32], AF.Identity, "ta0 ta1 M8f", "ME%d" % j, scale=T.M8f[:, j:j + 1], c=70)
    FE, ME = (" ".join(nm + str(j) for j in range(8)) for nm in ("FE", "ME"))
    for nm, src, by in (("CR", "I", "cr"), ("NB", "BA", -8.0), ("tC", "BA", "e0"),
                        ("Ipen", "I", "ip"), ("C15", "I", "e15"), ("CE15", "C15", E), ("BAw", "BA", "w"),
                        ("CI", "I", "ci"), ("PI", "BA", "pi"), ("PK", "BA", "pk"), ("BAk", "BA", "kc"), ("I5", "I", -0.5), ("I12", "I", -12288.0),
                        ("I75", "I", -0.75)):
        scaled(nm, src, by)
    ts(A("MF"), A("BA"), cols["e15"], OP.mult, "BA E0", "MF", -1.0, OP.mult)
    scaled("ShN", "Sh", -512.0)
    scaled("B16", "BA", 16.0)

    def both(out, nm, a, b, r):
        mm(B[7][:, 0:128], I, a, True, False, "I " + r, "bk7", 70)
        mm(B[7][:, 0:128], I, b, False, True, "I " + r, "bk7", 70)
        act(out, B[7][:, 0:128], AF.Copy, "bk7", nm, c=140)
    mm(B[6][:, 0:128], I, A("CI"), True, False, "I CI", "bk6", 70)
    mm(B[6][:, 0:128], I, A("tB"), False, False, "I tB", "bk6", 70)
    mm(B[6][:, 0:128], A("I5"), A("MF"), False, True, "I5 MF", "bk6", 70)
    act(A("Mx"), B[6][:, 0:128], AF.Identity, "bk6", "Mx", scale=8.0, c=140)
    op("G", lambda: g.affine_select(A("tA"), A("B16"), [[-1, 128]], OP.not_equal, -496.0, 0, 1), "B16", "tA", 440)
    for h in range(2):
        scaled("BH%d" % h, "tC", 8192.0, out=T.BH[:, 128 * h:128 * h + 128])
        scaled("TUr%d" % h, "Sh", -8192.0, out=T.TUr[:, 128 * h:128 * h + 128])
    act(T.kap[:, 0:12], T.ones[:, 0:12], AF.Identity, "ones", "kap0", scale=0.5, c=70)
    act(T.kap[:, 12:14], T.ones[:, 0:2], AF.Identity, "ones", "kap1", scale=4.0, c=70)
    ts(T.abi[:, 0:78], A("ib"), cols["s37"], OP.add, "ib c_s37", "abi", c=80)
    ts(T.abi[:, 78:156], T.abi[:, 0:78], 2047, OP.bitwise_and, "abi", "abj", c=80)
    ts(A("AB"), T.abi[:, 78:156], -1023.5, OP.add, "abj", "AB", c=80)
    ms(T.AB[:, 12:78:13], -1023.5, "AB")
    ts(A("MK"), A("jt"), cols["s"], OP.not_equal, "jt SC", "MK", -60000.0, OP.mult)
    act(A("ZM"), A("MK"), AF.Identity, "MK", "ZM", bias=-7.5 / 8, c=140)
    act(T.cols[:, 29:30], cols["s"], AF.Identity, "SC", "c_s16", bias=7.5, scale=16.0, c=70)
    act(A("bz"), T.i2[:, 0:128:16], AF.Identity, "i2 c_s16", "bz", bias=T.cols[:, 29:30], scale=8.0, c=70)

    def masked(j, src, b, out):
        ts(T.nmh[0:8, NP * j:NP * j + NP], T.nmi[:, NP * j:NP * j + NP], 1024.0, OP.mult, "nmi%d" % j, "nmh%d" % j, c=200)
        mm(L(b), R8, T.nmh[0:8, NP * j:NP * j + NP], True, False, "R8n nmh%d" % j, "bk%d" % b)
        mm(L(b), A("CR"), A("ones"), False, True, "CR ones", "bk%d" % b)
        tt(A(out), L(b), A(src), OP.max, "bk%d %s" % (b, src), out)

    def front(by):
        act(T.D1[:, 2:36:3], B[7][:, 448:460], AF.Identity, "bk7", "D1c", bias=E + OFF, scale=by, c=70)
        act(T.D0[:, 2:36:3], B[7][:, 448:460], AF.Identity, "bk7", "D0c", bias=16384.0 * (E - 0.5), scale=-16384.0 * by, c=70)

    def choose(now):
        now("scan")
        op("V", lambda: g.vector.tensor_tensor_scan(A("cf"), A("D0"), T.D1[:, 0:36], 0.0, OP.max, OP.min),
           "D0a D0b D0c D1a D1b D1c", "cf", 70)
        now("cl")
        lin(ON["cl"] if at[0] else "V", A("cl"), T.cf[:, 2:36:3], 1.0, 0.25 - OFF, "cf", "cl", 12)
        now("crep")
        at[0] = at[0] or (0, "first")
        act(A("crep"), A("IOT").indirect(A("cl")), AF.Copy, "IOT cl", "crep", c=G192)

    def hand_flags(now, on):
        now("hinv")
        if on["hinv"] == "A":
            act(HINV, A("Hp"), AF.Relu, "Hp", "hinv", bias=256.0 * (1 - E), scale=256.0)
        else:
            ts(HINV, A("Hp"), E - 0.5, OP.is_ge, "Hp", "hinv", 256.0, OP.mult, c=100)
        now("hfr")
        lin(on["hfr"], HFR, A("Hp"), cols["e0"], 0.0, "Hp E0", "hfr", NP)

    masked(0, "tri", 5, "fst")
    ts(T.TT[:, 0:NP], A("fst"), 3072.0, OP.min, "fst", "TTA0 TTB0", c=200)
    masked(1, "hai", 4, "RR")
    ts(A("Hs"), A("RR"), 3072.0, OP.min, "RR", "Hs", -E, OP.add, c=200)
    ts(A("Wk"), A("raw"), 0.0, OP.is_equal, "raw E0", "Wk", cols["e0"], OP.mult)
    diag(B[7][:, 448:460], "Wk", "Hs", NP, "Hs", "bk7", first=True)
    at[0] = (-1, "crep")
    front(1.0)
    at[0] = None
    ms(T.D0[:, 0:36:3], BIG, "D0a")
    ms(T.D0[:, 1:36:3], -BIG, "D0b")
    ms(T.D1[:, 1:36:3], BIG, "D1b")
    ts(T.D1[:, 0:39:3], T.AB[:, 0:13], 4096.0, OP.add, "AB", "D1a")
    choose(len)
    at[0] = None
    ms(T.nmh[0:32, 2 * NP:3 * NP], 2040.0 - (OFF - 0.5) / 8, "nmh2", 100)
    ts(T.nmh[0:8, 2 * NP:3 * NP], T.nmi[:, 2 * NP:3 * NP], -2040.0, OP.add, "nmi2", "nmh2", c=200)
    mm(L(3), A("Sh"), A("Hs"), True, False, "Sh Hs", "bk3")
    mm(L(3), A("CE15"), A("ones"), False, True, "CE15 ones", "bk3")
    cp(A("Hp"), L(3), "bk3", "Hp", 200)
    hand_flags(len, ON)
    mm(B[7][:, 0:128], I, A("MK"), True, False, "I MK", "bk7", 70)
    mm(B[7][:, 0:128], I, A("i2"), False, True, "I i2", "bk7", 70)
    act(A("KM"), B[7][:, 0:128], AF.Identity, "bk7", "KM", bias=NH / 8.0, c=140)
    both(A("MC"), "MC", A("tC"), T.TUr[:, 0:128], "tC TUr0")
    both(A("PH"), "PH", A("B16"), A("ShN"), "B16 ShN")
    both(A("HQ"), "HQ", A("Sh"), A("C15"), "Sh C15")

    def inside(lo, hi, parts=None):
        return [j for j, p in enumerate(parts or PIECES) if lo <= p[0] < hi]

    def xts(lo, hi):
        return " ".join("XT%d" % j for j in inside(lo, hi))

    def xt(p):
        return 16 * p if p < SP else XB + 16 * (p - SP)

    def cards(nm, r, j, b, out, to, length):
        ts(T.VL[:, NP * j:NP * j + NP], A(nm), E - 0.5, OP.is_lt, r, "VL%d" % j, c=100)
        mm(B[b][0:8, NP:2 * NP], A("M8"), T.VL[:, NP * j:NP * j + NP], True, True, "M8 VL%d" % j, "bk%d" % b)
        mm(L(b), I, A(nm), True, False, "I " + r, "bk%d" % b)
        mm(L(b), A("I3"), T.VL[:, NP * j:NP * j + NP], False, True, "I3 VL%d" % j, "bk%d" % b)
        if j:
            ts(A(out), L(b), R1 - E, OP.add, "bk%d" % b, out, -R1, OP.add, c=200)
        else:
            act(A(out), L(b), AF.Identity, "bk%d" % b, out, bias=-E)
        act(T.omn[:, NP * j:NP * j + NP], B[b][0:8, NP:2 * NP], AF.Copy, "bk%d" % b, "omn%d" % j)
        dma("S", "o" + to[1], T[to][:, :], A(out), out, "", 96)
        dma("S", "o" + length[1], T[length][:, :], T.omn[:, NP * j:NP * j + NP], "omn%d" % j, "", 6)

    nxt = T.cores[(rank + 1) % len(T.cores)]
    rid, pid = topo.addr(nxt, core)
    mask = 0
    for e in send_engines(topo, core, nxt):
        mask |= 1 << e

    for t in range(V):
        last = t == V - 1
        tn = "TTA%d TTB%d" % (t, t)
        tab = T.TT[:, NP * t:NP * t + NP]
        jj = 0 if last else (2 if t == 3 else 1)
        ro = 128 - 16 * jj

        def now(nm):
            at[0] = (t, nm)

        def rot(nm):
            return T[nm][:, ro:ro + 128] if jj else T[nm][:, 0:128]

        now("xc")
        cp(A("xc"), A("X").indirect(A("cl")), "XA XB Xp cl", "xc", G192)
        for j, (p, n, q) in enumerate(PIECES):
            now("g%d" % j)
            out, src = T.XT[:, xt(p):xt(p) + 16 * n], A("X").indirect(T.TT[:, NP * t + p:NP * t + p + n])
            r = "XA XB Xp TT%s%d" % ("AB"[p >= SP], t)
            if q == "A":
                act(out, src, AF.Copy, r, "XT%d" % j, c=60 + GATHER * 16 * n)
            else:
                cp(out, src, r, "XT%d" % j, 60 + GATHER * 16 * n)
        now("xh")
        lin(ON["xh"], A("xh"), A("xc"), 1.0, 2079.5, "xc", "xh", NP)
        for nm, lo, hi, b in PARTS:
            n, c2, bk, tn = hi - lo, (hi - lo) // 2 + 3, "bk%d" % (3 + 2 * b), "TT%s%d" % (nm, t)
            tab, th, inv, crep = T.TT[:, NP * t + lo:NP * t + hi], T.Th[:, lo:hi], T.DG[:, 2 * NP + lo:2 * NP + hi], T.crep[:, lo:hi]
            p3, p2 = B[3 + 2 * b][:, 0:n], B[3 + 2 * b][:, 128:128 + n]
            now("Th" + nm)
            lin(ON["Th"], th, tab, 1.0, -E, tn, "Th" + nm, n)
            now("inv" + nm)
            if ON["inv"] == "A":
                act(inv, tab, AF.Relu, tn + " c_ic c_ib", "inv" + nm, bias=cols["ib"], scale=cols["ic"], c=n + 5)
            else:
                ts(inv, tab, 3072.0, OP.is_ge, tn + " c_ic", "inv" + nm, cols["ic"], OP.mult)
            now("Tp" + nm)
            mm(p3, A("I12"), T.ones[:, 0:n], True, False, "I12 ones", bk, c2)
            mm(p2, A("C15"), crep, False, False, "C15 crep", bk, c2)
            mm(p3, I, crep, False, False, "I crep", bk, c2)
            now("Tapp" + nm)
            mm(p3, A("Mx"), inv, False, False, "Mx inv" + nm, bk, c2)
            mm(p2, A("MF"), inv, False, False, "MF inv" + nm, bk, c2)
            mm(p2, A("Sh"), th, False, True, "Sh Th" + nm, bk, c2)
            now("Q" + nm)
            tt(T.Q[:, lo:hi], p3, th, OP.min, bk + " Th" + nm, "Q" + nm, n + 5)
            now("Tapp" + nm)
            tt(T.Tapp[:, lo:hi], p2, T.Q[:, lo:hi], OP.max, bk + " Q" + nm, "Tapp" + nm, n + 5)
            now("Trot" + nm)
            mm(B[6][:, lo:hi], rot("I"), th, True, True, "I I2 Th" + nm, "bk6", c2)
            act(T.Trot[:, lo:hi], B[6][:, lo:hi], AF.Identity, "bk6", "Trot" + nm, bias=0.0 if last else E, c=n + 5)
        for j in range(16):
            now("LB" + "ab"[j // 8])
            mm(B[7][0:36, 256 + j:384:16], T.DG[:, j:3 * NP:16], A("SL"), j == 0, j == 15, "SL invA invB hinv hfr", "bk7", 20)
        now("x1")
        act(T.LT[0:36, :], B[7][0:36, 256:384], AF.Copy, "bk7", "LT", c=140)
        now("LT")
        mm(B[7][:, 448:472], T.LT[0:36, :], T.RL[0:36, :], True, True, "LT RL0 RL1", "bk7", 34)
        now("ql")
        lin(ON["ql"], A("ql"), B[7][:, 460:472], 1.0, 15.0 if last else 0.0, "bk7", "ql", 12)
        if not last:
            now("front")
            front(256.0)
        for j in range(4):
            now("F" + "ab"[j // 2])
            mm(B[6][:, NP * (j % 2):NP * (j % 2) + NP], T.FE[:, j, :], A("Tapp"), j == 0, j == 3, FE + " TappA TappB", "bk6")
        now("Gt")
        act(A("Gt"), T.TAB[:, 0:64].indirect(A("ql")), AF.Copy, "TAB ql", "Gt", c=G192)
        for j in range(2):
            now("U%d" % j)
            tt(T.U[:, NP * j:NP * j + NP], B[6][:, NP * j:NP * j + NP], A("Gt"), OP.mult, "bk6 Gt", "U%d" % j)

        def opening(b, lo, hi, nm):
            o, c, bk = B[b][0:hi - lo, 0:128], 67, "bk%d" % b
            now("thr" + nm)
            mm(o, T.nmh[0:9, 2 * NP + lo:2 * NP + hi], T.R8n[0:9, :], True, False, "R8n nmh2", bk, c)
            now("NB" + nm)
            mm(o, T.xc[:, lo:hi], A("NB"), False, False, "NB xc", bk + "+", c)
            now("Ipen" + nm)
            mm(o, T.DG[:, 2 * NP + lo:2 * NP + hi], A("Ipen"), False, False, "Ipen inv" + nm, bk + "+", c)

        now("SD")
        act(T.SD[:, 0:128:16], T.ones[:, 0:8], AF.Identity, "ones D1a", "SD", bias=3.5, scale=T.D1[:, 36:37], c=70)

        opening(4, 0, SP, "A")
        for b, p, n, r in ((1, 0, SP, REP[0]), (2, SP, NP - SP, REP[1])):
            now("four%d" % b)
            for s in range(r):
                mm(R(b, 0, r * n, s, r), I, T.xc[:, p:p + n], True, True, "I xc", "bk%d" % b, n // 2 + 2)
        for j, (p, n) in enumerate(MAXES):
            b, r = (1, REP[0]) if p < SP else (2, REP[1])
            o, st = r * (p - SP * (b - 1)), 16 // r
            for s in range(st):
                now("m%d_%d" % (j, s % 4))
                tt(T.MX[:, 16 * p + s:16 * (p + n):st], R(b, o, o + r * n), T.XT[:, xt(p) + s:xt(p) + 16 * n:st], OP.max,
                   "bk%d " % b + xts(p, p + n), "MX%d_%d" % (j, s), max(70, r * n + 10))
        for b in range(2):
            bk, D = "bk%d" % (4, 1)[b], B[(4, 1)[b]]
            if b:
                opening(1, SP, NP, "B")
            for c, (p, n) in enumerate(SX):
                for s in range(16 * (c == b)):
                    now("sx%d" % c + "abcd"[s // 4])
                    mm(D[0:n, s:128:16], T.XT[:, xt(p) + s:xt(p) + 16 * n:16], A("S8"), False, False,
                       "S8 " + xts(p, p + n), bk + "+", 34)
            for c, (p, n) in enumerate(SM):
                for k in range(16 * (c == b)):
                    now("sm%d" % c + "abcd"[k // 4])
                    s = k // 4 + 4 * (k % 4)
                    end = k == 15
                    mm(D[0:n, s:128:16], T.MX[:, 16 * p + s:16 * (p + n):16], A("S16"), False, end,
                       "S16 " + " ".join("MX%d_%d" % (j, s % (16 // REP[b])) for j in inside(p, p + n, MAXES)),
                       bk if end else bk + "+", 34)

        for nm, lo, hi, b in PARTS:
            n, bk, c2, pb = hi - lo, "bk%d" % (2 * b), (hi - lo) // 2 + 3, 2 * b
            x0, q0, q1 = xt(lo), lo // 16, hi // 16
            now("ok" + nm)
            op("V", lambda n=n, b=b: g.vector.tensor_tensor_scan(T["SQ" + "AB"[b]][0:n, 127::-1], T.SD[0:n, :], B[(4, 1)[b]][0:n, 127::-1],
                                                                 0.0, OP.max, OP.min), "bk%d SD" % (4, 1)[b], "ok" + nm, 140)
            now("d0" + nm)
            o, bo = R(4 * b, 384, 384 + n), "bk%d" % (4 * b)
            mm(o, A("I75"), T.xc[:, lo:hi], True, False, "I75 xc", bo, c2)
            mm(o, A("I5"), T.XT[:, x0:x0 + 16 * n:16], False, False, "I5 " + xts(lo, hi), bo, c2)
            mm(o, I, T.MX[:, 16 * lo:16 * hi:16], False, True, "I " + " ".join("MX%d_0" % j for j in inside(lo, hi, MAXES)), bo, c2)
            now("N0" + nm)
            act(T.XT[:, x0 + NH:x0 + NH + 16 * n:16], o, AF.Identity, bo, "N0" + nm, bias=0.5, scale=4.0, c=n + 5)
            now("tri" + nm)
            mm(R(pb, 128, 128 + n), T["SQ" + nm][0:n, :], T.I[0:n, 0:n], True, True, "I ok" + nm, bk, c2)
            now("K1" + nm)
            act(T.K1[:, lo:hi], R(pb, 128, 128 + n), AF.Sign, bk + " SD", "K1" + nm, bias=T.SD[:, 0:1], scale=-1.0, c=n + 5)
            now("k" + nm)
            mm(R(pb, 256, 256 + n), A("I8"), T.KM[:, 0:n], True, False, "I8 KM", bk, c2)
            mm(R(pb, 256, 256 + n), A("BAk"), T.K1[:, lo:hi], False, True, "BAk K1" + nm, bk, c2)
            pick(T.kl[:, q0:q1], R(pb, 256, 256 + n), bk, "kl" + nm, n + 5)
            br = bp = (3, 1)[b]
            pr, pp = B[br][:, NP + lo:NP + hi], B[bp][:, lo:hi]
            now("CE" + nm)
            mm(pr, A("CE" if last else "I3"), T.ones[:, 0:n], True, False, "CE I3 ones", "bk%d" % br, c2)
            now("pt" + nm)
            mm(pp, rot("I"), T.Tapp[:, lo:hi], False, False, "I I2 Tapp" + nm, "bk%d" % bp, c2)
            if not last:
                mm(pp, A("CE"), T.ones[:, 0:n], False, False, "CE ones", "bk%d" % bp, c2)
            now("ramp" + nm)
            mm(pr, rot("TUr"), T.K1[:, lo:hi], False, False, "TUr0 TUr1 K1" + nm, "bk%d" % br, c2)
            now("BH" + nm)
            mm(pp, rot("BH"), T.K1[:, lo:hi], False, True, "BH0 BH1 K1" + nm, "bk%d" % bp, c2)
            now("fst" + nm)
            tt(T.fst[:, lo:hi], pr, T.Trot[:, lo:hi], OP.max, "bk%d Trot%s fst" % (br, nm), "fst" + nm, n + 5)
            now("Tc" + nm)
            if last:
                tt(T.Tc[:, lo:hi], pp, T.fst[:, lo:hi], OP.min, "bk%d fst%s" % (bp, nm), "Tc" + nm, n + 5)
            else:
                to, there, arr = T.TO[:, NP * t + lo:NP * t + hi], T.TT[:, NP * (t + 1) + lo:NP * (t + 1) + hi], "arr%s%d" % (nm, t + 1)
                tt(to, pp, T.fst[:, lo:hi], OP.min, "bk%d fst%s" % (bp, nm), "TO" + arr, n + 5)
                op("G", lambda to=to, there=there, arr=arr: g.remote_dma(there, to, T.sem[arr], T.sem.snd, pid, rid, mask),
                   "TO" + arr, "sent" + arr, REMOTE * (2 if t == 0 and b == 0 else 1), dma="snd")
                op("R", None, "sent" + arr, "TT%s%d" % (nm, t + 1), 0, dma=arr)
            now("u" + nm)
            tt(T.u[:, lo:hi], T.XT[:, x0:x0 + NH + 16 * n].indirect(T.kl[:, q0:q1]), T.xh[:, lo:hi], OP.add,
               xts(lo, hi) + " N0%s kl%s xh" % (nm, nm), "u" + nm, 60 + GATHER * n)
            z0 = 384 * b
            k = ZR[b]
            now("zc" + nm)
            mm(R(pb, z0, z0 + n), A("I8"), T.ZM[:, 0:n], True, False, "I8 ZM", bk, c2)
            now("z" + nm)
            for h in range(k):
                mm(R(pb, z0 + h * n, z0 + h * n + n), A("BAw"), T.u[:, lo:hi], False, h == k - 1, "BAw u" + nm, bk, c2)
            now("y" + nm)
            lin(ON["y"], T.y[:, lo:hi], T.u[:, lo:hi], 0.5, -1040.0, "u" + nm, "y" + nm, n)
            now("zr" + nm)
            pick(T.zr[:, 2 * q0:2 * q0 + k * (q1 - q0)], R(pb, z0, z0 + k * n), bk, "zr" + nm, k * n + 5)
            if k == 1:
                now("zt" + nm)
                tt(T.zr[:, q0 + q1:2 * q1], T.zr[:, 2 * q0:q0 + q1], T.bz[:, 0:q1 - q0], OP.add, "bz zr" + nm, "zt" + nm, 70)
            now("zf" + nm)
            ts(T.zf[:, q0:q1], T.zr[:, 2 * q0:q0 + q1], R16, OP.add, "zr" + nm, "zf" + nm, -R16, OP.add)
            now("zl" + nm)
            tt(T.zl[:, q0:q1], T.zr[:, q0 + q1:2 * q1], T.zf[:, q0:q1], OP.subtract, "zr%s zf%s zt%s" % (nm, nm, nm), "zl" + nm, 70)
            now("X" + nm)
            cp(T.X[:, 16 * lo:16 * hi].indirect(T.zl[:, q0:q1]), T.y[:, lo:hi], "y%s zl%s" % (nm, nm), "X" + nm, 50 + SCATTER * n)
        if last:
            now("yt")
            cards("Tc", "TcA TcB", 0, 3, "oyt", "yt", "yn")
        else:
            now("CI")
            mm(L(3), A("CI"), INV, True, False, "CI invA invB", "bk3")
            now("cap")
            mm(L(3), A("MC"), A("K1"), False, True, "MC K1A K1B", "bk3")
            act(A("cap"), L(3), AF.Sign, "bk3", "cap acc", bias=-0.5, acc=T.acc[:, 0:1], c=220)
            now("D1b")
            tt(T.D1[:, 1:36:3], A("kl"), T.cf[:, 2:36:3], OP.max, "klA klB cf", "D1b", 70)
            now("D0b")
            lin(ON["D0b"], T.D0[:, 1:36:3], A("kl"), -1.0, NH + 3071.0, "klA klB", "D0b", 12)
            now("rA")
            act(T.rA[:, 0:13], T.kap[:, 0:13], AF.Identity, "kap0 kap1 acc", "rA", scale=T.acc[:, 0:1], c=70)
            pa = B[3][:, 400:413]
            now("pa")
            mm(pa, I, T.AB[:, 13 * t + 13:13 * t + 26], True, False, "I AB", "bk3", 34)
            mm(pa, T.ones[:, 0:128], T.rA[:, 0:13], False, True, "ones rA", "bk3", 34)
            now("rr")
            ts(T.rr[:, 0:13], pa, R2K, OP.add, "bk3", "rr", -R2K - 4096, OP.add)
            now("D1a")
            tt(T.D1[:, 0:39:3], pa, T.rr[:, 0:13], OP.subtract, "bk3 rr", "D1a", 70)
            choose(now)
        now("pen")
        mm(H(5), I if last else A("HQ"), A("Hp"), True, True, "I HQ Hp", "bk5")
        ph, cst = ("tA", "cq") if last else ("PH", "cp")
        mm(L(5), A(ph), HINV, True, False, ph + " hinv", "bk5")
        mm(L(5), A("PI"), INV, False, False, "PI invA invB", "bk5")
        now("PK")
        mm(L(5), A("PK"), A("K1"), False, True, "PK K1A K1B", "bk5")
        for j in range(2):
            now("Rv%d" % j)
            mm(L(7), T.ME[:, j, :], T.U[:, NP * j:NP * j + NP], j == 0, j == 1 and ON["RR"] == "V", ME + " U%d" % j, "bk7", 400)
        now("wall")
        if ON["RR"] == "V":
            act(A("wall"), L(5), AF.Identity, "bk5 c_" + cst, "wall", bias=cols[cst])
            now("RR")
            tt(A("RR"), L(7), A("wall"), OP.max, "bk7 wall", "RR")
            now("Hp")
            tt(A("Hp"), H(5), A("RR"), OP.min, "bk5 RR", "Hp")
        else:
            act(A("wall"), L(5), AF.Relu, "bk5 c_" + cst, "wall", bias=cols[cst], scale=1.0)
            mm(L(7), I, A("wall"), False, True, "I wall", "bk7")
            now("RR")
            act(A("RR"), H(5), AF.Copy, "bk5", "RR")
            now("Hp")
            tt(A("Hp"), L(7), A("RR"), OP.min, "bk7 RR", "Hp")
        if not last:
            hand_flags(now, ON)
        else:
            now("yh")
            cards("Hp", "Hp", 1, 6, "oyh", "yh", "ym")
    for nm, lo, hi, b in PARTS:
        dma("S", "ox" + nm, T.yx[:, 16 * lo:16 * hi], T.X[:, 16 * lo:16 * hi], "X" + nm, "", 4 * (hi - lo))

    emit(g, core, T, topo, plan(ops), rank)


def plan(ops):
    n = len(ops)
    hold = [60 if o["dma"] else o["c"] for o in ops]
    for q, names in ORDER.items():
        place = {nm.rstrip("-+"): ((nm[-1] == "-") - (nm[-1] == "+"), i) for i, nm in enumerate(names.split())}
        place["first"] = (0, 0)
        key = {k: (o["at"][0] + place[o["at"][1]][0], place[o["at"][1]][1]) for k, o in enumerate(ops) if o["q"] == q and o["at"]}
        for k in key:
            if key[k][0] >= V - 1:
                key[k] = (V - 1, LAST[q].split().index(ops[k]["at"][1] + "-" * (ops[k]["at"][0] < V - 1)))
            if ops[k]["at"] in LATER:
                key[k] = (ops[k]["at"][0], place[LATER[ops[k]["at"]][q]][1] + 0.5)
        mine = sorted(key, key=lambda k: (key[k], k))
        for a, b in zip(mine, mine[1:]):
            ops[b]["order"].add(a)
    for q in "GS":
        mine = [k for k, o in enumerate(ops) if o["q"] == q and (q == "G" or not o["deps"])]
        for a, b in zip(mine, mine[1:]):
            ops[b]["order"].add(a)
    succ = [[] for _ in ops]
    left = [0] * n
    for k, o in enumerate(ops):
        for d in o["deps"] | o["order"]:
            succ[d].append((k, WAKE if d in o["deps"] else hold[d] - ops[d]["c"]))
            left[k] += 1
    line, wait = [k for k in range(n) if not left[k]], list(left)
    for k in line:
        for s, lag in succ[k]:
            wait[s] -= 1
            if not wait[s]:
                line.append(s)
    assert len(line) == n, [ops[k]["at"] for k in range(n) if wait[k]][:9]
    tail = [0] * n
    for k in reversed(line):
        tail[k] = ops[k]["c"] + max([tail[s] + lag for s, lag in succ[k]] + [0])
    free, est, out = {}, [0] * n, []
    ready = [k for k in range(n) if not left[k]]
    while ready:
        start = {k: max(est[k], free.get(ops[k]["q"], 0)) for k in ready}
        first = min(ready, key=lambda k: start[k] + hold[k])
        lim = start[first] + hold[first]
        k = max([j for j in ready if ops[j]["q"] == ops[first]["q"] and (start[j] < lim or j == first)], key=lambda j: (tail[j], -j))
        ready.remove(k)
        out.append(k)
        free[ops[k]["q"]] = start[k] + hold[k]
        for s, lag in succ[k]:
            est[s] = max(est[s], start[k] + ops[k]["c"] + lag)
            left[s] -= 1
            if not left[s]:
                ready.append(s)
    new = {k: i for i, k in enumerate(out)}
    return [dict(ops[k], deps=set(new[d] for d in ops[k]["deps"]) if ops[k]["q"] != "R" else set()) for k in out]


def emit(g, core, T, topo, ops, rank):
    Q = {"V": g.vector, "A": g.scalar, "P": g.tensor, "G": g, "S": g.sync}
    sems = {"V": "qV", "A": "qA", "P": "qP", "G": "qG"}
    seq, pos = {}, {}
    for k, o in enumerate(ops):
        pos[k] = len(seq.setdefault(o["q"], []))
        seq[o["q"]].append(k)
    know = {q: ({}, set()) for q in "VAPGS"}
    after, needed, waits = {}, set(), {}
    for k, o in enumerate(ops):
        q = o["q"]
        if q == "R":
            after[k] = ({}, set())
            continue
        kn, kd = know[q]
        wl = []

        def learn(d):
            wl.append(d)
            kn2, kd2 = after[d]
            for a in kn2:
                kn[a] = max(kn.get(a, -1), kn2[a])
            kd.update(kd2)

        need = {}
        for d in sorted(o["deps"], reverse=True):
            od = ops[d]
            if not od["dma"]:
                need[od["q"]] = max(need.get(od["q"], -1), pos[d])
            elif d not in kd:
                kd.add(d)
                learn(d)
        for q2 in sorted(need, key=lambda a: -seq[a][need[a]]):
            p = need[q2]
            if kn.get(q2, -1) < p:
                kn[q2] = p
                needed.add(seq[q2][p])
                learn(seq[q2][p])
        waits[k] = wl
        after[k] = (dict(kn), set(kd))
    for q in "VAPG":
        comp = [k for k in seq.get(q, []) if not ops[k]["dma"]]
        if comp:
            needed.add(comp[-1])
    count = {}
    cnt = {q: 0 for q in "VAPG"}
    for k, o in enumerate(ops):
        if k in needed:
            cnt[o["q"]] += 1
            count[k] = cnt[o["q"]]
    n = len(T.cores)
    ein = len(send_engines(topo, T.cores[(rank - 1) % n], core))
    eout = len(send_engines(topo, core, T.cores[(rank + 1) % n]))
    nsend = 0
    for k, o in enumerate(ops):
        q = o["q"]
        if q == "R":
            continue
        e = Q[q]
        for d in waits[k]:
            od = ops[d]
            if od["dma"]:
                e.wait_ge(T.sem[od["dma"]], ein if od["dma"][:3] == "arr" else 16)
            else:
                e.wait_ge(T.sem[sems[od["q"]]], count[d])
        ins = o["f"]()
        if o["dma"] == "snd":
            nsend += 1
        elif o["dma"]:
            ins.then_inc(T.sem[o["dma"]], 16)
        elif k in needed:
            ins.then_inc(T.sem[sems[q]], 1)
    for k, o in enumerate(ops):
        if o["dma"] and o["dma"] != "snd":
            g.wait_ge(T.sem[o["dma"]], ein if o["dma"][:3] == "arr" else 16)
    g.wait_ge(T.sem.snd, eout * nsend)
    for q in "VAPG":
        if cnt[q]:
            g.wait_ge(T.sem[sems[q]], cnt[q])
